import numpy as np
import ml_dtypes


def mxq(x, axis, fmt="e4m3"):
    dtype, down = {"e4m3": (ml_dtypes.float8_e4m3fn, 7), "e5m2": (ml_dtypes.float8_e5m2, 14)}[fmt]
    v = np.moveaxis(np.asarray(x, np.float32).astype(ml_dtypes.bfloat16).astype(np.float64), axis, -1)
    blocks = v.reshape(v.shape[:-1] + (-1, 32))
    amax = np.abs(blocks).max(-1, keepdims=True)
    byte = np.maximum(np.where(amax > 0, np.frexp(amax)[1] - 1 + 127, 0) - down, 1)
    scale = np.exp2(byte - 127.0)
    codes = (blocks / scale).astype(np.float32).astype(dtype).astype(np.float64)
    return np.moveaxis((codes * scale).reshape(v.shape), -1, axis)


WIDE = False


def mx_kscale(k):
    if not WIDE:
        return np.ones(k)
    levels = np.array([10, -10, 5, -5, 0])
    if k % 512:
        return np.exp2(np.random.permutation(np.resize(levels, k // 32))).repeat(32)
    a = np.empty((k // 512, 16))
    for p in range(k // 512):
        a[p, :8] = np.random.permutation(np.resize(levels, 8))
        for g in range(8):
            far = levels[np.abs(levels - a[p, g]) >= 10]
            a[p, g + 8] = far[np.random.randint(len(far))]
    return np.exp2(a.ravel()).repeat(32)


def f64(x):
    return np.asarray(x).astype(np.float64)


def striped(idx):
    return np.tile(np.asarray(idx).reshape(-1, 16).T, (8, 1)).astype(np.uint16)


def unstriped(offs):
    return offs[:16].T.reshape(-1).astype(np.int64)


E2M1 = np.array([0.0, 0.5, 1.0, 1.5, 2.0, 3.0, 4.0, 6.0, -0.0, -0.5, -1.0, -1.5, -2.0, -3.0, -4.0, -6.0])


def pack_weight(w, fmt):
    k, n = w.shape
    w = f64(np.asarray(w, np.float32).astype(ml_dtypes.bfloat16)).reshape(k // 32, 32, n)
    amax = np.abs(w).max(1)
    if fmt == "e4m3":
        byte = np.frexp(amax)[1] - 1 + 127 - 7
    else:
        mant, ex = np.frexp(amax / 6.0)
        byte = np.where(mant > 0.5, ex, ex - 1) + 127
    byte = np.clip(np.where(amax > 0, byte, 1), 1, 254)
    scaled = (w * np.exp2(127.0 - byte)[:, None, :]).reshape(k, n).astype(np.float32)
    by_word = np.ascontiguousarray(scaled.reshape(k // 512, 128, 4, n).transpose(0, 1, 3, 2))
    if fmt == "e4m3":
        words = by_word.astype(ml_dtypes.float8_e4m3fn).view(np.uint8)
    else:
        c = by_word.astype(ml_dtypes.float4_e2m1fn).view(np.uint8) & 0xF
        words = (c[..., 0::2] | (c[..., 1::2] << 4)).reshape(k // 512, 128, 2 * n)
    return np.ascontiguousarray(words), np.ascontiguousarray(byte.astype(np.uint8).reshape(k // 512, 16, n))


def unpack_weight(words, scales, fmt):
    g, _, n = scales.shape
    words = np.ascontiguousarray(words).reshape(g, 128, n, -1)
    if fmt == "e4m3":
        vals = words.view(ml_dtypes.float8_e4m3fn).astype(np.float64)
    else:
        nib = np.empty((g, 128, n, 4), np.uint8)
        nib[..., 0::2] = words & 0xF
        nib[..., 1::2] = words >> 4
        vals = E2M1[nib]
    vals = vals * np.repeat(np.exp2(scales.astype(np.float64) - 127.0), 8, axis=1)[..., None]
    return vals.transpose(0, 1, 3, 2).reshape(g * 512, n)


def sigmoid(v):
    return 1.0 / (1.0 + np.exp(-v))


def bf(x):
    return np.asarray(x, np.float32).astype(ml_dtypes.bfloat16)


def planes(Y):
    r, m = Y.shape
    b = f64(bf(Y)).reshape(r // 32, 32, m)
    amax = np.abs(b).max(1)
    byte = np.clip(np.where(amax > 0, np.frexp(amax)[1] - 1 + 127 - 7, 1), 1, 254)
    codes = (b * np.exp2(127.0 - byte)[:, None, :]).reshape(r, m).astype(np.float32).astype(ml_dtypes.float8_e4m3fn).view(np.uint8)
    words = codes.reshape(r // 512, 128, 4, m).transpose(0, 1, 3, 2)
    return np.ascontiguousarray(words), np.ascontiguousarray(byte.astype(np.uint8).reshape(r // 512, 16, m))


D, T, I, J, Q = 512, 2048, 1024, 512, 512


def setup_inputs():
    n = np.random.standard_normal
    idx = np.random.permutation(T)[:I]
    idx2 = np.random.randint(0, I, J)
    idx3 = np.random.randint(0, I, J)
    fd = mx_kscale(D)
    itemp = pack_weight(n((D, T)) / fd[:, None], "e4m3")
    return {
        "query": (n((D, Q)) * 0.8 / np.sqrt(D) * fd[:, None]).astype(np.float32),
        "item_words": itemp[0],
        "item_scales": itemp[1],
        "ib": np.tile(0.3 * n(T), (128, 1)).astype(np.float32),
        "offs": striped(idx),
        "offs2": striped(idx2),
        "offs3": striped(idx3),
    }


def reference(query, item_words, item_scales, ib, offs, offs2, offs3):
    idx = unstriped(offs)
    idx2 = unstriped(offs2)
    idx3 = unstriped(offs3)
    itemu = unpack_weight(item_words, item_scales, "e4m3")
    queryq = mxq(f64(query), 0, "e4m3")
    itemidxg = itemu[:, idx]
    a = queryq.T @ itemidxg
    s = a + f64(ib)[:1][:, idx]
    y = sigmoid(s[:, idx2] - s[:, idx3])
    words, scales = planes(y)
    return y, words, scales

@@ -1,0 +1,152 @@
+from contextlib import ExitStack
+
+import concourse.mybir as mybir
+
+D, T, I, J, Q = 512, 2048, 1024, 512, 512
+FLOPS = 2 * D * I * Q
+
+F32 = mybir.dt.float32
+BF16 = mybir.dt.bfloat16
+I32 = mybir.dt.int32
+U32 = mybir.dt.uint32
+U16 = mybir.dt.uint16
+U8 = mybir.dt.uint8
+FP8X4 = mybir.dt.float8_e4m3fn_x4
+ACT = mybir.ActivationFunctionType
+ALU = mybir.AluOpType
+
+P = 128
+PACK = 4
+BANK = 512
+PAIR_CHUNKS = ((0, 256), (256, 512))
+
+
+def tile_attend_pairprefs_pl_kernel(tc, query, item_words, item_scales, ib, offs, offs2, offs3, out_0, out_1, out_2):
+    nc = tc.nc
+    with ExitStack() as ctx:
+        lists = ctx.enter_context(tc.tile_pool(name="lists", bufs=1))
+        sb = ctx.enter_context(tc.tile_pool(name="sb", bufs=1))
+        psum = ctx.enter_context(tc.psum_pool(name="psum", bufs=1))
+
+        slot_list = lists.tile([P, I // 16], U16, name="slot_list")
+        first_list = lists.tile([P, J // 16], U16, name="first_list")
+        second_list = lists.tile([P, J // 16], U16, name="second_list")
+        nc.sync.dma_start(slot_list[:], offs)
+
+        scale_pool = sb.tile([P, T], U8, name="scale_pool", align_bytes=64)
+        for quad in range(4):
+            nc.sync.dma_start(
+                scale_pool[32 * quad : 32 * quad + 32, :].bitcast(I32),
+                item_scales[:, 4 * quad : 4 * quad + 4, :].bitcast(I32).broadcast_to([8, 4, T // 4]),
+            )
+        word_pool = sb.tile([P, T], U32, name="word_pool", align_bytes=64)
+        nc.sync.dma_start(word_pool[:].bitcast(I32), item_words[0].rearrange("p n t -> p (n t)").bitcast(I32))
+        q_rows = query.rearrange("(p r) q -> p r q", r=PACK)
+        q_raw = [sb.tile([P, PACK, Q // 2], F32, name="q_raw%d" % h, align_bytes=64) for h in range(2)]
+        for h in range(2):
+            nc.sync.dma_start(q_raw[h][:], q_rows[:, :, h * (Q // 2) : (h + 1) * (Q // 2)])
+        bias_pool = sb.tile([P, T], F32, name="bias_pool", align_bytes=64)
+        nc.sync.dma_start(bias_pool[:], ib)
+        nc.sync.dma_start(first_list[:], offs2)
+        nc.sync.dma_start(second_list[:], offs3)
+
+        item_sc = sb.tile([P, I], U8, name="item_sc", align_bytes=64)
+        nc.vector.tensor_copy(item_sc[:], scale_pool[:].indirect(slot_list[:]))
+        item_cd = sb.tile([P, I], U32, name="item_cd", align_bytes=64)
+        nc.vector.tensor_copy(item_cd[:], word_pool[:].indirect(slot_list[:]))
+
+        q_bf = sb.tile([P, Q * PACK], BF16, name="q_bf", align_bytes=64)
+        q_dealt = q_bf[:].rearrange("p (t m r) -> p m t r", t=PACK, r=PACK)
+        nc.scalar.copy(q_dealt[:, : P // 2], q_raw[0][:].rearrange("p r (m t) -> p m t r", t=PACK))
+        nc.vector.tensor_copy(q_dealt[:, P // 2 :], q_raw[1][:].rearrange("p r (m t) -> p m t r", t=PACK))
+        q_cd = sb.tile([P, Q], U32, name="q_cd", align_bytes=64)
+        q_sc = sb.tile([P, Q], U8, name="q_sc", align_bytes=64)
+        nc.vector.quantize_mx(out=q_cd[:].bitcast(FP8X4), scales=q_sc[:], in_=q_bf[:])
+
+        bias = sb.tile([P, I], F32, name="bias", align_bytes=64)
+        nc.vector.tensor_copy(bias[:], bias_pool[:].indirect(slot_list[:]))
+
+        scores = []
+        y_tiles = [sb.tile([P, PACK, hi - lo], F32, name="y%d" % c, align_bytes=64) for c, (lo, hi) in enumerate(PAIR_CHUNKS)]
+
+        def look_up(t, lo, hi):
+            second = sb.tile([P, hi - lo], F32, name="second%d_%d" % (t, lo), align_bytes=64)
+            nc.vector.tensor_copy(second[:], scores[t][:].indirect(second_list[:, lo // 16 : hi // 16]))
+            return second
+
+        def prefer(t, lo, hi, second):
+            diff = sb.tile([P, hi - lo], F32, name="diff%d_%d" % (t, lo), align_bytes=64)
+            nc.vector.tensor_tensor(diff[:], scores[t][:].indirect(first_list[:, lo // 16 : hi // 16]), second[:], ALU.subtract)
+            for c, (a, b) in enumerate(PAIR_CHUNKS):
+                if lo <= a and b <= hi:
+                    nc.scalar.activation(y_tiles[c][:, t, :], diff[:, a - lo : b - lo], ACT.Sigmoid)
+
+        y_rows = out_0.rearrange("(p t) j -> p t j", t=PACK)
+        y_cd = sb.tile([P, J], U32, name="y_cd", align_bytes=64)
+        y_sc = sb.tile([P, J], U8, name="y_sc", align_bytes=64)
+        words_out = out_1[0].rearrange("p c t -> p (c t)").bitcast(I32)
+
+        def round_chunk(c):
+            lo, hi = PAIR_CHUNKS[c]
+            nc.sync.dma_start(y_rows[:, :, lo:hi], y_tiles[c][:])
+            y_bf = sb.tile([P, (hi - lo) * PACK], BF16, name="y_bf%d" % c, align_bytes=64)
+            nc.scalar.copy(y_bf[:].rearrange("p (j t) -> p j t", t=PACK), y_tiles[c][:].rearrange("p t j -> p j t"))
+            return y_bf
+
+        def quantise_chunk(c, y_bf):
+            lo, hi = PAIR_CHUNKS[c]
+            start = lo
+            while start < hi:
+                width = 256 if hi - start >= 256 else 128
+                cols = slice(start, start + width)
+                nc.vector.quantize_mx(
+                    out=y_cd[:, cols].bitcast(FP8X4),
+                    scales=y_sc[:, cols],
+                    in_=y_bf[:, (start - lo) * PACK : (start - lo + width) * PACK],
+                )
+                start = start + width
+            nc.sync.dma_start(words_out[:, lo:hi], y_cd[:, lo:hi].bitcast(I32))
+
+        def score(t):
+            s_t = sb.tile([P, I], F32, name="scores%d" % t, align_bytes=64)
+            scores.append(s_t)
+            rows = slice(t * P, (t + 1) * P)
+            for h in range(I // BANK):
+                cols = slice(h * BANK, (h + 1) * BANK)
+                acc = psum.tile([P, BANK], F32, name="acc%d_%d" % (t, h))
+                nc.tensor.matmul_mx(
+                    out=acc[:],
+                    lhsT=q_cd[:, rows].bitcast(FP8X4),
+                    lhsT_scale=q_sc[:, rows],
+                    rhs=item_cd[:, cols].bitcast(FP8X4),
+                    rhs_scale=item_sc[:, cols],
+                    start=True,
+                    stop=True,
+                )
+                nc.vector.tensor_tensor(s_t[:, cols], acc[:], bias[:, cols], ALU.add)
+
+        half = J // 2
+        score(0)
+        score(1)
+        g0 = look_up(0, 0, J)
+        g1 = look_up(1, 0, J)
+        prefer(0, 0, J, g0)
+        score(2)
+        prefer(1, 0, J, g1)
+        score(3)
+        g2 = look_up(2, 0, half)
+        g3 = look_up(3, 0, half)
+        prefer(2, 0, half, g2)
+        prefer(3, 0, half, g3)
+        first_bf = round_chunk(0)
+        g2 = look_up(2, half, J)
+        g3 = look_up(3, half, J)
+        prefer(2, half, J, g2)
+        prefer(3, half, J, g3)
+        quantise_chunk(0, first_bf)
+        quantise_chunk(1, round_chunk(1))
+        for quad in range(4):
+            nc.scalar.dma_start(
+                out_2[0, 4 * quad : 4 * quad + 4, :].bitcast(I32),
+                y_sc[32 * quad : 32 * quad + 4, :].bitcast(I32),
+            )

@@ -1,6 +1,7 @@
 from contextlib import ExitStack
 
 import concourse.mybir as mybir
+from concourse.masks import make_identity
 
 D, T, I, J, Q = 512, 2048, 1024, 512, 512
 FLOPS = 2 * D * I * Q
@@ -18,7 +19,11 @@ ALU = mybir.AluOpType
 P = 128
 PACK = 4
 BANK = 512
-PAIR_CHUNKS = ((0, 256), (256, 512))
+BLOCKS = BANK // P
+HALVES = I // BANK
+DIRECT = 1
+PAIR_HALF = J // 2
+VECTOR_SHARE = 96
 
 
 def tile_attend_pairprefs_pl_kernel(tc, query, item_words, item_scales, ib, offs, offs2, offs3, out_0, out_1, out_2):
@@ -26,48 +31,132 @@ def tile_attend_pairprefs_pl_kernel(tc, query, item_words, item_scales, ib, offs
     with ExitStack() as ctx:
         lists = ctx.enter_context(tc.tile_pool(name="lists", bufs=1))
         sb = ctx.enter_context(tc.tile_pool(name="sb", bufs=1))
-        psum = ctx.enter_context(tc.psum_pool(name="psum", bufs=1))
+        psum = ctx.enter_context(tc.psum_pool(name="psum", bufs=4))
 
         slot_list = lists.tile([P, I // 16], U16, name="slot_list")
         first_list = lists.tile([P, J // 16], U16, name="first_list")
         second_list = lists.tile([P, J // 16], U16, name="second_list")
         nc.sync.dma_start(slot_list[:], offs)
 
+        bias_pool = sb.tile([P, T], F32, name="bias_pool", align_bytes=64)
+        nc.sync.dma_start(bias_pool[0:32, :], ib[0:32, :])
+        nc.vector.memset(bias_pool[64:128, :].bitcast(I32), 0)
+        nc.gpsimd.memset(bias_pool[32:64, :].bitcast(I32), 0)
         scale_pool = sb.tile([P, T], U8, name="scale_pool", align_bytes=64)
         for quad in range(4):
             nc.sync.dma_start(
                 scale_pool[32 * quad : 32 * quad + 32, :].bitcast(I32),
                 item_scales[:, 4 * quad : 4 * quad + 4, :].bitcast(I32).broadcast_to([8, 4, T // 4]),
             )
-        word_pool = sb.tile([P, T], U32, name="word_pool", align_bytes=64)
-        nc.sync.dma_start(word_pool[:].bitcast(I32), item_words[0].rearrange("p n t -> p (n t)").bitcast(I32))
         q_rows = query.rearrange("(p r) q -> p r q", r=PACK)
-        q_raw = [sb.tile([P, PACK, Q // 2], F32, name="q_raw%d" % h, align_bytes=64) for h in range(2)]
+        q_raw = [sb.tile([P, PACK, Q // 2], F32, name="q_raw%d" % h, tag="q_raw%d" % h, align_bytes=64) for h in range(2)]
         for h in range(2):
             nc.sync.dma_start(q_raw[h][:], q_rows[:, :, h * (Q // 2) : (h + 1) * (Q // 2)])
-        bias_pool = sb.tile([P, T], F32, name="bias_pool", align_bytes=64)
-        nc.sync.dma_start(bias_pool[:], ib)
+        word_pool = sb.tile([P, T], U32, name="word_pool", align_bytes=64)
+        nc.sync.dma_start(word_pool[:].bitcast(I32), item_words[0].rearrange("p n t -> p (n t)").bitcast(I32))
         nc.sync.dma_start(first_list[:], offs2)
         nc.sync.dma_start(second_list[:], offs3)
 
+        ident = sb.tile([P, P], F32, name="ident", align_bytes=64)
+        make_identity(nc, ident[:])
+
+        def slot_half(h):
+            return slot_list[:, h * (BANK // 16) : (h + 1) * (BANK // 16)]
+
+        bias_row = [sb.tile([P, BANK], F32, name="bias_row%d" % h, align_bytes=64) for h in range(HALVES)]
+        for h in range(HALVES):
+            nc.vector.tensor_copy(bias_row[h][:], bias_pool[:].indirect(slot_half(h)))
         item_sc = sb.tile([P, I], U8, name="item_sc", align_bytes=64)
         nc.vector.tensor_copy(item_sc[:], scale_pool[:].indirect(slot_list[:]))
-        item_cd = sb.tile([P, I], U32, name="item_cd", align_bytes=64)
-        nc.vector.tensor_copy(item_cd[:], word_pool[:].indirect(slot_list[:]))
 
         q_bf = sb.tile([P, Q * PACK], BF16, name="q_bf", align_bytes=64)
         q_dealt = q_bf[:].rearrange("p (t m r) -> p m t r", t=PACK, r=PACK)
-        nc.scalar.copy(q_dealt[:, : P // 2], q_raw[0][:].rearrange("p r (m t) -> p m t r", t=PACK))
-        nc.vector.tensor_copy(q_dealt[:, P // 2 :], q_raw[1][:].rearrange("p r (m t) -> p m t r", t=PACK))
+        for h in range(2):
+            nc.scalar.copy(q_dealt[:, h * (P // 2) : (h + 1) * (P // 2)], q_raw[h][:].rearrange("p r (m t) -> p m t r", t=PACK))
         q_cd = sb.tile([P, Q], U32, name="q_cd", align_bytes=64)
         q_sc = sb.tile([P, Q], U8, name="q_sc", align_bytes=64)
         nc.vector.quantize_mx(out=q_cd[:].bitcast(FP8X4), scales=q_sc[:], in_=q_bf[:])
 
-        bias = sb.tile([P, I], F32, name="bias", align_bytes=64)
-        nc.vector.tensor_copy(bias[:], bias_pool[:].indirect(slot_list[:]))
+        item_cd = [sb.tile([P, BANK], U32, name="item_cd%d" % h, align_bytes=64) for h in range(HALVES)]
+        for h in range(HALVES):
+            nc.vector.tensor_copy(item_cd[h][:], word_pool[:].indirect(slot_half(h)))
 
-        scores = []
-        y_tiles = [sb.tile([P, PACK, hi - lo], F32, name="y%d" % c, align_bytes=64) for c, (lo, hi) in enumerate(PAIR_CHUNKS)]
+        bias_col = sb.tile([P, HALVES * BLOCKS], F32, name="bias_col", tag="q_raw0", align_bytes=64)
+        bias_all = [sb.tile([P, BANK], F32, name="bias_all%d" % h, align_bytes=64) for h in range(HALVES)]
+        for h in range(HALVES):
+            turned = psum.tile([P, BANK], F32, name="bias_turned", tag="first")
+            for b in range(BLOCKS):
+                nc.tensor.transpose(turned[:, b * P : (b + 1) * P], bias_row[h][:, b * P : (b + 1) * P], ident[:])
+            nc.scalar.copy(bias_col[:, h * BLOCKS : (h + 1) * BLOCKS], turned[:, 0:BANK:P])
+        for h in range(HALVES):
+            spread = psum.tile([P, BANK], F32, name="bias_spread", tag="second")
+            for b in range(BLOCKS):
+                c = h * BLOCKS + b
+                nc.tensor.transpose(spread[:, b * P : (b + 1) * P], bias_col[:, c : c + 1].to_broadcast([P, P]), ident[:])
+            nc.scalar.copy(bias_all[h][:], spread[:])
+
+        scores = [sb.tile([P, I], F32, name="scores%d" % t, align_bytes=64) for t in range(PACK)]
+
+        def score_direct(t):
+            rows = slice(t * P, (t + 1) * P)
+            for h in range(HALVES):
+                cols = slice(h * BANK, (h + 1) * BANK)
+                acc = psum.tile([P, BANK], F32, name="acc", tag="second")
+                nc.tensor.matmul_mx(
+                    out=acc[:],
+                    lhsT=q_cd[:, rows].bitcast(FP8X4),
+                    lhsT_scale=q_sc[:, rows],
+                    rhs=item_cd[h][:].bitcast(FP8X4),
+                    rhs_scale=item_sc[:, cols],
+                    start=True,
+                    stop=True,
+                )
+                nc.vector.tensor_tensor(scores[t][:, cols], acc[:], bias_all[h][:], ALU.add)
+
+        def score_by_slot(t):
+            rows = slice(t * P, (t + 1) * P)
+            by_slot = sb.tile([P, I], F32, name="by_slot%d" % t, tag="by_slot%d" % t, align_bytes=64)
+            for h in range(HALVES):
+                acc = psum.tile([P, BANK], F32, name="acc_by_slot", tag="first")
+                for b in range(BLOCKS):
+                    c = h * BLOCKS + b
+                    nc.tensor.matmul_mx(
+                        out=acc[:, b * P : (b + 1) * P],
+                        lhsT=item_cd[h][:, b * P : (b + 1) * P].bitcast(FP8X4),
+                        lhsT_scale=item_sc[:, c * P : (c + 1) * P],
+                        rhs=q_cd[:, rows].bitcast(FP8X4),
+                        rhs_scale=q_sc[:, rows],
+                        start=True,
+                        stop=True,
+                    )
+                for b in range(BLOCKS):
+                    c = h * BLOCKS + b
+                    nc.scalar.activation(
+                        by_slot[:, c * P : (c + 1) * P], acc[:, b * P : (b + 1) * P], ACT.Identity, bias=bias_col[:, c : c + 1]
+                    )
+            return by_slot
+
+        def turn_back(t, by_slot):
+            for h in range(HALVES):
+                turned = psum.tile([P, BANK], F32, name="turned", tag="second")
+                for b in range(BLOCKS):
+                    c = h * BLOCKS + b
+                    nc.tensor.transpose(turned[:, b * P : (b + 1) * P], by_slot[:, c * P : (c + 1) * P], ident[:])
+                nc.scalar.copy(scores[t][:, h * BANK : (h + 1) * BANK], turned[:])
+
+        for t in range(DIRECT):
+            score_direct(t)
+        for t in range(DIRECT, PACK):
+            turn_back(t, score_by_slot(t))
+
+        y = sb.tile([P, PACK, J], F32, name="y", tag="by_slot%d" % (PACK - 1), align_bytes=64)
+        y_rows = out_0.rearrange("(p t) j -> p t j", t=PACK)
+        y_bf = sb.tile([P, J * PACK], BF16, name="y_bf", align_bytes=64)
+        y_cd = sb.tile([P, J], U32, name="y_cd", align_bytes=64)
+        y_sc = sb.tile([P, J], U8, name="y_sc", align_bytes=64)
+        words_out = out_1[0].rearrange("p c t -> p (c t)").bitcast(I32)
+
+        diffs = {}
 
         def look_up(t, lo, hi):
             second = sb.tile([P, hi - lo], F32, name="second%d_%d" % (t, lo), align_bytes=64)
@@ -77,76 +166,38 @@ def tile_attend_pairprefs_pl_kernel(tc, query, item_words, item_scales, ib, offs
         def prefer(t, lo, hi, second):
             diff = sb.tile([P, hi - lo], F32, name="diff%d_%d" % (t, lo), align_bytes=64)
             nc.vector.tensor_tensor(diff[:], scores[t][:].indirect(first_list[:, lo // 16 : hi // 16]), second[:], ALU.subtract)
-            for c, (a, b) in enumerate(PAIR_CHUNKS):
-                if lo <= a and b <= hi:
-                    nc.scalar.activation(y_tiles[c][:, t, :], diff[:, a - lo : b - lo], ACT.Sigmoid)
+            diffs[(t, lo)] = diff
+            nc.scalar.activation(y[:, t, lo:hi], diff[:], ACT.Sigmoid)
+            nc.sync.dma_start(y_rows[:, t, lo:hi], y[:, t, lo:hi])
 
-        y_rows = out_0.rearrange("(p t) j -> p t j", t=PACK)
-        y_cd = sb.tile([P, J], U32, name="y_cd", align_bytes=64)
-        y_sc = sb.tile([P, J], U8, name="y_sc", align_bytes=64)
-        words_out = out_1[0].rearrange("p c t -> p (c t)").bitcast(I32)
+        def round_pairs(copy, lo, hi):
+            copy(y_bf[:, lo * PACK : hi * PACK].rearrange("p (j t) -> p j t", t=PACK), y[:, :, lo:hi].rearrange("p t j -> p j t"))
 
-        def round_chunk(c):
-            lo, hi = PAIR_CHUNKS[c]
-            nc.sync.dma_start(y_rows[:, :, lo:hi], y_tiles[c][:])
-            y_bf = sb.tile([P, (hi - lo) * PACK], BF16, name="y_bf%d" % c, align_bytes=64)
-            nc.scalar.copy(y_bf[:].rearrange("p (j t) -> p j t", t=PACK), y_tiles[c][:].rearrange("p t j -> p j t"))
-            return y_bf
-
-        def quantise_chunk(c, y_bf):
-            lo, hi = PAIR_CHUNKS[c]
-            start = lo
-            while start < hi:
-                width = 256 if hi - start >= 256 else 128
-                cols = slice(start, start + width)
-                nc.vector.quantize_mx(
-                    out=y_cd[:, cols].bitcast(FP8X4),
-                    scales=y_sc[:, cols],
-                    in_=y_bf[:, (start - lo) * PACK : (start - lo + width) * PACK],
-                )
-                start = start + width
+        def quantise_pairs(lo, hi):
+            nc.vector.quantize_mx(out=y_cd[:, lo:hi].bitcast(FP8X4), scales=y_sc[:, lo:hi], in_=y_bf[:, lo * PACK : hi * PACK])
             nc.sync.dma_start(words_out[:, lo:hi], y_cd[:, lo:hi].bitcast(I32))
 
-        def score(t):
-            s_t = sb.tile([P, I], F32, name="scores%d" % t, align_bytes=64)
-            scores.append(s_t)
-            rows = slice(t * P, (t + 1) * P)
-            for h in range(I // BANK):
-                cols = slice(h * BANK, (h + 1) * BANK)
-                acc = psum.tile([P, BANK], F32, name="acc%d_%d" % (t, h))
-                nc.tensor.matmul_mx(
-                    out=acc[:],
-                    lhsT=q_cd[:, rows].bitcast(FP8X4),
-                    lhsT_scale=q_sc[:, rows],
-                    rhs=item_cd[:, cols].bitcast(FP8X4),
-                    rhs_scale=item_sc[:, cols],
-                    start=True,
-                    stop=True,
-                )
-                nc.vector.tensor_tensor(s_t[:, cols], acc[:], bias[:, cols], ALU.add)
+        def two_tiles(t, lo, hi):
+            seconds = [look_up(t + k, lo, hi) for k in range(2)]
+            for k in range(2):
+                prefer(t + k, lo, hi, seconds[k])
 
-        half = J // 2
-        score(0)
-        score(1)
-        g0 = look_up(0, 0, J)
-        g1 = look_up(1, 0, J)
-        prefer(0, 0, J, g0)
-        score(2)
-        prefer(1, 0, J, g1)
-        score(3)
-        g2 = look_up(2, 0, half)
-        g3 = look_up(3, 0, half)
-        prefer(2, 0, half, g2)
-        prefer(3, 0, half, g3)
-        first_bf = round_chunk(0)
-        g2 = look_up(2, half, J)
-        g3 = look_up(3, half, J)
-        prefer(2, half, J, g2)
-        prefer(3, half, J, g3)
-        quantise_chunk(0, first_bf)
-        quantise_chunk(1, round_chunk(1))
+        def both_halves(t):
+            halves = (0, PAIR_HALF)
+            seconds = [look_up(t, lo, lo + PAIR_HALF) for lo in halves]
+            for lo, second in zip(halves, seconds):
+                prefer(t, lo, lo + PAIR_HALF, second)
+
+        for t in range(PACK):
+            both_halves(t)
+        round_pairs(nc.vector.tensor_copy, 0, PAIR_HALF)
+        quantise_pairs(0, PAIR_HALF)
+        round_pairs(nc.vector.tensor_copy, PAIR_HALF, PAIR_HALF + VECTOR_SHARE)
+        round_pairs(nc.scalar.copy, PAIR_HALF + VECTOR_SHARE, J)
+        quantise_pairs(PAIR_HALF, J)
         for quad in range(4):
-            nc.scalar.dma_start(
+            queue = nc.scalar if quad % 2 else nc.sync
+            queue.dma_start(
                 out_2[0, 4 * quad : 4 * quad + 4, :].bitcast(I32),
                 y_sc[32 * quad : 32 * quad + 4, :].bitcast(I32),
             )

@@ -38,16 +38,15 @@ def tile_attend_pairprefs_pl_kernel(tc, query, item_words, item_scales, ib, offs
         second_list = lists.tile([P, J // 16], U16, name="second_list")
         nc.sync.dma_start(slot_list[:], offs)
 
-        bias_pool = sb.tile([P, T], F32, name="bias_pool", align_bytes=64)
-        nc.sync.dma_start(bias_pool[0:32, :], ib[0:32, :])
-        nc.vector.memset(bias_pool[64:128, :].bitcast(I32), 0)
-        nc.gpsimd.memset(bias_pool[32:64, :].bitcast(I32), 0)
         scale_pool = sb.tile([P, T], U8, name="scale_pool", align_bytes=64)
         for quad in range(4):
             nc.sync.dma_start(
                 scale_pool[32 * quad : 32 * quad + 32, :].bitcast(I32),
                 item_scales[:, 4 * quad : 4 * quad + 4, :].bitcast(I32).broadcast_to([8, 4, T // 4]),
             )
+        bias_pool = sb.tile([P, T], F32, name="bias_pool", tag="bias_pool", align_bytes=64)
+        nc.vector.memset(bias_pool[:].bitcast(I32), 0)
+        nc.scalar.dma_start(bias_pool[0:1, :], ib[0:1, :])
         q_rows = query.rearrange("(p r) q -> p r q", r=PACK)
         q_raw = [sb.tile([P, PACK, Q // 2], F32, name="q_raw%d" % h, tag="q_raw%d" % h, align_bytes=64) for h in range(2)]
         for h in range(2):
@@ -63,23 +62,23 @@ def tile_attend_pairprefs_pl_kernel(tc, query, item_words, item_scales, ib, offs
         def slot_half(h):
             return slot_list[:, h * (BANK // 16) : (h + 1) * (BANK // 16)]
 
+        item_sc = sb.tile([P, I], U8, name="item_sc", align_bytes=64)
+        nc.vector.tensor_copy(item_sc[:], scale_pool[:].indirect(slot_list[:]))
         bias_row = [sb.tile([P, BANK], F32, name="bias_row%d" % h, align_bytes=64) for h in range(HALVES)]
         for h in range(HALVES):
             nc.vector.tensor_copy(bias_row[h][:], bias_pool[:].indirect(slot_half(h)))
-        item_sc = sb.tile([P, I], U8, name="item_sc", align_bytes=64)
-        nc.vector.tensor_copy(item_sc[:], scale_pool[:].indirect(slot_list[:]))
 
-        q_bf = sb.tile([P, Q * PACK], BF16, name="q_bf", align_bytes=64)
-        q_dealt = q_bf[:].rearrange("p (t m r) -> p m t r", t=PACK, r=PACK)
+        q_bf = sb.tile([P, Q * PACK], BF16, name="q_bf", tag="q_bf", align_bytes=64)
+        q_dealt = q_bf[:].rearrange("p (t m r) -> p m r t", t=PACK, r=PACK)
         for h in range(2):
-            nc.scalar.copy(q_dealt[:, h * (P // 2) : (h + 1) * (P // 2)], q_raw[h][:].rearrange("p r (m t) -> p m t r", t=PACK))
-        q_cd = sb.tile([P, Q], U32, name="q_cd", align_bytes=64)
+            nc.scalar.copy(q_dealt[:, h * (P // 2) : (h + 1) * (P // 2)], q_raw[h][:].rearrange("p r (m t) -> p m r t", t=PACK))
+        q_cd = sb.tile([P, Q], U32, name="q_cd", tag="bias_pool", align_bytes=64)
         q_sc = sb.tile([P, Q], U8, name="q_sc", align_bytes=64)
         nc.vector.quantize_mx(out=q_cd[:].bitcast(FP8X4), scales=q_sc[:], in_=q_bf[:])
 
-        item_cd = [sb.tile([P, BANK], U32, name="item_cd%d" % h, align_bytes=64) for h in range(HALVES)]
+        item_cd = sb.tile([P, I], U32, name="item_cd", tag="q_bf", align_bytes=64)
         for h in range(HALVES):
-            nc.vector.tensor_copy(item_cd[h][:], word_pool[:].indirect(slot_half(h)))
+            nc.vector.tensor_copy(item_cd[:, h * BANK : (h + 1) * BANK], word_pool[:].indirect(slot_half(h)))
 
         bias_col = sb.tile([P, HALVES * BLOCKS], F32, name="bias_col", tag="q_raw0", align_bytes=64)
         bias_all = [sb.tile([P, BANK], F32, name="bias_all%d" % h, align_bytes=64) for h in range(HALVES)]
@@ -106,50 +105,55 @@ def tile_attend_pairprefs_pl_kernel(tc, query, item_words, item_scales, ib, offs
                     out=acc[:],
                     lhsT=q_cd[:, rows].bitcast(FP8X4),
                     lhsT_scale=q_sc[:, rows],
-                    rhs=item_cd[h][:].bitcast(FP8X4),
+                    rhs=item_cd[:, cols].bitcast(FP8X4),
                     rhs_scale=item_sc[:, cols],
                     start=True,
                     stop=True,
                 )
                 nc.vector.tensor_tensor(scores[t][:, cols], acc[:], bias_all[h][:], ALU.add)
 
-        def score_by_slot(t):
-            rows = slice(t * P, (t + 1) * P)
-            by_slot = sb.tile([P, I], F32, name="by_slot%d" % t, tag="by_slot%d" % t, align_bytes=64)
-            for h in range(HALVES):
+        def score_by_slot(first, count):
+            width = count * P
+            users = slice(first * P, first * P + width)
+            by_slot = sb.tile([P, HALVES * BLOCKS * width], F32, name="by_slot%d" % first, tag="by_slot%d" % first, align_bytes=64)
+            per_bank = BANK // width
+            for c0 in range(0, HALVES * BLOCKS, per_bank):
                 acc = psum.tile([P, BANK], F32, name="acc_by_slot", tag="first")
-                for b in range(BLOCKS):
-                    c = h * BLOCKS + b
+                for b in range(per_bank):
+                    c = c0 + b
                     nc.tensor.matmul_mx(
-                        out=acc[:, b * P : (b + 1) * P],
-                        lhsT=item_cd[h][:, b * P : (b + 1) * P].bitcast(FP8X4),
+                        out=acc[:, b * width : (b + 1) * width],
+                        lhsT=item_cd[:, c * P : (c + 1) * P].bitcast(FP8X4),
                         lhsT_scale=item_sc[:, c * P : (c + 1) * P],
-                        rhs=q_cd[:, rows].bitcast(FP8X4),
-                        rhs_scale=q_sc[:, rows],
+                        rhs=q_cd[:, users].bitcast(FP8X4),
+                        rhs_scale=q_sc[:, users],
                         start=True,
                         stop=True,
                     )
-                for b in range(BLOCKS):
-                    c = h * BLOCKS + b
+                for b in range(per_bank):
+                    c = c0 + b
                     nc.scalar.activation(
-                        by_slot[:, c * P : (c + 1) * P], acc[:, b * P : (b + 1) * P], ACT.Identity, bias=bias_col[:, c : c + 1]
+                        by_slot[:, c * width : (c + 1) * width],
+                        acc[:, b * width : (b + 1) * width],
+                        ACT.Identity,
+                        bias=bias_col[:, c : c + 1],
                     )
             return by_slot
 
-        def turn_back(t, by_slot):
-            for h in range(HALVES):
-                turned = psum.tile([P, BANK], F32, name="turned", tag="second")
-                for b in range(BLOCKS):
-                    c = h * BLOCKS + b
-                    nc.tensor.transpose(turned[:, b * P : (b + 1) * P], by_slot[:, c * P : (c + 1) * P], ident[:])
-                nc.scalar.copy(scores[t][:, h * BANK : (h + 1) * BANK], turned[:])
+        def turn_back(first, count, by_slot):
+            for k in range(count):
+                for h in range(HALVES):
+                    turned = psum.tile([P, BANK], F32, name="turned", tag="second")
+                    for b in range(BLOCKS):
+                        lo = ((h * BLOCKS + b) * count + k) * P
+                        nc.tensor.transpose(turned[:, b * P : (b + 1) * P], by_slot[:, lo : lo + P], ident[:])
+                    nc.scalar.copy(scores[first + k][:, h * BANK : (h + 1) * BANK], turned[:])
 
-        for t in range(DIRECT):
-            score_direct(t)
-        for t in range(DIRECT, PACK):
-            turn_back(t, score_by_slot(t))
+        score_direct(0)
+        for first, count in ((1, 1), (2, 2)):
+            turn_back(first, count, score_by_slot(first, count))
 
-        y = sb.tile([P, PACK, J], F32, name="y", tag="by_slot%d" % (PACK - 1), align_bytes=64)
+        y = sb.tile([P, 2, PACK, PAIR_HALF], F32, name="y", tag="by_slot2", align_bytes=64)
         y_rows = out_0.rearrange("(p t) j -> p t j", t=PACK)
         y_bf = sb.tile([P, J * PACK], BF16, name="y_bf", align_bytes=64)
         y_cd = sb.tile([P, J], U32, name="y_cd", align_bytes=64)
@@ -159,28 +163,27 @@ def tile_attend_pairprefs_pl_kernel(tc, query, item_words, item_scales, ib, offs
         diffs = {}
 
         def look_up(t, lo, hi):
-            second = sb.tile([P, hi - lo], F32, name="second%d_%d" % (t, lo), align_bytes=64)
+            second = sb.tile([P, hi - lo], F32, name="second%d_%d" % (t, lo), tag="second%d_%d" % (t, lo), align_bytes=64)
             nc.vector.tensor_copy(second[:], scores[t][:].indirect(second_list[:, lo // 16 : hi // 16]))
             return second
 
-        def prefer(t, lo, hi, second):
-            diff = sb.tile([P, hi - lo], F32, name="diff%d_%d" % (t, lo), align_bytes=64)
+        def prefer(t, lo, hi, second, tag=None):
+            diff = sb.tile([P, hi - lo], F32, name="diff%d_%d" % (t, lo), tag=tag or "diff%d_%d" % (t, lo), align_bytes=64)
             nc.vector.tensor_tensor(diff[:], scores[t][:].indirect(first_list[:, lo // 16 : hi // 16]), second[:], ALU.subtract)
             diffs[(t, lo)] = diff
-            nc.scalar.activation(y[:, t, lo:hi], diff[:], ACT.Sigmoid)
-            nc.sync.dma_start(y_rows[:, t, lo:hi], y[:, t, lo:hi])
+            nc.scalar.activation(y[:, lo // PAIR_HALF, t, :], diff[:], ACT.Sigmoid)
+            nc.sync.dma_start(y_rows[:, t, lo:hi], y[:, lo // PAIR_HALF, t, :])
 
         def round_pairs(copy, lo, hi):
-            copy(y_bf[:, lo * PACK : hi * PACK].rearrange("p (j t) -> p j t", t=PACK), y[:, :, lo:hi].rearrange("p t j -> p j t"))
+            half, first = divmod(lo, PAIR_HALF)
+            copy(
+                y_bf[:, lo * PACK : hi * PACK].rearrange("p (c i t) -> p c t i", i=4, t=PACK),
+                y[:, half, :, first : first + hi - lo].rearrange("p t (c i) -> p c t i", i=4),
+            )
 
         def quantise_pairs(lo, hi):
             nc.vector.quantize_mx(out=y_cd[:, lo:hi].bitcast(FP8X4), scales=y_sc[:, lo:hi], in_=y_bf[:, lo * PACK : hi * PACK])
             nc.sync.dma_start(words_out[:, lo:hi], y_cd[:, lo:hi].bitcast(I32))
-
-        def two_tiles(t, lo, hi):
-            seconds = [look_up(t + k, lo, hi) for k in range(2)]
-            for k in range(2):
-                prefer(t + k, lo, hi, seconds[k])
 
         def both_halves(t):
             halves = (0, PAIR_HALF)

@@ -82,13 +82,14 @@ def tile_attend_pairprefs_pl_kernel(tc, query, item_words, item_scales, ib, offs
 
         bias_col = sb.tile([P, HALVES * BLOCKS], F32, name="bias_col", tag="q_raw0", align_bytes=64)
         bias_all = [sb.tile([P, BANK], F32, name="bias_all%d" % h, align_bytes=64) for h in range(HALVES)]
+        spreads = [psum.tile([P, BANK], F32, name="bias_spread", tag="first") for h in range(HALVES)]
         for h in range(HALVES):
             turned = psum.tile([P, BANK], F32, name="bias_turned", tag="first")
             for b in range(BLOCKS):
                 nc.tensor.transpose(turned[:, b * P : (b + 1) * P], bias_row[h][:, b * P : (b + 1) * P], ident[:])
             nc.scalar.copy(bias_col[:, h * BLOCKS : (h + 1) * BLOCKS], turned[:, 0:BANK:P])
         for h in range(HALVES):
-            spread = psum.tile([P, BANK], F32, name="bias_spread", tag="second")
+            spread = spreads[h]
             for b in range(BLOCKS):
                 c = h * BLOCKS + b
                 nc.tensor.transpose(spread[:, b * P : (b + 1) * P], bias_col[:, c : c + 1].to_broadcast([P, P]), ident[:])
@@ -96,64 +97,58 @@ def tile_attend_pairprefs_pl_kernel(tc, query, item_words, item_scales, ib, offs
 
         scores = [sb.tile([P, I], F32, name="scores%d" % t, align_bytes=64) for t in range(PACK)]
 
-        def score_direct(t):
-            rows = slice(t * P, (t + 1) * P)
-            for h in range(HALVES):
-                cols = slice(h * BANK, (h + 1) * BANK)
-                acc = psum.tile([P, BANK], F32, name="acc", tag="second")
+        def score_direct(h):
+            cols = slice(h * BANK, (h + 1) * BANK)
+            acc = psum.tile([P, BANK], F32, name="acc", tag="first")
+            nc.tensor.matmul_mx(
+                out=acc[:],
+                lhsT=q_cd[:, 0:P].bitcast(FP8X4),
+                lhsT_scale=q_sc[:, 0:P],
+                rhs=item_cd[:, cols].bitcast(FP8X4),
+                rhs_scale=item_sc[:, cols],
+                start=True,
+                stop=True,
+            )
+            nc.vector.tensor_tensor(scores[0][:, cols], acc[:], bias_all[h][:], ALU.add)
+
+        by_slot = {t: sb.tile([P, I], F32, name="by_slot%d" % t, tag="by_slot%d" % t, align_bytes=64) for t in range(1, PACK)}
+
+        def score_by_slot(t, h):
+            users = slice(t * P, (t + 1) * P)
+            acc = psum.tile([P, BANK], F32, name="acc_by_slot", tag="first")
+            for b in range(BLOCKS):
+                slots = slice(h * BANK + b * P, h * BANK + (b + 1) * P)
                 nc.tensor.matmul_mx(
-                    out=acc[:],
-                    lhsT=q_cd[:, rows].bitcast(FP8X4),
-                    lhsT_scale=q_sc[:, rows],
-                    rhs=item_cd[:, cols].bitcast(FP8X4),
-                    rhs_scale=item_sc[:, cols],
+                    out=acc[:, b * P : (b + 1) * P],
+                    lhsT=item_cd[:, slots].bitcast(FP8X4),
+                    lhsT_scale=item_sc[:, slots],
+                    rhs=q_cd[:, users].bitcast(FP8X4),
+                    rhs_scale=q_sc[:, users],
                     start=True,
                     stop=True,
                 )
-                nc.vector.tensor_tensor(scores[t][:, cols], acc[:], bias_all[h][:], ALU.add)
+            for b in range(BLOCKS):
+                c = h * BLOCKS + b
+                nc.scalar.activation(
+                    by_slot[t][:, c * P : (c + 1) * P], acc[:, b * P : (b + 1) * P], ACT.Identity, bias=bias_col[:, c : c + 1]
+                )
 
-        def score_by_slot(first, count):
-            width = count * P
-            users = slice(first * P, first * P + width)
-            by_slot = sb.tile([P, HALVES * BLOCKS * width], F32, name="by_slot%d" % first, tag="by_slot%d" % first, align_bytes=64)
-            per_bank = BANK // width
-            for c0 in range(0, HALVES * BLOCKS, per_bank):
-                acc = psum.tile([P, BANK], F32, name="acc_by_slot", tag="first")
-                for b in range(per_bank):
-                    c = c0 + b
-                    nc.tensor.matmul_mx(
-                        out=acc[:, b * width : (b + 1) * width],
-                        lhsT=item_cd[:, c * P : (c + 1) * P].bitcast(FP8X4),
-                        lhsT_scale=item_sc[:, c * P : (c + 1) * P],
-                        rhs=q_cd[:, users].bitcast(FP8X4),
-                        rhs_scale=q_sc[:, users],
-                        start=True,
-                        stop=True,
-                    )
-                for b in range(per_bank):
-                    c = c0 + b
-                    nc.scalar.activation(
-                        by_slot[:, c * width : (c + 1) * width],
-                        acc[:, b * width : (b + 1) * width],
-                        ACT.Identity,
-                        bias=bias_col[:, c : c + 1],
-                    )
-            return by_slot
+        def turn_back(t):
+            for h in range(HALVES):
+                turned = psum.tile([P, BANK], F32, name="turned", tag="second")
+                for b in range(BLOCKS):
+                    c = h * BLOCKS + b
+                    nc.tensor.transpose(turned[:, b * P : (b + 1) * P], by_slot[t][:, c * P : (c + 1) * P], ident[:])
+                nc.scalar.copy(scores[t][:, h * BANK : (h + 1) * BANK], turned[:])
 
-        def turn_back(first, count, by_slot):
-            for k in range(count):
-                for h in range(HALVES):
-                    turned = psum.tile([P, BANK], F32, name="turned", tag="second")
-                    for b in range(BLOCKS):
-                        lo = ((h * BLOCKS + b) * count + k) * P
-                        nc.tensor.transpose(turned[:, b * P : (b + 1) * P], by_slot[:, lo : lo + P], ident[:])
-                    nc.scalar.copy(scores[first + k][:, h * BANK : (h + 1) * BANK], turned[:])
+        for t in range(1, PACK):
+            for h in range(HALVES):
+                if t == 1:
+                    score_direct(h)
+                score_by_slot(t, h)
+            turn_back(t)
 
-        score_direct(0)
-        for first, count in ((1, 1), (2, 2)):
-            turn_back(first, count, score_by_slot(first, count))
-
-        y = sb.tile([P, 2, PACK, PAIR_HALF], F32, name="y", tag="by_slot2", align_bytes=64)
+        y = sb.tile([P, 2, PACK, PAIR_HALF], F32, name="y", tag="by_slot3", align_bytes=64)
         y_rows = out_0.rearrange("(p t) j -> p t j", t=PACK)
         y_bf = sb.tile([P, J * PACK], BF16, name="y_bf", align_bytes=64)
         y_cd = sb.tile([P, J], U32, name="y_cd", align_bytes=64)

@@ -19,6 +19,7 @@ ALU = mybir.AluOpType
 P = 128
 PACK = 4
 BANK = 512
+LAST = 96
 BLOCKS = BANK // P
 HALVES = I // BANK
 DIRECT = 1
@@ -39,14 +40,14 @@ def tile_attend_pairprefs_pl_kernel(tc, query, item_words, item_scales, ib, offs
         nc.sync.dma_start(slot_list[:], offs)
 
         scale_pool = sb.tile([P, T], U8, name="scale_pool", align_bytes=64)
-        for quad in range(4):
-            nc.sync.dma_start(
-                scale_pool[32 * quad : 32 * quad + 32, :].bitcast(I32),
-                item_scales[:, 4 * quad : 4 * quad + 4, :].bitcast(I32).broadcast_to([8, 4, T // 4]),
-            )
+        nc.vector.memset(scale_pool[0:LAST, :].bitcast(I32), 0)
+        nc.sync.dma_start(
+            scale_pool[LAST:P, :].bitcast(I32),
+            item_scales[0].bitcast(I32).unsqueeze(1).broadcast_to([16, 2, T // 4]),
+        )
         bias_pool = sb.tile([P, T], F32, name="bias_pool", tag="bias_pool", align_bytes=64)
-        nc.vector.memset(bias_pool[:].bitcast(I32), 0)
-        nc.scalar.dma_start(bias_pool[0:1, :], ib[0:1, :])
+        nc.vector.memset(bias_pool[0:LAST, :].bitcast(I32), 0)
+        nc.sync.dma_start(bias_pool[LAST:P, :], ib[LAST:P, :])
         q_rows = query.rearrange("(p r) q -> p r q", r=PACK)
         q_raw = [sb.tile([P, PACK, Q // 2], F32, name="q_raw%d" % h, tag="q_raw%d" % h, align_bytes=64) for h in range(2)]
         for h in range(2):
@@ -62,8 +63,15 @@ def tile_attend_pairprefs_pl_kernel(tc, query, item_words, item_scales, ib, offs
         def slot_half(h):
             return slot_list[:, h * (BANK // 16) : (h + 1) * (BANK // 16)]
 
+        picked_sc = sb.tile([P, I], U8, name="picked_sc", align_bytes=64)
+        nc.vector.tensor_copy(picked_sc[:], scale_pool[:].indirect(slot_list[:]))
         item_sc = sb.tile([P, I], U8, name="item_sc", align_bytes=64)
-        nc.vector.tensor_copy(item_sc[:], scale_pool[:].indirect(slot_list[:]))
+        nc.gpsimd.memset(item_sc[:].bitcast(I32), 0)
+        for quad in range(4):
+            nc.sync.dma_start(
+                item_sc[32 * quad : 32 * quad + 4, :].bitcast(I32),
+                picked_sc[LAST + 8 * quad : LAST + 8 * quad + 8 : 2, :].bitcast(I32),
+            )
         bias_row = [sb.tile([P, BANK], F32, name="bias_row%d" % h, align_bytes=64) for h in range(HALVES)]
         for h in range(HALVES):
             nc.vector.tensor_copy(bias_row[h][:], bias_pool[:].indirect(slot_half(h)))
@@ -87,7 +95,7 @@ def tile_attend_pairprefs_pl_kernel(tc, query, item_words, item_scales, ib, offs
             turned = psum.tile([P, BANK], F32, name="bias_turned", tag="first")
             for b in range(BLOCKS):
                 nc.tensor.transpose(turned[:, b * P : (b + 1) * P], bias_row[h][:, b * P : (b + 1) * P], ident[:])
-            nc.scalar.copy(bias_col[:, h * BLOCKS : (h + 1) * BLOCKS], turned[:, 0:BANK:P])
+            nc.scalar.copy(bias_col[:, h * BLOCKS : (h + 1) * BLOCKS], turned[:, LAST:BANK:P])
         for h in range(HALVES):
             spread = spreads[h]
             for b in range(BLOCKS):

@@ -19,12 +19,13 @@ ALU = mybir.AluOpType
 P = 128
 PACK = 4
 BANK = 512
-LAST = 96
+SCALE_ROW = P - 16
+BIAS_ROW = P - 1
 BLOCKS = BANK // P
 HALVES = I // BANK
 DIRECT = 1
 PAIR_HALF = J // 2
-VECTOR_SHARE = 96
+SCALAR_SHARE = (64, 128)
 
 
 def tile_attend_pairprefs_pl_kernel(tc, query, item_words, item_scales, ib, offs, offs2, offs3, out_0, out_1, out_2):
@@ -40,19 +41,16 @@ def tile_attend_pairprefs_pl_kernel(tc, query, item_words, item_scales, ib, offs
         nc.sync.dma_start(slot_list[:], offs)
 
         scale_pool = sb.tile([P, T], U8, name="scale_pool", align_bytes=64)
-        nc.vector.memset(scale_pool[0:LAST, :].bitcast(I32), 0)
-        nc.sync.dma_start(
-            scale_pool[LAST:P, :].bitcast(I32),
-            item_scales[0].bitcast(I32).unsqueeze(1).broadcast_to([16, 2, T // 4]),
-        )
+        nc.gpsimd.memset(scale_pool[0:SCALE_ROW, :].bitcast(I32), 0)
+        nc.sync.dma_start(scale_pool[SCALE_ROW:P, :].bitcast(I32), item_scales[0].bitcast(I32))
         bias_pool = sb.tile([P, T], F32, name="bias_pool", tag="bias_pool", align_bytes=64)
-        nc.vector.memset(bias_pool[0:LAST, :].bitcast(I32), 0)
-        nc.sync.dma_start(bias_pool[LAST:P, :], ib[LAST:P, :])
+        nc.vector.memset(bias_pool[0:BIAS_ROW, :].bitcast(I32), 0)
+        nc.sync.dma_start(bias_pool[BIAS_ROW:P, :], ib[0:1, :])
         q_rows = query.rearrange("(p r) q -> p r q", r=PACK)
         q_raw = [sb.tile([P, PACK, Q // 2], F32, name="q_raw%d" % h, tag="q_raw%d" % h, align_bytes=64) for h in range(2)]
         for h in range(2):
             nc.sync.dma_start(q_raw[h][:], q_rows[:, :, h * (Q // 2) : (h + 1) * (Q // 2)])
-        word_pool = sb.tile([P, T], U32, name="word_pool", align_bytes=64)
+        word_pool = sb.tile([P, T], U32, name="word_pool", tag="word_pool", align_bytes=64)
         nc.sync.dma_start(word_pool[:].bitcast(I32), item_words[0].rearrange("p n t -> p (n t)").bitcast(I32))
         nc.sync.dma_start(first_list[:], offs2)
         nc.sync.dma_start(second_list[:], offs3)
@@ -70,7 +68,7 @@ def tile_attend_pairprefs_pl_kernel(tc, query, item_words, item_scales, ib, offs
         for quad in range(4):
             nc.sync.dma_start(
                 item_sc[32 * quad : 32 * quad + 4, :].bitcast(I32),
-                picked_sc[LAST + 8 * quad : LAST + 8 * quad + 8 : 2, :].bitcast(I32),
+                picked_sc[SCALE_ROW + 4 * quad : SCALE_ROW + 4 * quad + 4, :].bitcast(I32),
             )
         bias_row = [sb.tile([P, BANK], F32, name="bias_row%d" % h, align_bytes=64) for h in range(HALVES)]
         for h in range(HALVES):
@@ -80,28 +78,38 @@ def tile_attend_pairprefs_pl_kernel(tc, query, item_words, item_scales, ib, offs
         q_dealt = q_bf[:].rearrange("p (t m r) -> p m r t", t=PACK, r=PACK)
         for h in range(2):
             nc.scalar.copy(q_dealt[:, h * (P // 2) : (h + 1) * (P // 2)], q_raw[h][:].rearrange("p r (m t) -> p m r t", t=PACK))
-        q_cd = sb.tile([P, Q], U32, name="q_cd", tag="bias_pool", align_bytes=64)
+        q_early = sb.tile([P, 2 * P], U32, name="q_early", align_bytes=64)
         q_sc = sb.tile([P, Q], U8, name="q_sc", align_bytes=64)
-        nc.vector.quantize_mx(out=q_cd[:].bitcast(FP8X4), scales=q_sc[:], in_=q_bf[:])
+        nc.vector.quantize_mx(out=q_early[:].bitcast(FP8X4), scales=q_sc[:, 0 : 2 * P], in_=q_bf[:, 0 : 2 * P * PACK])
 
-        item_cd = sb.tile([P, I], U32, name="item_cd", tag="q_bf", align_bytes=64)
+        item_cd = sb.tile([P, I], U32, name="item_cd", align_bytes=64)
         for h in range(HALVES):
             nc.vector.tensor_copy(item_cd[:, h * BANK : (h + 1) * BANK], word_pool[:].indirect(slot_half(h)))
 
-        bias_col = sb.tile([P, HALVES * BLOCKS], F32, name="bias_col", tag="q_raw0", align_bytes=64)
+        bias_col = sb.tile([P, HALVES * BLOCKS], F32, name="bias_col", tag="q_raw1", align_bytes=64)
         bias_all = [sb.tile([P, BANK], F32, name="bias_all%d" % h, align_bytes=64) for h in range(HALVES)]
         spreads = [psum.tile([P, BANK], F32, name="bias_spread", tag="first") for h in range(HALVES)]
         for h in range(HALVES):
             turned = psum.tile([P, BANK], F32, name="bias_turned", tag="first")
             for b in range(BLOCKS):
                 nc.tensor.transpose(turned[:, b * P : (b + 1) * P], bias_row[h][:, b * P : (b + 1) * P], ident[:])
-            nc.scalar.copy(bias_col[:, h * BLOCKS : (h + 1) * BLOCKS], turned[:, LAST:BANK:P])
+            nc.scalar.copy(bias_col[:, h * BLOCKS : (h + 1) * BLOCKS], turned[:, BIAS_ROW:BANK:P])
         for h in range(HALVES):
             spread = spreads[h]
             for b in range(BLOCKS):
                 c = h * BLOCKS + b
                 nc.tensor.transpose(spread[:, b * P : (b + 1) * P], bias_col[:, c : c + 1].to_broadcast([P, P]), ident[:])
             nc.scalar.copy(bias_all[h][:], spread[:])
+
+        q_late = sb.tile([P, 2 * P], U32, name="q_late", tag="word_pool", align_bytes=64)
+
+        def q_codes(t):
+            return (q_early if t < 2 else q_late)[:, (t % 2) * P : (t % 2 + 1) * P].bitcast(FP8X4)
+
+        def quantise_users(t):
+            nc.vector.quantize_mx(
+                out=q_codes(t), scales=q_sc[:, t * P : (t + 1) * P], in_=q_bf[:, t * P * PACK : (t + 1) * P * PACK]
+            )
 
         scores = [sb.tile([P, I], F32, name="scores%d" % t, align_bytes=64) for t in range(PACK)]
 
@@ -110,7 +118,7 @@ def tile_attend_pairprefs_pl_kernel(tc, query, item_words, item_scales, ib, offs
             acc = psum.tile([P, BANK], F32, name="acc", tag="first")
             nc.tensor.matmul_mx(
                 out=acc[:],
-                lhsT=q_cd[:, 0:P].bitcast(FP8X4),
+                lhsT=q_codes(0),
                 lhsT_scale=q_sc[:, 0:P],
                 rhs=item_cd[:, cols].bitcast(FP8X4),
                 rhs_scale=item_sc[:, cols],
@@ -130,7 +138,7 @@ def tile_attend_pairprefs_pl_kernel(tc, query, item_words, item_scales, ib, offs
                     out=acc[:, b * P : (b + 1) * P],
                     lhsT=item_cd[:, slots].bitcast(FP8X4),
                     lhsT_scale=item_sc[:, slots],
-                    rhs=q_cd[:, users].bitcast(FP8X4),
+                    rhs=q_codes(t),
                     rhs_scale=q_sc[:, users],
                     start=True,
                     stop=True,
@@ -153,6 +161,7 @@ def tile_attend_pairprefs_pl_kernel(tc, query, item_words, item_scales, ib, offs
             for h in range(HALVES):
                 if t == 1:
                     score_direct(h)
+                    quantise_users(2 + h)
                 score_by_slot(t, h)
             turn_back(t)
 
@@ -162,45 +171,55 @@ def tile_attend_pairprefs_pl_kernel(tc, query, item_words, item_scales, ib, offs
         y_cd = sb.tile([P, J], U32, name="y_cd", align_bytes=64)
         y_sc = sb.tile([P, J], U8, name="y_sc", align_bytes=64)
         words_out = out_1[0].rearrange("p c t -> p (c t)").bitcast(I32)
+        diff = [sb.tile([P, PACK, PAIR_HALF], F32, name="diff%d" % half, align_bytes=64) for half in range(2)]
 
-        diffs = {}
+        def pairs_of(half):
+            return slice(half * PAIR_HALF, (half + 1) * PAIR_HALF)
 
-        def look_up(t, lo, hi):
-            second = sb.tile([P, hi - lo], F32, name="second%d_%d" % (t, lo), tag="second%d_%d" % (t, lo), align_bytes=64)
-            nc.vector.tensor_copy(second[:], scores[t][:].indirect(second_list[:, lo // 16 : hi // 16]))
-            return second
+        def entries(pair_list, half):
+            return pair_list[:, half * (PAIR_HALF // 16) : (half + 1) * (PAIR_HALF // 16)]
 
-        def prefer(t, lo, hi, second, tag=None):
-            diff = sb.tile([P, hi - lo], F32, name="diff%d_%d" % (t, lo), tag=tag or "diff%d_%d" % (t, lo), align_bytes=64)
-            nc.vector.tensor_tensor(diff[:], scores[t][:].indirect(first_list[:, lo // 16 : hi // 16]), second[:], ALU.subtract)
-            diffs[(t, lo)] = diff
-            nc.scalar.activation(y[:, lo // PAIR_HALF, t, :], diff[:], ACT.Sigmoid)
-            nc.sync.dma_start(y_rows[:, t, lo:hi], y[:, lo // PAIR_HALF, t, :])
+        def differences(t):
+            seconds = [sb.tile([P, PAIR_HALF], F32, name="second%d_%d" % (t, half), align_bytes=64) for half in range(2)]
+            for half in range(2):
+                nc.vector.tensor_copy(seconds[half][:], scores[t][:].indirect(entries(second_list, half)))
+            for half in range(2):
+                nc.vector.tensor_tensor(
+                    diff[half][:, t, :], scores[t][:].indirect(entries(first_list, half)), seconds[half][:], ALU.subtract
+                )
 
-        def round_pairs(copy, lo, hi):
-            half, first = divmod(lo, PAIR_HALF)
-            copy(
-                y_bf[:, lo * PACK : hi * PACK].rearrange("p (c i t) -> p c t i", i=4, t=PACK),
-                y[:, half, :, first : first + hi - lo].rearrange("p t (c i) -> p c t i", i=4),
+        def prefer(half, lo, hi):
+            nc.scalar.activation(y[:, half, lo:hi, :], diff[half][:, lo:hi, :], ACT.Sigmoid)
+            nc.sync.dma_start(y_rows[:, lo:hi, pairs_of(half)], y[:, half, lo:hi, :])
+
+        def woven(half, lo, hi):
+            first = half * PAIR_HALF
+            return y_bf[:, (first + lo) * PACK : (first + hi) * PACK].rearrange("p (c i t) -> p c t i", i=4, t=PACK)
+
+        def round_on_scalar(half, lo, hi):
+            nc.scalar.activation(woven(half, lo, hi), diff[half][:, :, lo:hi].rearrange("p t (c i) -> p c t i", i=4), ACT.Sigmoid)
+
+        def round_on_vector(half, lo, hi):
+            nc.vector.tensor_copy(woven(half, lo, hi), y[:, half, :, lo:hi].rearrange("p t (c i) -> p c t i", i=4))
+
+        def quantise(half):
+            cols = pairs_of(half)
+            nc.vector.quantize_mx(
+                out=y_cd[:, cols].bitcast(FP8X4), scales=y_sc[:, cols], in_=y_bf[:, cols.start * PACK : cols.stop * PACK]
             )
-
-        def quantise_pairs(lo, hi):
-            nc.vector.quantize_mx(out=y_cd[:, lo:hi].bitcast(FP8X4), scales=y_sc[:, lo:hi], in_=y_bf[:, lo * PACK : hi * PACK])
-            nc.sync.dma_start(words_out[:, lo:hi], y_cd[:, lo:hi].bitcast(I32))
-
-        def both_halves(t):
-            halves = (0, PAIR_HALF)
-            seconds = [look_up(t, lo, lo + PAIR_HALF) for lo in halves]
-            for lo, second in zip(halves, seconds):
-                prefer(t, lo, lo + PAIR_HALF, second)
+            nc.sync.dma_start(words_out[:, cols], y_cd[:, cols].bitcast(I32))
 
         for t in range(PACK):
-            both_halves(t)
-        round_pairs(nc.vector.tensor_copy, 0, PAIR_HALF)
-        quantise_pairs(0, PAIR_HALF)
-        round_pairs(nc.vector.tensor_copy, PAIR_HALF, PAIR_HALF + VECTOR_SHARE)
-        round_pairs(nc.scalar.copy, PAIR_HALF + VECTOR_SHARE, J)
-        quantise_pairs(PAIR_HALF, J)
+            differences(t)
+        for half in range(2):
+            prefer(half, 0, PACK - 1)
+        for half in range(2):
+            prefer(half, PACK - 1, PACK)
+            round_on_scalar(half, 0, SCALAR_SHARE[half])
+        for half in range(2):
+            round_on_vector(half, SCALAR_SHARE[half], PAIR_HALF)
+        for half in range(2):
+            quantise(half)
         for quad in range(4):
             queue = nc.scalar if quad % 2 else nc.sync
             queue.dma_start(

@@ -19,7 +19,6 @@ ALU = mybir.AluOpType
 P = 128
 PACK = 4
 BANK = 512
-SCALE_ROW = P - 16
 BIAS_ROW = P - 1
 BLOCKS = BANK // P
 HALVES = I // BANK
@@ -40,16 +39,20 @@ def tile_attend_pairprefs_pl_kernel(tc, query, item_words, item_scales, ib, offs
         second_list = lists.tile([P, J // 16], U16, name="second_list")
         nc.sync.dma_start(slot_list[:], offs)
 
-        scale_pool = sb.tile([P, T], U8, name="scale_pool", align_bytes=64)
-        nc.gpsimd.memset(scale_pool[0:SCALE_ROW, :].bitcast(I32), 0)
-        nc.sync.dma_start(scale_pool[SCALE_ROW:P, :].bitcast(I32), item_scales[0].bitcast(I32))
         bias_pool = sb.tile([P, T], F32, name="bias_pool", tag="bias_pool", align_bytes=64)
         nc.vector.memset(bias_pool[0:BIAS_ROW, :].bitcast(I32), 0)
         nc.sync.dma_start(bias_pool[BIAS_ROW:P, :], ib[0:1, :])
         q_rows = query.rearrange("(p r) q -> p r q", r=PACK)
         q_raw = [sb.tile([P, PACK, Q // 2], F32, name="q_raw%d" % h, tag="q_raw%d" % h, align_bytes=64) for h in range(2)]
-        for h in range(2):
-            nc.sync.dma_start(q_raw[h][:], q_rows[:, :, h * (Q // 2) : (h + 1) * (Q // 2)])
+        nc.sync.dma_start(q_raw[0][:], q_rows[:, :, 0 : Q // 2])
+        scale_pool = sb.tile([P, T], U8, name="scale_pool", align_bytes=64)
+        nc.gpsimd.memset(scale_pool[:].bitcast(I32), 0)
+        for quad in range(4):
+            nc.sync.dma_start(
+                scale_pool[32 * quad : 32 * quad + 4, :].bitcast(I32),
+                item_scales[0, 4 * quad : 4 * quad + 4, :].bitcast(I32),
+            )
+        nc.sync.dma_start(q_raw[1][:], q_rows[:, :, Q // 2 : Q])
         word_pool = sb.tile([P, T], U32, name="word_pool", tag="word_pool", align_bytes=64)
         nc.sync.dma_start(word_pool[:].bitcast(I32), item_words[0].rearrange("p n t -> p (n t)").bitcast(I32))
         nc.sync.dma_start(first_list[:], offs2)
@@ -61,18 +64,11 @@ def tile_attend_pairprefs_pl_kernel(tc, query, item_words, item_scales, ib, offs
         def slot_half(h):
             return slot_list[:, h * (BANK // 16) : (h + 1) * (BANK // 16)]
 
-        picked_sc = sb.tile([P, I], U8, name="picked_sc", align_bytes=64)
-        nc.vector.tensor_copy(picked_sc[:], scale_pool[:].indirect(slot_list[:]))
-        item_sc = sb.tile([P, I], U8, name="item_sc", align_bytes=64)
-        nc.gpsimd.memset(item_sc[:].bitcast(I32), 0)
-        for quad in range(4):
-            nc.sync.dma_start(
-                item_sc[32 * quad : 32 * quad + 4, :].bitcast(I32),
-                picked_sc[SCALE_ROW + 4 * quad : SCALE_ROW + 4 * quad + 4, :].bitcast(I32),
-            )
         bias_row = [sb.tile([P, BANK], F32, name="bias_row%d" % h, align_bytes=64) for h in range(HALVES)]
         for h in range(HALVES):
             nc.vector.tensor_copy(bias_row[h][:], bias_pool[:].indirect(slot_half(h)))
+        item_sc = sb.tile([P, I], U8, name="item_sc", align_bytes=64)
+        nc.vector.tensor_copy(item_sc[:], scale_pool[:].indirect(slot_list[:]))
 
         q_bf = sb.tile([P, Q * PACK], BF16, name="q_bf", tag="q_bf", align_bytes=64)
         q_dealt = q_bf[:].rearrange("p (t m r) -> p m r t", t=PACK, r=PACK)
@@ -82,11 +78,11 @@ def tile_attend_pairprefs_pl_kernel(tc, query, item_words, item_scales, ib, offs
         q_sc = sb.tile([P, Q], U8, name="q_sc", align_bytes=64)
         nc.vector.quantize_mx(out=q_early[:].bitcast(FP8X4), scales=q_sc[:, 0 : 2 * P], in_=q_bf[:, 0 : 2 * P * PACK])
 
-        item_cd = sb.tile([P, I], U32, name="item_cd", align_bytes=64)
+        item_cd = sb.tile([P, I], U32, name="item_cd", tag="q_raw1", align_bytes=64)
         for h in range(HALVES):
             nc.vector.tensor_copy(item_cd[:, h * BANK : (h + 1) * BANK], word_pool[:].indirect(slot_half(h)))
 
-        bias_col = sb.tile([P, HALVES * BLOCKS], F32, name="bias_col", tag="q_raw1", align_bytes=64)
+        bias_col = sb.tile([P, HALVES * BLOCKS], F32, name="bias_col", tag="q_raw0", align_bytes=64)
         bias_all = [sb.tile([P, BANK], F32, name="bias_all%d" % h, align_bytes=64) for h in range(HALVES)]
         spreads = [psum.tile([P, BANK], F32, name="bias_spread", tag="first") for h in range(HALVES)]
         for h in range(HALVES):

@@ -58,6 +58,10 @@ def tile_attend_pairprefs_pl_kernel(tc, query, item_words, item_scales, ib, offs
         nc.sync.dma_start(first_list[:], offs2)
         nc.sync.dma_start(second_list[:], offs3)
 
+        warm_in = sb.tile([P, 1], F32, name="warm_in", align_bytes=64)
+        warm_out = sb.tile([P, 1], F32, name="warm_out", align_bytes=64)
+        nc.gpsimd.memset(warm_in[:], 0.0)
+        nc.scalar.activation(warm_out[:], warm_in[:], ACT.Sigmoid)
         ident = sb.tile([P, P], F32, name="ident", align_bytes=64)
         make_identity(nc, ident[:])
 

@@ -22,9 +22,11 @@ BANK = 512
 BIAS_ROW = P - 1
 BLOCKS = BANK // P
 HALVES = I // BANK
-DIRECT = 1
 PAIR_HALF = J // 2
-SCALAR_SHARE = (64, 128)
+CHUNK = J // 4
+LIST_ROWS = 16
+QUARTER = I // 4
+EARLY_SCALES = 3 * QUARTER
 
 
 def tile_attend_pairprefs_pl_kernel(tc, query, item_words, item_scales, ib, offs, offs2, offs3, out_0, out_1, out_2):
@@ -32,19 +34,27 @@ def tile_attend_pairprefs_pl_kernel(tc, query, item_words, item_scales, ib, offs
     with ExitStack() as ctx:
         lists = ctx.enter_context(tc.tile_pool(name="lists", bufs=1))
         sb = ctx.enter_context(tc.tile_pool(name="sb", bufs=1))
-        psum = ctx.enter_context(tc.psum_pool(name="psum", bufs=4))
+        reused = ctx.enter_context(tc.tile_pool(name="reused", bufs=1))
+        ring = ctx.enter_context(tc.tile_pool(name="ring", bufs=1))
+        psum2 = ctx.enter_context(tc.psum_pool(name="psum2", bufs=2))
+        psum4 = ctx.enter_context(tc.psum_pool(name="psum4", bufs=4))
 
-        slot_list = lists.tile([P, I // 16], U16, name="slot_list")
-        first_list = lists.tile([P, J // 16], U16, name="first_list")
-        second_list = lists.tile([P, J // 16], U16, name="second_list")
+        def entries(tile, lo, hi):
+            return tile[:, lo // LIST_ROWS : hi // LIST_ROWS]
+
+        slot_list = lists.tile([P, I // LIST_ROWS], U16, name="slot_list")
+        first_list = lists.tile([P, J // LIST_ROWS], U16, name="first_list")
+        second_list = lists.tile([P, J // LIST_ROWS], U16, name="second_list")
         nc.sync.dma_start(slot_list[:], offs)
 
-        bias_pool = sb.tile([P, T], F32, name="bias_pool", tag="bias_pool", align_bytes=64)
+        bias_pool = sb.tile([P, T], F32, name="bias_pool", align_bytes=64)
         nc.vector.memset(bias_pool[0:BIAS_ROW, :].bitcast(I32), 0)
         nc.sync.dma_start(bias_pool[BIAS_ROW:P, :], ib[0:1, :])
         q_rows = query.rearrange("(p r) q -> p r q", r=PACK)
-        q_raw = [sb.tile([P, PACK, Q // 2], F32, name="q_raw%d" % h, tag="q_raw%d" % h, align_bytes=64) for h in range(2)]
-        nc.sync.dma_start(q_raw[0][:], q_rows[:, :, 0 : Q // 2])
+        q_raw0 = sb.tile([P, PACK, Q // 2], F32, name="q_raw0", align_bytes=64)
+        q_raw1 = reused.tile([P, PACK + 1, Q // 2], F32, name="q_raw1", offset=0, align_bytes=64)
+        q_raw = [q_raw0[:], q_raw1[:, 0:PACK, :]]
+        nc.sync.dma_start(q_raw0[:], q_rows[:, :, 0 : Q // 2])
         scale_pool = sb.tile([P, T], U8, name="scale_pool", align_bytes=64)
         nc.gpsimd.memset(scale_pool[:].bitcast(I32), 0)
         for quad in range(4):
@@ -52,8 +62,8 @@ def tile_attend_pairprefs_pl_kernel(tc, query, item_words, item_scales, ib, offs
                 scale_pool[32 * quad : 32 * quad + 4, :].bitcast(I32),
                 item_scales[0, 4 * quad : 4 * quad + 4, :].bitcast(I32),
             )
-        nc.sync.dma_start(q_raw[1][:], q_rows[:, :, Q // 2 : Q])
-        word_pool = sb.tile([P, T], U32, name="word_pool", tag="word_pool", align_bytes=64)
+        nc.sync.dma_start(q_raw[1], q_rows[:, :, Q // 2 : Q])
+        word_pool = sb.tile([P, T], U32, name="word_pool", align_bytes=64)
         nc.sync.dma_start(word_pool[:].bitcast(I32), item_words[0].rearrange("p n t -> p (n t)").bitcast(I32))
         nc.sync.dma_start(first_list[:], offs2)
         nc.sync.dma_start(second_list[:], offs3)
@@ -65,161 +75,186 @@ def tile_attend_pairprefs_pl_kernel(tc, query, item_words, item_scales, ib, offs
         ident = sb.tile([P, P], F32, name="ident", align_bytes=64)
         make_identity(nc, ident[:])
 
-        def slot_half(h):
-            return slot_list[:, h * (BANK // 16) : (h + 1) * (BANK // 16)]
-
         bias_row = [sb.tile([P, BANK], F32, name="bias_row%d" % h, align_bytes=64) for h in range(HALVES)]
         for h in range(HALVES):
-            nc.vector.tensor_copy(bias_row[h][:], bias_pool[:].indirect(slot_half(h)))
-        item_sc = sb.tile([P, I], U8, name="item_sc", align_bytes=64)
-        nc.vector.tensor_copy(item_sc[:], scale_pool[:].indirect(slot_list[:]))
+            nc.vector.tensor_copy(bias_row[h][:], bias_pool[:].indirect(entries(slot_list, h * BANK, (h + 1) * BANK)))
+        item_sc0 = sb.tile([P, EARLY_SCALES], U8, name="item_sc0", align_bytes=64)
+        nc.vector.tensor_copy(item_sc0[:], scale_pool[:].indirect(entries(slot_list, 0, EARLY_SCALES)))
 
-        q_bf = sb.tile([P, Q * PACK], BF16, name="q_bf", tag="q_bf", align_bytes=64)
+        q_bf = sb.tile([P, Q * PACK], BF16, name="q_bf", align_bytes=64)
         q_dealt = q_bf[:].rearrange("p (t m r) -> p m r t", t=PACK, r=PACK)
         for h in range(2):
-            nc.scalar.copy(q_dealt[:, h * (P // 2) : (h + 1) * (P // 2)], q_raw[h][:].rearrange("p r (m t) -> p m r t", t=PACK))
-        q_early = sb.tile([P, 2 * P], U32, name="q_early", align_bytes=64)
+            nc.scalar.copy(q_dealt[:, h * (P // 2) : (h + 1) * (P // 2)], q_raw[h].rearrange("p r (m t) -> p m r t", t=PACK))
+        q_cd = sb.tile([P, 3 * P], U32, name="q_cd", align_bytes=64)
         q_sc = sb.tile([P, Q], U8, name="q_sc", align_bytes=64)
-        nc.vector.quantize_mx(out=q_early[:].bitcast(FP8X4), scales=q_sc[:, 0 : 2 * P], in_=q_bf[:, 0 : 2 * P * PACK])
 
-        item_cd = sb.tile([P, I], U32, name="item_cd", tag="q_raw1", align_bytes=64)
-        for h in range(HALVES):
-            nc.vector.tensor_copy(item_cd[:, h * BANK : (h + 1) * BANK], word_pool[:].indirect(slot_half(h)))
+        def quantise_users(codes, lo, hi):
+            nc.vector.quantize_mx(out=codes.bitcast(FP8X4), scales=q_sc[:, lo:hi], in_=q_bf[:, lo * PACK : hi * PACK])
 
-        bias_col = sb.tile([P, HALVES * BLOCKS], F32, name="bias_col", tag="q_raw0", align_bytes=64)
-        bias_all = [sb.tile([P, BANK], F32, name="bias_all%d" % h, align_bytes=64) for h in range(HALVES)]
-        spreads = [psum.tile([P, BANK], F32, name="bias_spread", tag="first") for h in range(HALVES)]
+        for lo, hi in ((0, 2 * P), (2 * P, 3 * P)):
+            quantise_users(q_cd[:, lo:hi], lo, hi)
+
+        item_cd = reused.tile([P, I], U32, name="item_cd", offset=0, align_bytes=64)
+        item_sc1 = reused.tile([P, I - EARLY_SCALES], U8, name="item_sc1", offset=4096, align_bytes=64)
+
+        def gather_words(lo, hi):
+            nc.vector.tensor_copy(item_cd[:, lo:hi], word_pool[:].indirect(entries(slot_list, lo, hi)))
+
+        gather_words(0, BANK)
+        nc.vector.tensor_copy(item_sc1[:], scale_pool[:].indirect(entries(slot_list, EARLY_SCALES, I)))
+        gather_words(BANK, BANK + QUARTER)
+        gather_words(BANK + QUARTER, I)
+
+        bias_col = reused.tile([P, HALVES * BLOCKS], F32, name="bias_col", offset=4096 + 256, align_bytes=64)
+        bias_all = [sb.tile([P, BANK], F32, name="bias_all%d" % h, tag="bias_all%d" % h, align_bytes=64) for h in range(HALVES)]
         for h in range(HALVES):
-            turned = psum.tile([P, BANK], F32, name="bias_turned", tag="first")
+            turned = psum2.tile([P, BANK], F32, name="bias_turned", tag="direct")
             for b in range(BLOCKS):
                 nc.tensor.transpose(turned[:, b * P : (b + 1) * P], bias_row[h][:, b * P : (b + 1) * P], ident[:])
             nc.scalar.copy(bias_col[:, h * BLOCKS : (h + 1) * BLOCKS], turned[:, BIAS_ROW:BANK:P])
         for h in range(HALVES):
-            spread = spreads[h]
+            spread = psum2.tile([P, BANK], F32, name="bias_spread", tag="back")
             for b in range(BLOCKS):
                 c = h * BLOCKS + b
                 nc.tensor.transpose(spread[:, b * P : (b + 1) * P], bias_col[:, c : c + 1].to_broadcast([P, P]), ident[:])
             nc.scalar.copy(bias_all[h][:], spread[:])
 
-        q_late = sb.tile([P, 2 * P], U32, name="q_late", tag="word_pool", align_bytes=64)
-
-        def q_codes(t):
-            return (q_early if t < 2 else q_late)[:, (t % 2) * P : (t % 2 + 1) * P].bitcast(FP8X4)
-
-        def quantise_users(t):
-            nc.vector.quantize_mx(
-                out=q_codes(t), scales=q_sc[:, t * P : (t + 1) * P], in_=q_bf[:, t * P * PACK : (t + 1) * P * PACK]
-            )
-
         scores = [sb.tile([P, I], F32, name="scores%d" % t, align_bytes=64) for t in range(PACK)]
 
-        def score_direct(h):
-            cols = slice(h * BANK, (h + 1) * BANK)
-            acc = psum.tile([P, BANK], F32, name="acc", tag="first")
+        def product(out, stationary, moving):
             nc.tensor.matmul_mx(
-                out=acc[:],
-                lhsT=q_codes(0),
-                lhsT_scale=q_sc[:, 0:P],
-                rhs=item_cd[:, cols].bitcast(FP8X4),
-                rhs_scale=item_sc[:, cols],
+                out=out,
+                lhsT=stationary[0].bitcast(FP8X4),
+                lhsT_scale=stationary[1],
+                rhs=moving[0].bitcast(FP8X4),
+                rhs_scale=moving[1],
                 start=True,
                 stop=True,
             )
-            nc.vector.tensor_tensor(scores[0][:, cols], acc[:], bias_all[h][:], ALU.add)
 
-        by_slot = {t: sb.tile([P, I], F32, name="by_slot%d" % t, tag="by_slot%d" % t, align_bytes=64) for t in range(1, PACK)}
+        q_late = sb.tile([P, P], U32, name="q_late", tag="bias_all1", align_bytes=64)
+
+        def users(t):
+            return (q_late[:] if t == PACK - 1 else q_cd[:, t * P : (t + 1) * P]), q_sc[:, t * P : (t + 1) * P]
+
+        def items(lo, hi):
+            scales = item_sc0[:, lo:hi] if hi <= EARLY_SCALES else item_sc1[:, lo - EARLY_SCALES : hi - EARLY_SCALES]
+            return item_cd[:, lo:hi], scales
+
+        def score_direct(lo, hi, tag):
+            acc = psum2.tile([P, hi - lo], F32, name="acc", tag=tag)
+            product(acc[:], users(0), items(lo, hi))
+            nc.vector.tensor_tensor(scores[0][:, lo:hi], acc[:], bias_all[lo // BANK][:, lo % BANK : lo % BANK + hi - lo], ALU.add)
+
+        by_slot = {
+            (t, h): sb.tile([P, BANK], F32, name="by_slot%d_%d" % (t, h), tag="by_slot%d_%d" % (t, h), align_bytes=64)
+            for t in range(1, PACK)
+            for h in range(HALVES)
+        }
 
         def score_by_slot(t, h):
-            users = slice(t * P, (t + 1) * P)
-            acc = psum.tile([P, BANK], F32, name="acc_by_slot", tag="first")
+            acc = psum4.tile([P, BANK], F32, name="acc_by_slot")
             for b in range(BLOCKS):
-                slots = slice(h * BANK + b * P, h * BANK + (b + 1) * P)
-                nc.tensor.matmul_mx(
-                    out=acc[:, b * P : (b + 1) * P],
-                    lhsT=item_cd[:, slots].bitcast(FP8X4),
-                    lhsT_scale=item_sc[:, slots],
-                    rhs=q_codes(t),
-                    rhs_scale=q_sc[:, users],
-                    start=True,
-                    stop=True,
-                )
+                product(acc[:, b * P : (b + 1) * P], items(h * BANK + b * P, h * BANK + (b + 1) * P), users(t))
             for b in range(BLOCKS):
                 c = h * BLOCKS + b
                 nc.scalar.activation(
-                    by_slot[t][:, c * P : (c + 1) * P], acc[:, b * P : (b + 1) * P], ACT.Identity, bias=bias_col[:, c : c + 1]
+                    by_slot[t, h][:, b * P : (b + 1) * P], acc[:, b * P : (b + 1) * P], ACT.Identity, bias=bias_col[:, c : c + 1]
                 )
 
-        def turn_back(t):
-            for h in range(HALVES):
-                turned = psum.tile([P, BANK], F32, name="turned", tag="second")
-                for b in range(BLOCKS):
-                    c = h * BLOCKS + b
-                    nc.tensor.transpose(turned[:, b * P : (b + 1) * P], by_slot[t][:, c * P : (c + 1) * P], ident[:])
-                nc.scalar.copy(scores[t][:, h * BANK : (h + 1) * BANK], turned[:])
+        def turn_back(t, h):
+            turned = psum2.tile([P, BANK], F32, name="turned", tag="back")
+            for b in range(BLOCKS):
+                nc.tensor.transpose(turned[:, b * P : (b + 1) * P], by_slot[t, h][:, b * P : (b + 1) * P], ident[:])
+            nc.scalar.copy(scores[t][:, h * BANK : (h + 1) * BANK], turned[:])
 
-        for t in range(1, PACK):
-            for h in range(HALVES):
-                if t == 1:
-                    score_direct(h)
-                    quantise_users(2 + h)
-                score_by_slot(t, h)
-            turn_back(t)
+        score_direct(0, BANK, "direct")
+        score_by_slot(1, 0)
+        score_by_slot(2, 0)
+        score_direct(BANK, BANK + QUARTER, "direct")
+        score_direct(BANK + QUARTER, I, "back")
+        score_by_slot(1, 1)
+        turn_back(1, 0)
+        score_by_slot(2, 1)
+        turn_back(1, 1)
 
-        y = sb.tile([P, 2, PACK, PAIR_HALF], F32, name="y", tag="by_slot3", align_bytes=64)
+        seconds = {}
+
+        def look_up_second(t, lo, hi, place):
+            seconds[t, lo] = ring.tile([P, hi - lo], F32, name="second%d_%d" % (t, lo), offset=place, align_bytes=64)
+            nc.vector.tensor_copy(seconds[t, lo][:], scores[t][:].indirect(entries(second_list, lo, hi)))
+
+        def subtract(t, lo, hi):
+            nc.vector.tensor_tensor(
+                diff_all[:, t, lo:hi], scores[t][:].indirect(entries(first_list, lo, hi)), seconds[t, lo][:], ALU.subtract
+            )
+
+        diff_all = sb.tile([P, PACK, J], F32, name="diff_all", align_bytes=64)
+        look_up_second(0, 0, J, 0)
+        quantise_users(q_late[:], 3 * P, Q)
+        subtract(0, 0, J)
+
+        score_by_slot(3, 0)
+        turn_back(2, 0)
+        score_by_slot(3, 1)
+        turn_back(2, 1)
+        turn_back(3, 0)
+        turn_back(3, 1)
+
+        y = sb.tile([P, PACK, J], F32, name="y", tag="by_slot3_1", align_bytes=64)
         y_rows = out_0.rearrange("(p t) j -> p t j", t=PACK)
         y_bf = sb.tile([P, J * PACK], BF16, name="y_bf", align_bytes=64)
         y_cd = sb.tile([P, J], U32, name="y_cd", align_bytes=64)
         y_sc = sb.tile([P, J], U8, name="y_sc", align_bytes=64)
         words_out = out_1[0].rearrange("p c t -> p (c t)").bitcast(I32)
-        diff = [sb.tile([P, PACK, PAIR_HALF], F32, name="diff%d" % half, align_bytes=64) for half in range(2)]
 
-        def pairs_of(half):
-            return slice(half * PAIR_HALF, (half + 1) * PAIR_HALF)
+        def prefer(tiles, lo, hi):
+            nc.scalar.activation(y[:, tiles, lo:hi], diff_all[:, tiles, lo:hi], ACT.Sigmoid)
 
-        def entries(pair_list, half):
-            return pair_list[:, half * (PAIR_HALF // 16) : (half + 1) * (PAIR_HALF // 16)]
+        def store(queue, tiles, lo, hi):
+            queue.dma_start(y_rows[:, tiles, lo:hi], y[:, tiles, lo:hi])
 
-        def differences(t):
-            seconds = [sb.tile([P, PAIR_HALF], F32, name="second%d_%d" % (t, half), align_bytes=64) for half in range(2)]
-            for half in range(2):
-                nc.vector.tensor_copy(seconds[half][:], scores[t][:].indirect(entries(second_list, half)))
-            for half in range(2):
-                nc.vector.tensor_tensor(
-                    diff[half][:, t, :], scores[t][:].indirect(entries(first_list, half)), seconds[half][:], ALU.subtract
-                )
-
-        def prefer(half, lo, hi):
-            nc.scalar.activation(y[:, half, lo:hi, :], diff[half][:, lo:hi, :], ACT.Sigmoid)
-            nc.sync.dma_start(y_rows[:, lo:hi, pairs_of(half)], y[:, half, lo:hi, :])
-
-        def woven(half, lo, hi):
-            first = half * PAIR_HALF
-            return y_bf[:, (first + lo) * PACK : (first + hi) * PACK].rearrange("p (c i t) -> p c t i", i=4, t=PACK)
-
-        def round_on_scalar(half, lo, hi):
-            nc.scalar.activation(woven(half, lo, hi), diff[half][:, :, lo:hi].rearrange("p t (c i) -> p c t i", i=4), ACT.Sigmoid)
-
-        def round_on_vector(half, lo, hi):
-            nc.vector.tensor_copy(woven(half, lo, hi), y[:, half, :, lo:hi].rearrange("p t (c i) -> p c t i", i=4))
-
-        def quantise(half):
-            cols = pairs_of(half)
-            nc.vector.quantize_mx(
-                out=y_cd[:, cols].bitcast(FP8X4), scales=y_sc[:, cols], in_=y_bf[:, cols.start * PACK : cols.stop * PACK]
+        def prefer_rounded(lo, hi):
+            nc.scalar.activation(
+                y_bf[:, lo * PACK : hi * PACK].rearrange("p (c i t) -> p c t i", i=4, t=PACK),
+                diff_all[:, :, lo:hi].rearrange("p t (c i) -> p c t i", i=4),
+                ACT.Sigmoid,
             )
-            nc.sync.dma_start(words_out[:, cols], y_cd[:, cols].bitcast(I32))
 
-        for t in range(PACK):
-            differences(t)
-        for half in range(2):
-            prefer(half, 0, PACK - 1)
-        for half in range(2):
-            prefer(half, PACK - 1, PACK)
-            round_on_scalar(half, 0, SCALAR_SHARE[half])
-        for half in range(2):
-            round_on_vector(half, SCALAR_SHARE[half], PAIR_HALF)
-        for half in range(2):
-            quantise(half)
+        def quantise(lo, hi):
+            nc.vector.quantize_mx(out=y_cd[:, lo:hi].bitcast(FP8X4), scales=y_sc[:, lo:hi], in_=y_bf[:, lo * PACK : hi * PACK])
+
+        early, late = slice(0, 2), slice(2, PACK)
+        third, fourth = PAIR_HALF, PAIR_HALF + CHUNK
+        for t, width in ((1, PAIR_HALF), (2, CHUNK)):
+            for k in range(2):
+                look_up_second(t, k * width, (k + 1) * width, 2048 * t + 1024 * k)
+            for k in range(2):
+                subtract(t, k * width, (k + 1) * width)
+        look_up_second(3, 0, third, 6144)
+        look_up_second(3, third, fourth, 7168)
+        subtract(3, 0, third)
+        subtract(3, third, fourth)
+        look_up_second(2, third, fourth, 6144)
+        look_up_second(3, fourth, J, 7168)
+        subtract(2, third, fourth)
+        look_up_second(2, fourth, J, 6144 + 512)
+        subtract(3, fourth, J)
+        subtract(2, fourth, J)
+
+        for tiles, lo, hi in ((early, third, J), (slice(0, 3), 0, third)):
+            prefer(tiles, lo, hi)
+            store(nc.sync, tiles, lo, hi)
+        runs = [(0, third), (third, fourth), (fourth, J)]
+        for lo, hi in runs:
+            prefer_rounded(lo, hi)
+            tiles = slice(3, PACK) if lo == 0 else late
+            prefer(tiles, lo, hi)
+            store(nc.scalar if hi == J else nc.sync, tiles, lo, hi)
+        for lo, hi in runs:
+            quantise(lo, hi)
+        for lo, hi in ((0, fourth), (fourth, J)):
+            nc.sync.dma_start(words_out[:, lo:hi], y_cd[:, lo:hi].bitcast(I32))
         for quad in range(4):
             queue = nc.scalar if quad % 2 else nc.sync
             queue.dma_start(

@@ -27,6 +27,7 @@ CHUNK = J // 4
 LIST_ROWS = 16
 QUARTER = I // 4
 EARLY_SCALES = 3 * QUARTER
+SCALAR_SHARE = (64, 128)
 
 
 def tile_attend_pairprefs_pl_kernel(tc, query, item_words, item_scales, ib, offs, offs2, offs3, out_0, out_1, out_2):
@@ -175,8 +176,8 @@ def tile_attend_pairprefs_pl_kernel(tc, query, item_words, item_scales, ib, offs
         score_direct(BANK + QUARTER, I, "back")
         score_by_slot(1, 1)
         turn_back(1, 0)
-        score_by_slot(2, 1)
         turn_back(1, 1)
+        score_by_slot(2, 1)
 
         seconds = {}
 
@@ -196,8 +197,8 @@ def tile_attend_pairprefs_pl_kernel(tc, query, item_words, item_scales, ib, offs
 
         score_by_slot(3, 0)
         turn_back(2, 0)
-        score_by_slot(3, 1)
         turn_back(2, 1)
+        score_by_slot(3, 1)
         turn_back(3, 0)
         turn_back(3, 1)
 
@@ -224,36 +225,30 @@ def tile_attend_pairprefs_pl_kernel(tc, query, item_words, item_scales, ib, offs
         def quantise(lo, hi):
             nc.vector.quantize_mx(out=y_cd[:, lo:hi].bitcast(FP8X4), scales=y_sc[:, lo:hi], in_=y_bf[:, lo * PACK : hi * PACK])
 
-        early, late = slice(0, 2), slice(2, PACK)
-        third, fourth = PAIR_HALF, PAIR_HALF + CHUNK
-        for t, width in ((1, PAIR_HALF), (2, CHUNK)):
-            for k in range(2):
-                look_up_second(t, k * width, (k + 1) * width, 2048 * t + 1024 * k)
-            for k in range(2):
-                subtract(t, k * width, (k + 1) * width)
-        look_up_second(3, 0, third, 6144)
-        look_up_second(3, third, fourth, 7168)
-        subtract(3, 0, third)
-        subtract(3, third, fourth)
-        look_up_second(2, third, fourth, 6144)
-        look_up_second(3, fourth, J, 7168)
-        subtract(2, third, fourth)
-        look_up_second(2, fourth, J, 6144 + 512)
-        subtract(3, fourth, J)
-        subtract(2, fourth, J)
+        def round_on_vector(lo, hi):
+            nc.vector.tensor_copy(
+                y_bf[:, lo * PACK : hi * PACK].rearrange("p (c i t) -> p c t i", i=4, t=PACK),
+                y[:, :, lo:hi].rearrange("p t (c i) -> p c t i", i=4),
+            )
 
-        for tiles, lo, hi in ((early, third, J), (slice(0, 3), 0, third)):
-            prefer(tiles, lo, hi)
-            store(nc.sync, tiles, lo, hi)
-        runs = [(0, third), (third, fourth), (fourth, J)]
-        for lo, hi in runs:
-            prefer_rounded(lo, hi)
-            tiles = slice(3, PACK) if lo == 0 else late
-            prefer(tiles, lo, hi)
-            store(nc.scalar if hi == J else nc.sync, tiles, lo, hi)
-        for lo, hi in runs:
+        for t in range(1, PACK):
+            for k in range(2):
+                look_up_second(t, k * PAIR_HALF, (k + 1) * PAIR_HALF, 2048 * t + 1024 * k)
+            for k in range(2):
+                subtract(t, k * PAIR_HALF, (k + 1) * PAIR_HALF)
+
+        halves = [(0, PAIR_HALF), (PAIR_HALF, J)]
+        for tiles in (slice(0, 2), slice(2, 3)):
+            prefer(tiles, 0, J)
+            store(nc.sync, tiles, 0, J)
+        for (lo, hi), share in zip(halves, SCALAR_SHARE):
+            prefer(slice(3, PACK), lo, hi)
+            store(nc.sync, slice(3, PACK), lo, hi)
+            prefer_rounded(lo, lo + share)
+        for (lo, hi), share in zip(halves, SCALAR_SHARE):
+            round_on_vector(lo + share, hi)
+        for lo, hi in halves:
             quantise(lo, hi)
-        for lo, hi in ((0, fourth), (fourth, J)):
             nc.sync.dma_start(words_out[:, lo:hi], y_cd[:, lo:hi].bitcast(I32))
         for quad in range(4):
             queue = nc.scalar if quad % 2 else nc.sync

@@ -26,7 +26,6 @@ PAIR_HALF = J // 2
 CHUNK = J // 4
 LIST_ROWS = 16
 QUARTER = I // 4
-EARLY_SCALES = 3 * QUARTER
 SCALAR_SHARE = (64, 128)
 
 
@@ -50,20 +49,17 @@ def tile_attend_pairprefs_pl_kernel(tc, query, item_words, item_scales, ib, offs
 
         bias_pool = sb.tile([P, T], F32, name="bias_pool", align_bytes=64)
         nc.vector.memset(bias_pool[0:BIAS_ROW, :].bitcast(I32), 0)
-        nc.sync.dma_start(bias_pool[BIAS_ROW:P, :], ib[0:1, :])
-        q_rows = query.rearrange("(p r) q -> p r q", r=PACK)
-        q_raw0 = sb.tile([P, PACK, Q // 2], F32, name="q_raw0", align_bytes=64)
-        q_raw1 = reused.tile([P, PACK + 1, Q // 2], F32, name="q_raw1", offset=0, align_bytes=64)
-        q_raw = [q_raw0[:], q_raw1[:, 0:PACK, :]]
-        nc.sync.dma_start(q_raw0[:], q_rows[:, :, 0 : Q // 2])
+        nc.scalar.dma_start(bias_pool[BIAS_ROW:P, :], ib[0:1, :])
         scale_pool = sb.tile([P, T], U8, name="scale_pool", align_bytes=64)
         nc.gpsimd.memset(scale_pool[:].bitcast(I32), 0)
         for quad in range(4):
-            nc.sync.dma_start(
+            queue = nc.scalar if quad % 2 else nc.sync
+            queue.dma_start(
                 scale_pool[32 * quad : 32 * quad + 4, :].bitcast(I32),
                 item_scales[0, 4 * quad : 4 * quad + 4, :].bitcast(I32),
             )
-        nc.sync.dma_start(q_raw[1], q_rows[:, :, Q // 2 : Q])
+        q_raw = reused.tile([P, PACK, Q], F32, name="q_raw", offset=0, align_bytes=64)
+        nc.sync.dma_start(q_raw[:], query.rearrange("(p r) q -> p r q", r=PACK))
         word_pool = sb.tile([P, T], U32, name="word_pool", align_bytes=64)
         nc.sync.dma_start(word_pool[:].bitcast(I32), item_words[0].rearrange("p n t -> p (n t)").bitcast(I32))
         nc.sync.dma_start(first_list[:], offs2)
@@ -79,34 +75,29 @@ def tile_attend_pairprefs_pl_kernel(tc, query, item_words, item_scales, ib, offs
         bias_row = [sb.tile([P, BANK], F32, name="bias_row%d" % h, align_bytes=64) for h in range(HALVES)]
         for h in range(HALVES):
             nc.vector.tensor_copy(bias_row[h][:], bias_pool[:].indirect(entries(slot_list, h * BANK, (h + 1) * BANK)))
-        item_sc0 = sb.tile([P, EARLY_SCALES], U8, name="item_sc0", align_bytes=64)
-        nc.vector.tensor_copy(item_sc0[:], scale_pool[:].indirect(entries(slot_list, 0, EARLY_SCALES)))
+        item_sc = sb.tile([P, I], U8, name="item_sc", align_bytes=64)
+        nc.vector.tensor_copy(item_sc[:], scale_pool[:].indirect(slot_list[:]))
 
-        q_bf = sb.tile([P, Q * PACK], BF16, name="q_bf", align_bytes=64)
-        q_dealt = q_bf[:].rearrange("p (t m r) -> p m r t", t=PACK, r=PACK)
-        for h in range(2):
-            nc.scalar.copy(q_dealt[:, h * (P // 2) : (h + 1) * (P // 2)], q_raw[h].rearrange("p r (m t) -> p m r t", t=PACK))
-        q_cd = sb.tile([P, 3 * P], U32, name="q_cd", align_bytes=64)
+        q_bf = [sb.tile([P, 2 * P * PACK], BF16, name="q_bf%d" % k, align_bytes=64) for k in range(2)]
+        for k in range(2):
+            nc.scalar.copy(
+                q_bf[k][:].rearrange("p (t m r) -> p m r t", t=2, r=PACK),
+                q_raw[:].rearrange("p r (m t) -> p m r t", t=PACK)[:, :, :, 2 * k : 2 * k + 2],
+            )
+        q_cd = sb.tile([P, 2 * P], U32, name="q_cd", align_bytes=64)
         q_sc = sb.tile([P, Q], U8, name="q_sc", align_bytes=64)
 
         def quantise_users(codes, lo, hi):
-            nc.vector.quantize_mx(out=codes.bitcast(FP8X4), scales=q_sc[:, lo:hi], in_=q_bf[:, lo * PACK : hi * PACK])
+            rows = q_bf[lo // 2][:, (lo % 2) * P * PACK : (lo % 2 + hi - lo) * P * PACK]
+            nc.vector.quantize_mx(out=codes.bitcast(FP8X4), scales=q_sc[:, lo * P : hi * P], in_=rows)
 
-        for lo, hi in ((0, 2 * P), (2 * P, 3 * P)):
-            quantise_users(q_cd[:, lo:hi], lo, hi)
+        quantise_users(q_cd[:], 0, 2)
 
         item_cd = reused.tile([P, I], U32, name="item_cd", offset=0, align_bytes=64)
-        item_sc1 = reused.tile([P, I - EARLY_SCALES], U8, name="item_sc1", offset=4096, align_bytes=64)
-
-        def gather_words(lo, hi):
+        for lo, hi in ((0, BANK), (BANK, BANK + QUARTER), (BANK + QUARTER, I)):
             nc.vector.tensor_copy(item_cd[:, lo:hi], word_pool[:].indirect(entries(slot_list, lo, hi)))
 
-        gather_words(0, BANK)
-        nc.vector.tensor_copy(item_sc1[:], scale_pool[:].indirect(entries(slot_list, EARLY_SCALES, I)))
-        gather_words(BANK, BANK + QUARTER)
-        gather_words(BANK + QUARTER, I)
-
-        bias_col = reused.tile([P, HALVES * BLOCKS], F32, name="bias_col", offset=4096 + 256, align_bytes=64)
+        bias_col = reused.tile([P, HALVES * BLOCKS], F32, name="bias_col", offset=4096, align_bytes=64)
         bias_all = [sb.tile([P, BANK], F32, name="bias_all%d" % h, tag="bias_all%d" % h, align_bytes=64) for h in range(HALVES)]
         for h in range(HALVES):
             turned = psum2.tile([P, BANK], F32, name="bias_turned", tag="direct")
@@ -133,14 +124,13 @@ def tile_attend_pairprefs_pl_kernel(tc, query, item_words, item_scales, ib, offs
                 stop=True,
             )
 
-        q_late = sb.tile([P, P], U32, name="q_late", tag="bias_all1", align_bytes=64)
+        q_late = [sb.tile([P, P], U32, name="q_late%d" % h, tag="bias_all%d" % h, align_bytes=64) for h in range(HALVES)]
 
         def users(t):
-            return (q_late[:] if t == PACK - 1 else q_cd[:, t * P : (t + 1) * P]), q_sc[:, t * P : (t + 1) * P]
+            return (q_late[t - 2][:] if t >= 2 else q_cd[:, t * P : (t + 1) * P]), q_sc[:, t * P : (t + 1) * P]
 
         def items(lo, hi):
-            scales = item_sc0[:, lo:hi] if hi <= EARLY_SCALES else item_sc1[:, lo - EARLY_SCALES : hi - EARLY_SCALES]
-            return item_cd[:, lo:hi], scales
+            return item_cd[:, lo:hi], item_sc[:, lo:hi]
 
         def score_direct(lo, hi, tag):
             acc = psum2.tile([P, hi - lo], F32, name="acc", tag=tag)
@@ -171,13 +161,12 @@ def tile_attend_pairprefs_pl_kernel(tc, query, item_words, item_scales, ib, offs
 
         score_direct(0, BANK, "direct")
         score_by_slot(1, 0)
-        score_by_slot(2, 0)
         score_direct(BANK, BANK + QUARTER, "direct")
         score_direct(BANK + QUARTER, I, "back")
+        quantise_users(q_late[0][:], 2, 3)
         score_by_slot(1, 1)
         turn_back(1, 0)
         turn_back(1, 1)
-        score_by_slot(2, 1)
 
         seconds = {}
 
@@ -192,15 +181,14 @@ def tile_attend_pairprefs_pl_kernel(tc, query, item_words, item_scales, ib, offs
 
         diff_all = sb.tile([P, PACK, J], F32, name="diff_all", align_bytes=64)
         look_up_second(0, 0, J, 0)
-        quantise_users(q_late[:], 3 * P, Q)
+        quantise_users(q_late[1][:], 3, PACK)
         subtract(0, 0, J)
 
-        score_by_slot(3, 0)
-        turn_back(2, 0)
-        turn_back(2, 1)
-        score_by_slot(3, 1)
-        turn_back(3, 0)
-        turn_back(3, 1)
+        for t in range(2, PACK):
+            for h in range(HALVES):
+                score_by_slot(t, h)
+            for h in range(HALVES):
+                turn_back(t, h)
 
         y = sb.tile([P, PACK, J], F32, name="y", tag="by_slot3_1", align_bytes=64)
         y_rows = out_0.rearrange("(p t) j -> p t j", t=PACK)

@@ -49,17 +49,20 @@ def tile_attend_pairprefs_pl_kernel(tc, query, item_words, item_scales, ib, offs
 
         bias_pool = sb.tile([P, T], F32, name="bias_pool", align_bytes=64)
         nc.vector.memset(bias_pool[0:BIAS_ROW, :].bitcast(I32), 0)
-        nc.scalar.dma_start(bias_pool[BIAS_ROW:P, :], ib[0:1, :])
+        nc.sync.dma_start(bias_pool[BIAS_ROW:P, :], ib[0:1, :])
+        q_rows = query.rearrange("(p r) q -> p r q", r=PACK)
+        q_raw0 = reused.tile([P, PACK, Q // 2], F32, name="q_raw0", offset=0, align_bytes=64)
+        q_raw1 = reused.tile([P, PACK + 1, Q // 2], F32, name="q_raw1", offset=4096, align_bytes=64)
+        q_raw = [q_raw0[:], q_raw1[:, 0:PACK, :]]
+        nc.sync.dma_start(q_raw[0], q_rows[:, :, 0 : Q // 2])
         scale_pool = sb.tile([P, T], U8, name="scale_pool", align_bytes=64)
         nc.gpsimd.memset(scale_pool[:].bitcast(I32), 0)
         for quad in range(4):
-            queue = nc.scalar if quad % 2 else nc.sync
-            queue.dma_start(
+            nc.sync.dma_start(
                 scale_pool[32 * quad : 32 * quad + 4, :].bitcast(I32),
                 item_scales[0, 4 * quad : 4 * quad + 4, :].bitcast(I32),
             )
-        q_raw = reused.tile([P, PACK, Q], F32, name="q_raw", offset=0, align_bytes=64)
-        nc.sync.dma_start(q_raw[:], query.rearrange("(p r) q -> p r q", r=PACK))
+        nc.sync.dma_start(q_raw[1], q_rows[:, :, Q // 2 : Q])
         word_pool = sb.tile([P, T], U32, name="word_pool", align_bytes=64)
         nc.sync.dma_start(word_pool[:].bitcast(I32), item_words[0].rearrange("p n t -> p (n t)").bitcast(I32))
         nc.sync.dma_start(first_list[:], offs2)
@@ -78,37 +81,47 @@ def tile_attend_pairprefs_pl_kernel(tc, query, item_words, item_scales, ib, offs
         item_sc = sb.tile([P, I], U8, name="item_sc", align_bytes=64)
         nc.vector.tensor_copy(item_sc[:], scale_pool[:].indirect(slot_list[:]))
 
-        q_bf = [sb.tile([P, 2 * P * PACK], BF16, name="q_bf%d" % k, align_bytes=64) for k in range(2)]
-        for k in range(2):
-            nc.scalar.copy(
-                q_bf[k][:].rearrange("p (t m r) -> p m r t", t=2, r=PACK),
-                q_raw[:].rearrange("p r (m t) -> p m r t", t=PACK)[:, :, :, 2 * k : 2 * k + 2],
-            )
+        item_cd = [
+            sb.tile([P, BANK], U32, name="item_cd0", align_bytes=64),
+            reused.tile([P, BANK], U32, name="item_cd1", offset=4096, align_bytes=64),
+        ]
+
+        def gather_words(lo, hi):
+            h = lo // BANK
+            nc.vector.tensor_copy(item_cd[h][:, lo - h * BANK : hi - h * BANK], word_pool[:].indirect(entries(slot_list, lo, hi)))
+
+        q_bf = sb.tile([P, Q * PACK], BF16, name="q_bf", align_bytes=64)
+        q_dealt = q_bf[:].rearrange("p (t m r) -> p m r t", t=PACK, r=PACK)
+        for h in range(2):
+            nc.scalar.copy(q_dealt[:, h * (P // 2) : (h + 1) * (P // 2)], q_raw[h].rearrange("p r (m t) -> p m r t", t=PACK))
         q_cd = sb.tile([P, 2 * P], U32, name="q_cd", align_bytes=64)
         q_sc = sb.tile([P, Q], U8, name="q_sc", align_bytes=64)
 
         def quantise_users(codes, lo, hi):
-            rows = q_bf[lo // 2][:, (lo % 2) * P * PACK : (lo % 2 + hi - lo) * P * PACK]
-            nc.vector.quantize_mx(out=codes.bitcast(FP8X4), scales=q_sc[:, lo * P : hi * P], in_=rows)
+            nc.vector.quantize_mx(
+                out=codes.bitcast(FP8X4), scales=q_sc[:, lo * P : hi * P], in_=q_bf[:, lo * P * PACK : hi * P * PACK]
+            )
 
+        gather_words(0, BANK)
         quantise_users(q_cd[:], 0, 2)
+        gather_words(BANK, BANK + QUARTER)
+        gather_words(BANK + QUARTER, I)
 
-        item_cd = reused.tile([P, I], U32, name="item_cd", offset=0, align_bytes=64)
-        for lo, hi in ((0, BANK), (BANK, BANK + QUARTER), (BANK + QUARTER, I)):
-            nc.vector.tensor_copy(item_cd[:, lo:hi], word_pool[:].indirect(entries(slot_list, lo, hi)))
-
-        bias_col = reused.tile([P, HALVES * BLOCKS], F32, name="bias_col", offset=4096, align_bytes=64)
-        bias_all = [sb.tile([P, BANK], F32, name="bias_all%d" % h, tag="bias_all%d" % h, align_bytes=64) for h in range(HALVES)]
+        bias_col = [
+            reused.tile([P, BLOCKS], F32, name="bias_col%d" % h, offset=8192 * h, align_bytes=64) for h in range(HALVES)
+        ]
+        bias_all = [
+            reused.tile([P, BANK], F32, name="bias_all%d" % h, offset=(6144, 9216)[h], align_bytes=64) for h in range(HALVES)
+        ]
         for h in range(HALVES):
             turned = psum2.tile([P, BANK], F32, name="bias_turned", tag="direct")
             for b in range(BLOCKS):
                 nc.tensor.transpose(turned[:, b * P : (b + 1) * P], bias_row[h][:, b * P : (b + 1) * P], ident[:])
-            nc.scalar.copy(bias_col[:, h * BLOCKS : (h + 1) * BLOCKS], turned[:, BIAS_ROW:BANK:P])
+            nc.scalar.copy(bias_col[h][:], turned[:, BIAS_ROW:BANK:P])
         for h in range(HALVES):
             spread = psum2.tile([P, BANK], F32, name="bias_spread", tag="back")
             for b in range(BLOCKS):
-                c = h * BLOCKS + b
-                nc.tensor.transpose(spread[:, b * P : (b + 1) * P], bias_col[:, c : c + 1].to_broadcast([P, P]), ident[:])
+                nc.tensor.transpose(spread[:, b * P : (b + 1) * P], bias_col[h][:, b : b + 1].to_broadcast([P, P]), ident[:])
             nc.scalar.copy(bias_all[h][:], spread[:])
 
         scores = [sb.tile([P, I], F32, name="scores%d" % t, align_bytes=64) for t in range(PACK)]
@@ -124,13 +137,14 @@ def tile_attend_pairprefs_pl_kernel(tc, query, item_words, item_scales, ib, offs
                 stop=True,
             )
 
-        q_late = [sb.tile([P, P], U32, name="q_late%d" % h, tag="bias_all%d" % h, align_bytes=64) for h in range(HALVES)]
+        q_late = [reused.tile([P, P], U32, name="q_late%d" % h, offset=(6144, 9216)[h], align_bytes=64) for h in range(HALVES)]
 
         def users(t):
             return (q_late[t - 2][:] if t >= 2 else q_cd[:, t * P : (t + 1) * P]), q_sc[:, t * P : (t + 1) * P]
 
         def items(lo, hi):
-            return item_cd[:, lo:hi], item_sc[:, lo:hi]
+            h = lo // BANK
+            return item_cd[h][:, lo - h * BANK : hi - h * BANK], item_sc[:, lo:hi]
 
         def score_direct(lo, hi, tag):
             acc = psum2.tile([P, hi - lo], F32, name="acc", tag=tag)
@@ -148,9 +162,8 @@ def tile_attend_pairprefs_pl_kernel(tc, query, item_words, item_scales, ib, offs
             for b in range(BLOCKS):
                 product(acc[:, b * P : (b + 1) * P], items(h * BANK + b * P, h * BANK + (b + 1) * P), users(t))
             for b in range(BLOCKS):
-                c = h * BLOCKS + b
                 nc.scalar.activation(
-                    by_slot[t, h][:, b * P : (b + 1) * P], acc[:, b * P : (b + 1) * P], ACT.Identity, bias=bias_col[:, c : c + 1]
+                    by_slot[t, h][:, b * P : (b + 1) * P], acc[:, b * P : (b + 1) * P], ACT.Identity, bias=bias_col[h][:, b : b + 1]
                 )
 
         def turn_back(t, h):

@@ -82,8 +82,7 @@ def tile_attend_pairprefs_pl_kernel(tc, query, item_words, item_scales, ib, offs
         nc.vector.tensor_copy(item_sc[:], scale_pool[:].indirect(slot_list[:]))
 
         item_cd = [
-            sb.tile([P, BANK], U32, name="item_cd0", align_bytes=64),
-            reused.tile([P, BANK], U32, name="item_cd1", offset=4096, align_bytes=64),
+            reused.tile([P, BANK], U32, name="item_cd%d" % h, offset=(8256, 4096)[h], align_bytes=64) for h in range(HALVES)
         ]
 
         def gather_words(lo, hi):
@@ -102,8 +101,8 @@ def tile_attend_pairprefs_pl_kernel(tc, query, item_words, item_scales, ib, offs
                 out=codes.bitcast(FP8X4), scales=q_sc[:, lo * P : hi * P], in_=q_bf[:, lo * P * PACK : hi * P * PACK]
             )
 
-        gather_words(0, BANK)
         quantise_users(q_cd[:], 0, 2)
+        gather_words(0, BANK)
         gather_words(BANK, BANK + QUARTER)
         gather_words(BANK + QUARTER, I)
 
@@ -111,7 +110,7 @@ def tile_attend_pairprefs_pl_kernel(tc, query, item_words, item_scales, ib, offs
             reused.tile([P, BLOCKS], F32, name="bias_col%d" % h, offset=8192 * h, align_bytes=64) for h in range(HALVES)
         ]
         bias_all = [
-            reused.tile([P, BANK], F32, name="bias_all%d" % h, offset=(6144, 9216)[h], align_bytes=64) for h in range(HALVES)
+            reused.tile([P, BANK], F32, name="bias_all%d" % h, offset=(6144, 10304)[h], align_bytes=64) for h in range(HALVES)
         ]
         for h in range(HALVES):
             turned = psum2.tile([P, BANK], F32, name="bias_turned", tag="direct")
@@ -137,7 +136,7 @@ def tile_attend_pairprefs_pl_kernel(tc, query, item_words, item_scales, ib, offs
                 stop=True,
             )
 
-        q_late = [reused.tile([P, P], U32, name="q_late%d" % h, offset=(6144, 9216)[h], align_bytes=64) for h in range(HALVES)]
+        q_late = [reused.tile([P, P], U32, name="q_late%d" % h, offset=(6144, 10304)[h], align_bytes=64) for h in range(HALVES)]
 
         def users(t):
             return (q_late[t - 2][:] if t >= 2 else q_cd[:, t * P : (t + 1) * P]), q_sc[:, t * P : (t + 1) * P]

@@ -156,14 +156,20 @@ def tile_attend_pairprefs_pl_kernel(tc, query, item_words, item_scales, ib, offs
             for h in range(HALVES)
         }
 
-        def score_by_slot(t, h):
-            acc = psum4.tile([P, BANK], F32, name="acc_by_slot")
-            for b in range(BLOCKS):
+        def products_by_slot(acc, t, h, blocks):
+            for b in blocks:
                 product(acc[:, b * P : (b + 1) * P], items(h * BANK + b * P, h * BANK + (b + 1) * P), users(t))
+
+        def bias_by_slot(acc, t, h):
             for b in range(BLOCKS):
                 nc.scalar.activation(
                     by_slot[t, h][:, b * P : (b + 1) * P], acc[:, b * P : (b + 1) * P], ACT.Identity, bias=bias_col[h][:, b : b + 1]
                 )
+
+        def score_by_slot(t, h):
+            acc = psum4.tile([P, BANK], F32, name="acc_by_slot")
+            products_by_slot(acc, t, h, range(BLOCKS))
+            bias_by_slot(acc, t, h)
 
         def turn_back(t, h):
             turned = psum2.tile([P, BANK], F32, name="turned", tag="back")
@@ -172,9 +178,12 @@ def tile_attend_pairprefs_pl_kernel(tc, query, item_words, item_scales, ib, offs
             nc.scalar.copy(scores[t][:, h * BANK : (h + 1) * BANK], turned[:])
 
         score_direct(0, BANK, "direct")
-        score_by_slot(1, 0)
+        first_by_slot = psum4.tile([P, BANK], F32, name="acc_by_slot")
+        products_by_slot(first_by_slot, 1, 0, range(0, BLOCKS // 2))
         score_direct(BANK, BANK + QUARTER, "direct")
         score_direct(BANK + QUARTER, I, "back")
+        products_by_slot(first_by_slot, 1, 0, range(BLOCKS // 2, BLOCKS))
+        bias_by_slot(first_by_slot, 1, 0)
         quantise_users(q_late[0][:], 2, 3)
         score_by_slot(1, 1)
         turn_back(1, 0)

@@ -25,6 +25,7 @@ HALVES = I // BANK
 PAIR_HALF = J // 2
 CHUNK = J // 4
 LIST_ROWS = 16
+WARM_PASSES = 4
 QUARTER = I // 4
 SCALAR_SHARE = (64, 128)
 
@@ -176,6 +177,10 @@ def tile_attend_pairprefs_pl_kernel(tc, query, item_words, item_scales, ib, offs
             for b in range(BLOCKS):
                 nc.tensor.transpose(turned[:, b * P : (b + 1) * P], by_slot[t, h][:, b * P : (b + 1) * P], ident[:])
             nc.scalar.copy(scores[t][:, h * BANK : (h + 1) * BANK], turned[:])
+
+        warm_bank = psum4.tile([P, BANK], F32, name="acc_by_slot")
+        for k in range(WARM_PASSES):
+            product(warm_bank[:, (k % 2) * 2 * P : (k % 2 + 1) * 2 * P], users(0), (q_cd[:], q_sc[:, 0 : 2 * P]))
 
         score_direct(0, BANK, "direct")
         first_by_slot = psum4.tile([P, BANK], F32, name="acc_by_slot")

@@ -23,11 +23,9 @@ BIAS_ROW = P - 1
 BLOCKS = BANK // P
 HALVES = I // BANK
 PAIR_HALF = J // 2
-CHUNK = J // 4
 LIST_ROWS = 16
-WARM_PASSES = 4
 QUARTER = I // 4
-SCALAR_SHARE = (64, 128)
+VECTOR_ZEROES = 1280
 
 
 def tile_attend_pairprefs_pl_kernel(tc, query, item_words, item_scales, ib, offs, offs2, offs3, out_0, out_1, out_2):
@@ -36,7 +34,6 @@ def tile_attend_pairprefs_pl_kernel(tc, query, item_words, item_scales, ib, offs
         lists = ctx.enter_context(tc.tile_pool(name="lists", bufs=1))
         sb = ctx.enter_context(tc.tile_pool(name="sb", bufs=1))
         reused = ctx.enter_context(tc.tile_pool(name="reused", bufs=1))
-        ring = ctx.enter_context(tc.tile_pool(name="ring", bufs=1))
         psum2 = ctx.enter_context(tc.psum_pool(name="psum2", bufs=2))
         psum4 = ctx.enter_context(tc.psum_pool(name="psum4", bufs=4))
 
@@ -49,13 +46,11 @@ def tile_attend_pairprefs_pl_kernel(tc, query, item_words, item_scales, ib, offs
         nc.sync.dma_start(slot_list[:], offs)
 
         bias_pool = sb.tile([P, T], F32, name="bias_pool", align_bytes=64)
-        nc.vector.memset(bias_pool[0:BIAS_ROW, :].bitcast(I32), 0)
+        nc.vector.memset(bias_pool[0:BIAS_ROW, 0:VECTOR_ZEROES].bitcast(I32), 0)
         nc.sync.dma_start(bias_pool[BIAS_ROW:P, :], ib[0:1, :])
         q_rows = query.rearrange("(p r) q -> p r q", r=PACK)
-        q_raw0 = reused.tile([P, PACK, Q // 2], F32, name="q_raw0", offset=0, align_bytes=64)
-        q_raw1 = reused.tile([P, PACK + 1, Q // 2], F32, name="q_raw1", offset=4096, align_bytes=64)
-        q_raw = [q_raw0[:], q_raw1[:, 0:PACK, :]]
-        nc.sync.dma_start(q_raw[0], q_rows[:, :, 0 : Q // 2])
+        q_raw = [reused.tile([P, PACK, Q // 2], F32, name="q_raw%d" % h, offset=4096 * h, align_bytes=64) for h in range(2)]
+        nc.sync.dma_start(q_raw[0][:], q_rows[:, :, 0 : Q // 2])
         scale_pool = sb.tile([P, T], U8, name="scale_pool", align_bytes=64)
         nc.gpsimd.memset(scale_pool[:].bitcast(I32), 0)
         for quad in range(4):
@@ -63,207 +58,146 @@ def tile_attend_pairprefs_pl_kernel(tc, query, item_words, item_scales, ib, offs
                 scale_pool[32 * quad : 32 * quad + 4, :].bitcast(I32),
                 item_scales[0, 4 * quad : 4 * quad + 4, :].bitcast(I32),
             )
-        nc.sync.dma_start(q_raw[1], q_rows[:, :, Q // 2 : Q])
+        nc.sync.dma_start(q_raw[1][:], q_rows[:, :, Q // 2 : Q])
         word_pool = sb.tile([P, T], U32, name="word_pool", align_bytes=64)
         nc.sync.dma_start(word_pool[:].bitcast(I32), item_words[0].rearrange("p n t -> p (n t)").bitcast(I32))
-        nc.sync.dma_start(first_list[:], offs2)
         nc.sync.dma_start(second_list[:], offs3)
+        nc.sync.dma_start(first_list[:], offs2)
 
         warm_in = sb.tile([P, 1], F32, name="warm_in", align_bytes=64)
         warm_out = sb.tile([P, 1], F32, name="warm_out", align_bytes=64)
         nc.gpsimd.memset(warm_in[:], 0.0)
+        nc.gpsimd.memset(bias_pool[0:BIAS_ROW, VECTOR_ZEROES:T].bitcast(I32), 0)
         nc.scalar.activation(warm_out[:], warm_in[:], ACT.Sigmoid)
         ident = sb.tile([P, P], F32, name="ident", align_bytes=64)
         make_identity(nc, ident[:])
 
-        bias_row = [sb.tile([P, BANK], F32, name="bias_row%d" % h, align_bytes=64) for h in range(HALVES)]
-        for h in range(HALVES):
-            nc.vector.tensor_copy(bias_row[h][:], bias_pool[:].indirect(entries(slot_list, h * BANK, (h + 1) * BANK)))
-        item_sc = sb.tile([P, I], U8, name="item_sc", align_bytes=64)
-        nc.vector.tensor_copy(item_sc[:], scale_pool[:].indirect(slot_list[:]))
-
-        item_cd = [
-            reused.tile([P, BANK], U32, name="item_cd%d" % h, offset=(8256, 4096)[h], align_bytes=64) for h in range(HALVES)
-        ]
-
-        def gather_words(lo, hi):
-            h = lo // BANK
-            nc.vector.tensor_copy(item_cd[h][:, lo - h * BANK : hi - h * BANK], word_pool[:].indirect(entries(slot_list, lo, hi)))
-
         q_bf = sb.tile([P, Q * PACK], BF16, name="q_bf", align_bytes=64)
         q_dealt = q_bf[:].rearrange("p (t m r) -> p m r t", t=PACK, r=PACK)
-        for h in range(2):
-            nc.scalar.copy(q_dealt[:, h * (P // 2) : (h + 1) * (P // 2)], q_raw[h].rearrange("p r (m t) -> p m r t", t=PACK))
-        q_cd = sb.tile([P, 2 * P], U32, name="q_cd", align_bytes=64)
-        q_sc = sb.tile([P, Q], U8, name="q_sc", align_bytes=64)
 
-        def quantise_users(codes, lo, hi):
-            nc.vector.quantize_mx(
-                out=codes.bitcast(FP8X4), scales=q_sc[:, lo * P : hi * P], in_=q_bf[:, lo * P * PACK : hi * P * PACK]
-            )
+        def dealt(h):
+            return q_dealt[:, h * (P // 2) : (h + 1) * (P // 2)], q_raw[h][:].rearrange("p r (m t) -> p m r t", t=PACK)
 
-        quantise_users(q_cd[:], 0, 2)
-        gather_words(0, BANK)
-        gather_words(BANK, BANK + QUARTER)
-        gather_words(BANK + QUARTER, I)
-
+        bias_row = [sb.tile([P, BANK], F32, name="bias_row%d" % h, align_bytes=64) for h in range(HALVES)]
         bias_col = [
-            reused.tile([P, BLOCKS], F32, name="bias_col%d" % h, offset=8192 * h, align_bytes=64) for h in range(HALVES)
+            sb.tile([P, BLOCKS], F32, name="bias_col0", align_bytes=64),
+            reused.tile([P, BLOCKS], F32, name="bias_col1", offset=6208, align_bytes=64),
         ]
         bias_all = [
-            reused.tile([P, BANK], F32, name="bias_all%d" % h, offset=(6144, 10304)[h], align_bytes=64) for h in range(HALVES)
+            reused.tile([P, BANK], F32, name="bias_all0", offset=4160, align_bytes=64),
+            sb.tile([P, BANK], F32, name="bias_all1", align_bytes=64),
         ]
-        for h in range(HALVES):
-            turned = psum2.tile([P, BANK], F32, name="bias_turned", tag="direct")
+
+        def gather_bias(h):
+            nc.scalar.activation(bias_row[h][:], bias_pool[:].indirect(entries(slot_list, h * BANK, (h + 1) * BANK)), ACT.Copy)
+
+        def bias_to_columns(h):
+            turned = psum2.tile([P, BANK], F32, name="bias_turned")
             for b in range(BLOCKS):
                 nc.tensor.transpose(turned[:, b * P : (b + 1) * P], bias_row[h][:, b * P : (b + 1) * P], ident[:])
             nc.scalar.copy(bias_col[h][:], turned[:, BIAS_ROW:BANK:P])
-        for h in range(HALVES):
-            spread = psum2.tile([P, BANK], F32, name="bias_spread", tag="back")
+
+        def bias_to_all_rows(h):
+            spread = psum2.tile([P, BANK], F32, name="bias_spread")
             for b in range(BLOCKS):
                 nc.tensor.transpose(spread[:, b * P : (b + 1) * P], bias_col[h][:, b : b + 1].to_broadcast([P, P]), ident[:])
             nc.scalar.copy(bias_all[h][:], spread[:])
 
+        nc.vector.tensor_copy(*dealt(0))
+        item_sc = sb.tile([P, I], U8, name="item_sc", align_bytes=64)
+        nc.vector.tensor_copy(item_sc[:], scale_pool[:].indirect(slot_list[:]))
+
+        gather_bias(0)
+        gather_bias(1)
+        bias_to_columns(0)
+        nc.scalar.copy(*dealt(1))
+        bias_to_columns(1)
+        bias_to_all_rows(0)
+        bias_to_all_rows(1)
+
+        q_cd = sb.tile([P, Q], U32, name="q_cd", align_bytes=64)
+        q_sc = sb.tile([P, Q], U8, name="q_sc", align_bytes=64)
+        nc.vector.quantize_mx(out=q_cd[:].bitcast(FP8X4), scales=q_sc[:], in_=q_bf[:])
+
+        item_cd = reused.tile([P, I], U32, name="item_cd", offset=64, align_bytes=64)
+        pieces = [(0, BANK), (BANK, BANK + QUARTER), (BANK + QUARTER, I)]
+        for lo, hi in pieces:
+            nc.vector.tensor_copy(item_cd[:, lo:hi], word_pool[:].indirect(entries(slot_list, lo, hi)))
+
         scores = [sb.tile([P, I], F32, name="scores%d" % t, align_bytes=64) for t in range(PACK)]
-
-        def product(out, stationary, moving):
-            nc.tensor.matmul_mx(
-                out=out,
-                lhsT=stationary[0].bitcast(FP8X4),
-                lhsT_scale=stationary[1],
-                rhs=moving[0].bitcast(FP8X4),
-                rhs_scale=moving[1],
-                start=True,
-                stop=True,
-            )
-
-        q_late = [reused.tile([P, P], U32, name="q_late%d" % h, offset=(6144, 10304)[h], align_bytes=64) for h in range(HALVES)]
-
-        def users(t):
-            return (q_late[t - 2][:] if t >= 2 else q_cd[:, t * P : (t + 1) * P]), q_sc[:, t * P : (t + 1) * P]
-
-        def items(lo, hi):
-            h = lo // BANK
-            return item_cd[h][:, lo - h * BANK : hi - h * BANK], item_sc[:, lo:hi]
-
-        def score_direct(lo, hi, tag):
-            acc = psum2.tile([P, hi - lo], F32, name="acc", tag=tag)
-            product(acc[:], users(0), items(lo, hi))
-            nc.vector.tensor_tensor(scores[0][:, lo:hi], acc[:], bias_all[lo // BANK][:, lo % BANK : lo % BANK + hi - lo], ALU.add)
-
-        by_slot = {
-            (t, h): sb.tile([P, BANK], F32, name="by_slot%d_%d" % (t, h), tag="by_slot%d_%d" % (t, h), align_bytes=64)
-            for t in range(1, PACK)
-            for h in range(HALVES)
-        }
-
-        def products_by_slot(acc, t, h, blocks):
-            for b in blocks:
-                product(acc[:, b * P : (b + 1) * P], items(h * BANK + b * P, h * BANK + (b + 1) * P), users(t))
-
-        def bias_by_slot(acc, t, h):
-            for b in range(BLOCKS):
-                nc.scalar.activation(
-                    by_slot[t, h][:, b * P : (b + 1) * P], acc[:, b * P : (b + 1) * P], ACT.Identity, bias=bias_col[h][:, b : b + 1]
-                )
-
-        def score_by_slot(t, h):
-            acc = psum4.tile([P, BANK], F32, name="acc_by_slot")
-            products_by_slot(acc, t, h, range(BLOCKS))
-            bias_by_slot(acc, t, h)
-
-        def turn_back(t, h):
-            turned = psum2.tile([P, BANK], F32, name="turned", tag="back")
-            for b in range(BLOCKS):
-                nc.tensor.transpose(turned[:, b * P : (b + 1) * P], by_slot[t, h][:, b * P : (b + 1) * P], ident[:])
-            nc.scalar.copy(scores[t][:, h * BANK : (h + 1) * BANK], turned[:])
-
-        warm_bank = psum4.tile([P, BANK], F32, name="acc_by_slot")
-        for k in range(WARM_PASSES):
-            product(warm_bank[:, (k % 2) * 2 * P : (k % 2 + 1) * 2 * P], users(0), (q_cd[:], q_sc[:, 0 : 2 * P]))
-
-        score_direct(0, BANK, "direct")
-        first_by_slot = psum4.tile([P, BANK], F32, name="acc_by_slot")
-        products_by_slot(first_by_slot, 1, 0, range(0, BLOCKS // 2))
-        score_direct(BANK, BANK + QUARTER, "direct")
-        score_direct(BANK + QUARTER, I, "back")
-        products_by_slot(first_by_slot, 1, 0, range(BLOCKS // 2, BLOCKS))
-        bias_by_slot(first_by_slot, 1, 0)
-        quantise_users(q_late[0][:], 2, 3)
-        score_by_slot(1, 1)
-        turn_back(1, 0)
-        turn_back(1, 1)
-
-        seconds = {}
-
-        def look_up_second(t, lo, hi, place):
-            seconds[t, lo] = ring.tile([P, hi - lo], F32, name="second%d_%d" % (t, lo), offset=place, align_bytes=64)
-            nc.vector.tensor_copy(seconds[t, lo][:], scores[t][:].indirect(entries(second_list, lo, hi)))
-
-        def subtract(t, lo, hi):
-            nc.vector.tensor_tensor(
-                diff_all[:, t, lo:hi], scores[t][:].indirect(entries(first_list, lo, hi)), seconds[t, lo][:], ALU.subtract
-            )
-
-        diff_all = sb.tile([P, PACK, J], F32, name="diff_all", align_bytes=64)
-        look_up_second(0, 0, J, 0)
-        quantise_users(q_late[1][:], 3, PACK)
-        subtract(0, 0, J)
-
-        for t in range(2, PACK):
-            for h in range(HALVES):
-                score_by_slot(t, h)
-            for h in range(HALVES):
-                turn_back(t, h)
-
-        y = sb.tile([P, PACK, J], F32, name="y", tag="by_slot3_1", align_bytes=64)
+        seconds = [sb.tile([P, J], F32, name="seconds%d" % t, align_bytes=64) for t in range(PACK)]
+        diff = sb.tile([P, PACK, J], F32, name="diff", align_bytes=64)
+        y = sb.tile([P, PACK, J], F32, name="y", align_bytes=64)
         y_rows = out_0.rearrange("(p t) j -> p t j", t=PACK)
         y_bf = sb.tile([P, J * PACK], BF16, name="y_bf", align_bytes=64)
         y_cd = sb.tile([P, J], U32, name="y_cd", align_bytes=64)
         y_sc = sb.tile([P, J], U8, name="y_sc", align_bytes=64)
         words_out = out_1[0].rearrange("p c t -> p (c t)").bitcast(I32)
 
-        def prefer(tiles, lo, hi):
-            nc.scalar.activation(y[:, tiles, lo:hi], diff_all[:, tiles, lo:hi], ACT.Sigmoid)
-
-        def store(queue, tiles, lo, hi):
-            queue.dma_start(y_rows[:, tiles, lo:hi], y[:, tiles, lo:hi])
-
-        def prefer_rounded(lo, hi):
-            nc.scalar.activation(
-                y_bf[:, lo * PACK : hi * PACK].rearrange("p (c i t) -> p c t i", i=4, t=PACK),
-                diff_all[:, :, lo:hi].rearrange("p t (c i) -> p c t i", i=4),
-                ACT.Sigmoid,
+        def product(out, t, lo, hi):
+            nc.tensor.matmul_mx(
+                out=out,
+                lhsT=q_cd[:, t * P : (t + 1) * P].bitcast(FP8X4),
+                lhsT_scale=q_sc[:, t * P : (t + 1) * P],
+                rhs=item_cd[:, lo:hi].bitcast(FP8X4),
+                rhs_scale=item_sc[:, lo:hi],
+                start=True,
+                stop=True,
             )
+
+        def score(t):
+            for h in range(HALVES):
+                acc = psum4.tile([P, BANK], F32, name="acc")
+                cuts = [c for c in pieces if c[0] // BANK == h] if t == 0 else [(h * BANK, (h + 1) * BANK)]
+                for lo, hi in cuts:
+                    product(acc[:, lo - h * BANK : hi - h * BANK], t, lo, hi)
+                nc.vector.tensor_tensor(scores[t][:, h * BANK : (h + 1) * BANK], acc[:], bias_all[h][:], ALU.add)
+            nc.scalar.activation(seconds[t][:], scores[t][:].indirect(second_list[:]), ACT.Copy)
+
+        def subtract(t, lo, hi):
+            nc.vector.tensor_tensor(
+                diff[:, t, lo:hi], scores[t][:].indirect(entries(first_list, lo, hi)), seconds[t][:, lo:hi], ALU.subtract
+            )
+
+        def prefer(tiles, lo, hi):
+            nc.scalar.activation(y[:, tiles, lo:hi], diff[:, tiles, lo:hi], ACT.Sigmoid)
+
+        def store(tiles, lo, hi):
+            nc.sync.dma_start(y_rows[:, tiles, lo:hi], y[:, tiles, lo:hi])
+
+        def woven(tiles, lo, hi):
+            return y_bf[:, lo * PACK : hi * PACK].rearrange("p (c i t) -> p c t i", i=4, t=PACK)[:, :, tiles, :]
+
+        def by_fours(source, tiles, lo, hi):
+            return source[:, tiles, lo:hi].rearrange("p t (c i) -> p c t i", i=4)
+
+        def prefer_rounded(tiles, lo, hi):
+            nc.scalar.activation(woven(tiles, lo, hi), by_fours(diff, tiles, lo, hi), ACT.Sigmoid)
 
         def quantise(lo, hi):
             nc.vector.quantize_mx(out=y_cd[:, lo:hi].bitcast(FP8X4), scales=y_sc[:, lo:hi], in_=y_bf[:, lo * PACK : hi * PACK])
-
-        def round_on_vector(lo, hi):
-            nc.vector.tensor_copy(
-                y_bf[:, lo * PACK : hi * PACK].rearrange("p (c i t) -> p c t i", i=4, t=PACK),
-                y[:, :, lo:hi].rearrange("p t (c i) -> p c t i", i=4),
-            )
-
-        for t in range(1, PACK):
-            for k in range(2):
-                look_up_second(t, k * PAIR_HALF, (k + 1) * PAIR_HALF, 2048 * t + 1024 * k)
-            for k in range(2):
-                subtract(t, k * PAIR_HALF, (k + 1) * PAIR_HALF)
-
-        halves = [(0, PAIR_HALF), (PAIR_HALF, J)]
-        for tiles in (slice(0, 2), slice(2, 3)):
-            prefer(tiles, 0, J)
-            store(nc.sync, tiles, 0, J)
-        for (lo, hi), share in zip(halves, SCALAR_SHARE):
-            prefer(slice(3, PACK), lo, hi)
-            store(nc.sync, slice(3, PACK), lo, hi)
-            prefer_rounded(lo, lo + share)
-        for (lo, hi), share in zip(halves, SCALAR_SHARE):
-            round_on_vector(lo + share, hi)
-        for lo, hi in halves:
-            quantise(lo, hi)
             nc.sync.dma_start(words_out[:, lo:hi], y_cd[:, lo:hi].bitcast(I32))
+
+        early, late = slice(0, 2), slice(2, PACK)
+        front, back = (0, PAIR_HALF), (PAIR_HALF, J)
+        for t in range(PACK):
+            score(t)
+        for tiles in (early, late):
+            for lo, hi in (front, back):
+                for t in range(tiles.start, tiles.stop):
+                    subtract(t, lo, hi)
+        for lo, hi in (front, back):
+            prefer(early, lo, hi)
+            prefer_rounded(early, lo, hi)
+        store(early, 0, J)
+        prefer(late, *front)
+        store(late, *front)
+        prefer_rounded(late, *back)
+        prefer(late, *back)
+        nc.vector.tensor_copy(woven(late, *front), by_fours(y, late, *front))
+        quantise(*front)
+        store(late, *back)
+        quantise(*back)
         for quad in range(4):
             queue = nc.scalar if quad % 2 else nc.sync
             queue.dma_start(

@@ -34,8 +34,7 @@ def tile_attend_pairprefs_pl_kernel(tc, query, item_words, item_scales, ib, offs
         lists = ctx.enter_context(tc.tile_pool(name="lists", bufs=1))
         sb = ctx.enter_context(tc.tile_pool(name="sb", bufs=1))
         reused = ctx.enter_context(tc.tile_pool(name="reused", bufs=1))
-        psum2 = ctx.enter_context(tc.psum_pool(name="psum2", bufs=2))
-        psum4 = ctx.enter_context(tc.psum_pool(name="psum4", bufs=4))
+        psum = ctx.enter_context(tc.psum_pool(name="psum", bufs=1))
 
         def entries(tile, lo, hi):
             return tile[:, lo // LIST_ROWS : hi // LIST_ROWS]
@@ -80,7 +79,7 @@ def tile_attend_pairprefs_pl_kernel(tc, query, item_words, item_scales, ib, offs
 
         bias_row = [sb.tile([P, BANK], F32, name="bias_row%d" % h, align_bytes=64) for h in range(HALVES)]
         bias_col = [
-            sb.tile([P, BLOCKS], F32, name="bias_col0", align_bytes=64),
+            reused.tile([P, BLOCKS], F32, name="bias_col0", offset=6272, align_bytes=64),
             reused.tile([P, BLOCKS], F32, name="bias_col1", offset=6208, align_bytes=64),
         ]
         bias_all = [
@@ -88,29 +87,26 @@ def tile_attend_pairprefs_pl_kernel(tc, query, item_words, item_scales, ib, offs
             sb.tile([P, BANK], F32, name="bias_all1", align_bytes=64),
         ]
 
-        def gather_bias(h):
-            nc.scalar.activation(bias_row[h][:], bias_pool[:].indirect(entries(slot_list, h * BANK, (h + 1) * BANK)), ACT.Copy)
-
         def bias_to_columns(h):
-            turned = psum2.tile([P, BANK], F32, name="bias_turned")
+            turned = psum.tile([P, BANK], F32, name="bias_turned", tag="bank%d" % h)
             for b in range(BLOCKS):
                 nc.tensor.transpose(turned[:, b * P : (b + 1) * P], bias_row[h][:, b * P : (b + 1) * P], ident[:])
             nc.scalar.copy(bias_col[h][:], turned[:, BIAS_ROW:BANK:P])
 
         def bias_to_all_rows(h):
-            spread = psum2.tile([P, BANK], F32, name="bias_spread")
+            spread = psum.tile([P, BANK], F32, name="bias_spread", tag="bank%d" % (2 + h))
             for b in range(BLOCKS):
                 nc.tensor.transpose(spread[:, b * P : (b + 1) * P], bias_col[h][:, b : b + 1].to_broadcast([P, P]), ident[:])
             nc.scalar.copy(bias_all[h][:], spread[:])
 
-        nc.vector.tensor_copy(*dealt(0))
+        nc.vector.tensor_copy(bias_row[0][:], bias_pool[:].indirect(entries(slot_list, 0, BANK)))
+        nc.scalar.activation(bias_row[1][:], bias_pool[:].indirect(entries(slot_list, BANK, I)), ACT.Copy)
         item_sc = sb.tile([P, I], U8, name="item_sc", align_bytes=64)
         nc.vector.tensor_copy(item_sc[:], scale_pool[:].indirect(slot_list[:]))
 
-        gather_bias(0)
-        gather_bias(1)
+        for h in range(2):
+            nc.scalar.copy(*dealt(h))
         bias_to_columns(0)
-        nc.scalar.copy(*dealt(1))
         bias_to_columns(1)
         bias_to_all_rows(0)
         bias_to_all_rows(1)
@@ -120,9 +116,8 @@ def tile_attend_pairprefs_pl_kernel(tc, query, item_words, item_scales, ib, offs
         nc.vector.quantize_mx(out=q_cd[:].bitcast(FP8X4), scales=q_sc[:], in_=q_bf[:])
 
         item_cd = reused.tile([P, I], U32, name="item_cd", offset=64, align_bytes=64)
-        pieces = [(0, BANK), (BANK, BANK + QUARTER), (BANK + QUARTER, I)]
-        for lo, hi in pieces:
-            nc.vector.tensor_copy(item_cd[:, lo:hi], word_pool[:].indirect(entries(slot_list, lo, hi)))
+        for lo in range(0, I, QUARTER):
+            nc.vector.tensor_copy(item_cd[:, lo : lo + QUARTER], word_pool[:].indirect(entries(slot_list, lo, lo + QUARTER)))
 
         scores = [sb.tile([P, I], F32, name="scores%d" % t, align_bytes=64) for t in range(PACK)]
         seconds = [sb.tile([P, J], F32, name="seconds%d" % t, align_bytes=64) for t in range(PACK)]
@@ -134,9 +129,16 @@ def tile_attend_pairprefs_pl_kernel(tc, query, item_words, item_scales, ib, offs
         y_sc = sb.tile([P, J], U8, name="y_sc", align_bytes=64)
         words_out = out_1[0].rearrange("p c t -> p (c t)").bitcast(I32)
 
-        def product(out, t, lo, hi):
+        acc = {
+            (t, h): psum.tile([P, BANK], F32, name="acc%d_%d" % (t, h), tag="bank%d" % (t if h else PACK + t))
+            for t in range(PACK)
+            for h in range(HALVES)
+        }
+
+        def product(t, lo, hi):
+            h = lo // BANK
             nc.tensor.matmul_mx(
-                out=out,
+                out=acc[t, h][:, lo - h * BANK : hi - h * BANK],
                 lhsT=q_cd[:, t * P : (t + 1) * P].bitcast(FP8X4),
                 lhsT_scale=q_sc[:, t * P : (t + 1) * P],
                 rhs=item_cd[:, lo:hi].bitcast(FP8X4),
@@ -145,14 +147,34 @@ def tile_attend_pairprefs_pl_kernel(tc, query, item_words, item_scales, ib, offs
                 stop=True,
             )
 
-        def score(t):
-            for h in range(HALVES):
-                acc = psum4.tile([P, BANK], F32, name="acc")
-                cuts = [c for c in pieces if c[0] // BANK == h] if t == 0 else [(h * BANK, (h + 1) * BANK)]
-                for lo, hi in cuts:
-                    product(acc[:, lo - h * BANK : hi - h * BANK], t, lo, hi)
-                nc.vector.tensor_tensor(scores[t][:, h * BANK : (h + 1) * BANK], acc[:], bias_all[h][:], ALU.add)
+        def quarter_product(t, k):
+            product(t, k * QUARTER, (k + 1) * QUARTER)
+
+        def add_on_vector(t, h):
+            nc.vector.tensor_tensor(scores[t][:, h * BANK : (h + 1) * BANK], acc[t, h][:], bias_all[h][:], ALU.add)
+
+        def add_on_gpsimd(t):
+            sums = sb.tile([P, BANK], F32, name="sums%d" % t, align_bytes=64)
+            nc.scalar.copy(sums[:], acc[t, 0][:])
+            nc.gpsimd.tensor_tensor(scores[t][:, 0:BANK], sums[:], bias_all[0][:], ALU.add)
+
+        def look_up_second(t):
             nc.scalar.activation(seconds[t][:], scores[t][:].indirect(second_list[:]), ACT.Copy)
+
+        for k in range(2):
+            for t in (1, 2, 0):
+                quarter_product(t, k)
+        quarter_product(0, 2)
+        quarter_product(0, 3)
+        for t in (1, 2):
+            add_on_gpsimd(t)
+        for h in range(HALVES):
+            add_on_vector(0, h)
+        for t, h in ((1, 1), (2, 1), (3, 0), (3, 1)):
+            product(t, h * BANK, (h + 1) * BANK)
+            add_on_vector(t, h)
+        for t in range(PACK):
+            look_up_second(t)
 
         def subtract(t, lo, hi):
             nc.vector.tensor_tensor(
@@ -178,26 +200,22 @@ def tile_attend_pairprefs_pl_kernel(tc, query, item_words, item_scales, ib, offs
             nc.vector.quantize_mx(out=y_cd[:, lo:hi].bitcast(FP8X4), scales=y_sc[:, lo:hi], in_=y_bf[:, lo * PACK : hi * PACK])
             nc.sync.dma_start(words_out[:, lo:hi], y_cd[:, lo:hi].bitcast(I32))
 
-        early, late = slice(0, 2), slice(2, PACK)
+        early, late, every = slice(0, 2), slice(2, PACK), slice(0, PACK)
         front, back = (0, PAIR_HALF), (PAIR_HALF, J)
-        for t in range(PACK):
-            score(t)
-        for tiles in (early, late):
-            for lo, hi in (front, back):
-                for t in range(tiles.start, tiles.stop):
-                    subtract(t, lo, hi)
-        for lo, hi in (front, back):
-            prefer(early, lo, hi)
-            prefer_rounded(early, lo, hi)
-        store(early, 0, J)
-        prefer(late, *front)
-        store(late, *front)
+        for t, half in ((0, front), (1, front), (2, front), (0, back), (3, front), (1, back), (2, back), (3, back)):
+            subtract(t, *half)
+        prefer(slice(0, 3), *front)
+        prefer(slice(3, PACK), *front)
+        store(every, *front)
+        prefer(early, *back)
+        store(early, *back)
+        prefer_rounded(early, *back)
         prefer_rounded(late, *back)
         prefer(late, *back)
-        nc.vector.tensor_copy(woven(late, *front), by_fours(y, late, *front))
-        quantise(*front)
+        nc.vector.tensor_copy(woven(every, *front), by_fours(y, every, *front))
         store(late, *back)
         quantise(*back)
+        quantise(*front)
         for quad in range(4):
             queue = nc.scalar if quad % 2 else nc.sync
             queue.dma_start(

@@ -25,6 +25,7 @@ HALVES = I // BANK
 PAIR_HALF = J // 2
 LIST_ROWS = 16
 QUARTER = I // 4
+LAST_PAIRS = 384
 VECTOR_ZEROES = 1280
 
 
@@ -201,21 +202,19 @@ def tile_attend_pairprefs_pl_kernel(tc, query, item_words, item_scales, ib, offs
             nc.sync.dma_start(words_out[:, lo:hi], y_cd[:, lo:hi].bitcast(I32))
 
         early, late, every = slice(0, 2), slice(2, PACK), slice(0, PACK)
-        front, back = (0, PAIR_HALF), (PAIR_HALF, J)
-        for t, half in ((0, front), (1, front), (2, front), (0, back), (3, front), (1, back), (2, back), (3, back)):
-            subtract(t, *half)
-        prefer(slice(0, 3), *front)
-        prefer(slice(3, PACK), *front)
-        store(every, *front)
-        prefer(early, *back)
-        store(early, *back)
-        prefer_rounded(early, *back)
-        prefer_rounded(late, *back)
-        prefer(late, *back)
-        nc.vector.tensor_copy(woven(every, *front), by_fours(y, every, *front))
-        store(late, *back)
-        quantise(*back)
-        quantise(*front)
+        for lo, hi in ((0, LAST_PAIRS), (LAST_PAIRS, J)):
+            for t in range(PACK):
+                subtract(t, lo, hi)
+        for tiles in (early, late):
+            prefer(tiles, 0, LAST_PAIRS)
+            store(tiles, 0, LAST_PAIRS)
+        prefer_rounded(every, PAIR_HALF, LAST_PAIRS)
+        prefer_rounded(every, LAST_PAIRS, J)
+        prefer(every, LAST_PAIRS, J)
+        nc.vector.tensor_copy(woven(every, 0, PAIR_HALF), by_fours(y, every, 0, PAIR_HALF))
+        store(every, LAST_PAIRS, J)
+        quantise(PAIR_HALF, J)
+        quantise(0, PAIR_HALF)
         for quad in range(4):
             queue = nc.scalar if quad % 2 else nc.sync
             queue.dma_start(

@@ -167,13 +167,14 @@ def tile_attend_pairprefs_pl_kernel(tc, query, item_words, item_scales, ib, offs
                 quarter_product(t, k)
         quarter_product(0, 2)
         quarter_product(0, 3)
-        for t in (1, 2):
+        product(3, 0, BANK)
+        for t in range(1, PACK):
             add_on_gpsimd(t)
         for h in range(HALVES):
             add_on_vector(0, h)
-        for t, h in ((1, 1), (2, 1), (3, 0), (3, 1)):
-            product(t, h * BANK, (h + 1) * BANK)
-            add_on_vector(t, h)
+        for t in range(1, PACK):
+            product(t, BANK, I)
+            add_on_vector(t, 1)
         for t in range(PACK):
             look_up_second(t)
 
@@ -202,19 +203,26 @@ def tile_attend_pairprefs_pl_kernel(tc, query, item_words, item_scales, ib, offs
             nc.sync.dma_start(words_out[:, lo:hi], y_cd[:, lo:hi].bitcast(I32))
 
         early, late, every = slice(0, 2), slice(2, PACK), slice(0, PACK)
-        for lo, hi in ((0, LAST_PAIRS), (LAST_PAIRS, J)):
-            for t in range(PACK):
-                subtract(t, lo, hi)
-        for tiles in (early, late):
-            prefer(tiles, 0, LAST_PAIRS)
-            store(tiles, 0, LAST_PAIRS)
-        prefer_rounded(every, PAIR_HALF, LAST_PAIRS)
+        for t in range(PACK - 1):
+            subtract(t, 0, LAST_PAIRS)
+        for t in range(2):
+            subtract(t, LAST_PAIRS, J)
+        subtract(PACK - 1, 0, LAST_PAIRS)
+        for t in range(2, PACK):
+            subtract(t, LAST_PAIRS, J)
+        prefer(early, 0, LAST_PAIRS)
+        prefer(slice(2, 3), 0, LAST_PAIRS)
+        prefer(early, LAST_PAIRS, J)
+        store(early, 0, J)
+        prefer(slice(3, PACK), 0, LAST_PAIRS)
+        store(late, 0, LAST_PAIRS)
         prefer_rounded(every, LAST_PAIRS, J)
-        prefer(every, LAST_PAIRS, J)
-        nc.vector.tensor_copy(woven(every, 0, PAIR_HALF), by_fours(y, every, 0, PAIR_HALF))
-        store(every, LAST_PAIRS, J)
-        quantise(PAIR_HALF, J)
+        prefer(late, LAST_PAIRS, J)
+        for lo, hi in ((0, PAIR_HALF), (PAIR_HALF, LAST_PAIRS)):
+            nc.vector.tensor_copy(woven(every, lo, hi), by_fours(y, every, lo, hi))
+        store(late, LAST_PAIRS, J)
         quantise(0, PAIR_HALF)
+        quantise(PAIR_HALF, J)
         for quad in range(4):
             queue = nc.scalar if quad % 2 else nc.sync
             queue.dma_start(

@@ -175,9 +175,6 @@ def tile_attend_pairprefs_pl_kernel(tc, query, item_words, item_scales, ib, offs
         for t in range(1, PACK):
             product(t, BANK, I)
             add_on_vector(t, 1)
-        for t in range(PACK):
-            look_up_second(t)
-
         def subtract(t, lo, hi):
             nc.vector.tensor_tensor(
                 diff[:, t, lo:hi], scores[t][:].indirect(entries(first_list, lo, hi)), seconds[t][:, lo:hi], ALU.subtract
@@ -202,25 +199,28 @@ def tile_attend_pairprefs_pl_kernel(tc, query, item_words, item_scales, ib, offs
             nc.vector.quantize_mx(out=y_cd[:, lo:hi].bitcast(FP8X4), scales=y_sc[:, lo:hi], in_=y_bf[:, lo * PACK : hi * PACK])
             nc.sync.dma_start(words_out[:, lo:hi], y_cd[:, lo:hi].bitcast(I32))
 
-        early, late, every = slice(0, 2), slice(2, PACK), slice(0, PACK)
-        for t in range(PACK - 1):
-            subtract(t, 0, LAST_PAIRS)
-        for t in range(2):
-            subtract(t, LAST_PAIRS, J)
-        subtract(PACK - 1, 0, LAST_PAIRS)
-        for t in range(2, PACK):
-            subtract(t, LAST_PAIRS, J)
-        prefer(early, 0, LAST_PAIRS)
-        prefer(slice(2, 3), 0, LAST_PAIRS)
-        prefer(early, LAST_PAIRS, J)
-        store(early, 0, J)
-        prefer(slice(3, PACK), 0, LAST_PAIRS)
-        store(late, 0, LAST_PAIRS)
+        def finish(t, lo, hi):
+            prefer(slice(t, t + 1), lo, hi)
+            store(slice(t, t + 1), lo, hi)
+
+        every, last = slice(0, PACK), PACK - 1
+        for t in range(last):
+            look_up_second(t)
+        for t in range(last):
+            subtract(t, 0, J)
+        finish(0, 0, J)
+        look_up_second(last)
+        for lo, hi in ((0, PAIR_HALF), (PAIR_HALF, LAST_PAIRS), (LAST_PAIRS, J)):
+            subtract(last, lo, hi)
+        finish(1, 0, J)
+        finish(2, 0, J)
+        prefer(slice(last, PACK), 0, PAIR_HALF)
+        prefer(slice(last, PACK), PAIR_HALF, LAST_PAIRS)
+        store(slice(last, PACK), 0, LAST_PAIRS)
         prefer_rounded(every, LAST_PAIRS, J)
-        prefer(late, LAST_PAIRS, J)
+        finish(last, LAST_PAIRS, J)
         for lo, hi in ((0, PAIR_HALF), (PAIR_HALF, LAST_PAIRS)):
             nc.vector.tensor_copy(woven(every, lo, hi), by_fours(y, every, lo, hi))
-        store(late, LAST_PAIRS, J)
         quantise(0, PAIR_HALF)
         quantise(PAIR_HALF, J)
         for quad in range(4):

@@ -53,11 +53,8 @@ def tile_attend_pairprefs_pl_kernel(tc, query, item_words, item_scales, ib, offs
         nc.sync.dma_start(q_raw[0][:], q_rows[:, :, 0 : Q // 2])
         scale_pool = sb.tile([P, T], U8, name="scale_pool", align_bytes=64)
         nc.gpsimd.memset(scale_pool[:].bitcast(I32), 0)
-        for quad in range(4):
-            nc.sync.dma_start(
-                scale_pool[32 * quad : 32 * quad + 4, :].bitcast(I32),
-                item_scales[0, 4 * quad : 4 * quad + 4, :].bitcast(I32),
-            )
+        for row in range(4):
+            nc.sync.dma_start(scale_pool[row:P:32, :].bitcast(I32), item_scales[0, row:16:4, :].bitcast(I32))
         nc.sync.dma_start(q_raw[1][:], q_rows[:, :, Q // 2 : Q])
         word_pool = sb.tile([P, T], U32, name="word_pool", align_bytes=64)
         nc.sync.dma_start(word_pool[:].bitcast(I32), item_words[0].rearrange("p n t -> p (n t)").bitcast(I32))

@@ -25,6 +25,7 @@ HALVES = I // BANK
 PAIR_HALF = J // 2
 LIST_ROWS = 16
 QUARTER = I // 4
+VECTOR_BIASES = 640
 LAST_PAIRS = 384
 VECTOR_ZEROES = 1280
 
@@ -75,7 +76,7 @@ def tile_attend_pairprefs_pl_kernel(tc, query, item_words, item_scales, ib, offs
         def dealt(h):
             return q_dealt[:, h * (P // 2) : (h + 1) * (P // 2)], q_raw[h][:].rearrange("p r (m t) -> p m r t", t=PACK)
 
-        bias_row = [sb.tile([P, BANK], F32, name="bias_row%d" % h, align_bytes=64) for h in range(HALVES)]
+        bias_row = sb.tile([P, I], F32, name="bias_row", align_bytes=64)
         bias_col = [
             reused.tile([P, BLOCKS], F32, name="bias_col0", offset=6272, align_bytes=64),
             reused.tile([P, BLOCKS], F32, name="bias_col1", offset=6208, align_bytes=64),
@@ -88,7 +89,7 @@ def tile_attend_pairprefs_pl_kernel(tc, query, item_words, item_scales, ib, offs
         def bias_to_columns(h):
             turned = psum.tile([P, BANK], F32, name="bias_turned", tag="bank%d" % h)
             for b in range(BLOCKS):
-                nc.tensor.transpose(turned[:, b * P : (b + 1) * P], bias_row[h][:, b * P : (b + 1) * P], ident[:])
+                nc.tensor.transpose(turned[:, b * P : (b + 1) * P], bias_row[:, h * BANK + b * P : h * BANK + (b + 1) * P], ident[:])
             nc.scalar.copy(bias_col[h][:], turned[:, BIAS_ROW:BANK:P])
 
         def bias_to_all_rows(h):
@@ -97,8 +98,8 @@ def tile_attend_pairprefs_pl_kernel(tc, query, item_words, item_scales, ib, offs
                 nc.tensor.transpose(spread[:, b * P : (b + 1) * P], bias_col[h][:, b : b + 1].to_broadcast([P, P]), ident[:])
             nc.scalar.copy(bias_all[h][:], spread[:])
 
-        nc.vector.tensor_copy(bias_row[0][:], bias_pool[:].indirect(entries(slot_list, 0, BANK)))
-        nc.scalar.activation(bias_row[1][:], bias_pool[:].indirect(entries(slot_list, BANK, I)), ACT.Copy)
+        nc.vector.tensor_copy(bias_row[:, 0:VECTOR_BIASES], bias_pool[:].indirect(entries(slot_list, 0, VECTOR_BIASES)))
+        nc.scalar.activation(bias_row[:, VECTOR_BIASES:I], bias_pool[:].indirect(entries(slot_list, VECTOR_BIASES, I)), ACT.Copy)
         item_sc = sb.tile([P, I], U8, name="item_sc", align_bytes=64)
         nc.vector.tensor_copy(item_sc[:], scale_pool[:].indirect(slot_list[:]))
 
@@ -148,30 +149,39 @@ def tile_attend_pairprefs_pl_kernel(tc, query, item_words, item_scales, ib, offs
         def quarter_product(t, k):
             product(t, k * QUARTER, (k + 1) * QUARTER)
 
-        def add_on_vector(t, h):
-            nc.vector.tensor_tensor(scores[t][:, h * BANK : (h + 1) * BANK], acc[t, h][:], bias_all[h][:], ALU.add)
+        def add_on_vector(t, lo, hi):
+            h = lo // BANK
+            cols = slice(lo - h * BANK, hi - h * BANK)
+            nc.vector.tensor_tensor(scores[t][:, lo:hi], acc[t, h][:, cols], bias_all[h][:, cols], ALU.add)
 
-        def add_on_gpsimd(t):
-            sums = sb.tile([P, BANK], F32, name="sums%d" % t, align_bytes=64)
-            nc.scalar.copy(sums[:], acc[t, 0][:])
-            nc.gpsimd.tensor_tensor(scores[t][:, 0:BANK], sums[:], bias_all[0][:], ALU.add)
+        def add_on_gpsimd(t, hi):
+            sums = sb.tile([P, hi], F32, name="sums%d" % t, align_bytes=64)
+            nc.scalar.copy(sums[:], acc[t, 0][:, 0:hi])
+            nc.gpsimd.tensor_tensor(scores[t][:, 0:hi], sums[:], bias_all[0][:, 0:hi], ALU.add)
 
         def look_up_second(t):
             nc.scalar.activation(seconds[t][:], scores[t][:].indirect(second_list[:]), ACT.Copy)
 
+        quarter_product(3, 0)
+        add_on_gpsimd(3, QUARTER)
         for k in range(2):
-            for t in (1, 2, 0):
+            for t in (1, 0):
                 quarter_product(t, k)
+        add_on_gpsimd(1, BANK)
+        quarter_product(2, 0)
         quarter_product(0, 2)
         quarter_product(0, 3)
-        product(3, 0, BANK)
-        for t in range(1, PACK):
-            add_on_gpsimd(t)
+        quarter_product(2, 1)
+        add_on_gpsimd(2, BANK)
         for h in range(HALVES):
-            add_on_vector(0, h)
-        for t in range(1, PACK):
+            add_on_vector(0, h * BANK, (h + 1) * BANK)
+        for t in (1, 2):
             product(t, BANK, I)
-            add_on_vector(t, 1)
+            add_on_vector(t, BANK, I)
+        quarter_product(3, 1)
+        add_on_vector(3, QUARTER, BANK)
+        product(3, BANK, I)
+        add_on_vector(3, BANK, I)
         def subtract(t, lo, hi):
             nc.vector.tensor_tensor(
                 diff[:, t, lo:hi], scores[t][:].indirect(entries(first_list, lo, hi)), seconds[t][:, lo:hi], ALU.subtract
@@ -201,17 +211,18 @@ def tile_attend_pairprefs_pl_kernel(tc, query, item_words, item_scales, ib, offs
             store(slice(t, t + 1), lo, hi)
 
         every, last = slice(0, PACK), PACK - 1
-        for t in range(last):
+        for t in range(PACK):
             look_up_second(t)
         for t in range(last):
             subtract(t, 0, J)
         finish(0, 0, J)
-        look_up_second(last)
         for lo, hi in ((0, PAIR_HALF), (PAIR_HALF, LAST_PAIRS), (LAST_PAIRS, J)):
             subtract(last, lo, hi)
         finish(1, 0, J)
-        finish(2, 0, J)
+        prefer(slice(2, 3), 0, PAIR_HALF)
         prefer(slice(last, PACK), 0, PAIR_HALF)
+        prefer(slice(2, 3), PAIR_HALF, J)
+        store(slice(2, 3), 0, J)
         prefer(slice(last, PACK), PAIR_HALF, LAST_PAIRS)
         store(slice(last, PACK), 0, LAST_PAIRS)
         prefer_rounded(every, LAST_PAIRS, J)

@@ -222,11 +222,11 @@ def tile_attend_pairprefs_pl_kernel(tc, query, item_words, item_scales, ib, offs
         prefer(slice(2, 3), 0, PAIR_HALF)
         prefer(slice(last, PACK), 0, PAIR_HALF)
         prefer(slice(2, 3), PAIR_HALF, J)
-        store(slice(2, 3), 0, J)
         prefer(slice(last, PACK), PAIR_HALF, LAST_PAIRS)
-        store(slice(last, PACK), 0, LAST_PAIRS)
+        store(slice(2, PACK), 0, LAST_PAIRS)
         prefer_rounded(every, LAST_PAIRS, J)
-        finish(last, LAST_PAIRS, J)
+        prefer(slice(last, PACK), LAST_PAIRS, J)
+        store(slice(2, PACK), LAST_PAIRS, J)
         for lo, hi in ((0, PAIR_HALF), (PAIR_HALF, LAST_PAIRS)):
             nc.vector.tensor_copy(woven(every, lo, hi), by_fours(y, every, lo, hi))
         quantise(0, PAIR_HALF)

@@ -26,7 +26,7 @@ PAIR_HALF = J // 2
 LIST_ROWS = 16
 QUARTER = I // 4
 VECTOR_BIASES = 640
-LAST_PAIRS = 384
+PAIR_QUARTER = J // 4
 VECTOR_ZEROES = 1280
 
 
@@ -78,7 +78,7 @@ def tile_attend_pairprefs_pl_kernel(tc, query, item_words, item_scales, ib, offs
 
         bias_row = sb.tile([P, I], F32, name="bias_row", align_bytes=64)
         bias_col = [
-            reused.tile([P, BLOCKS], F32, name="bias_col0", offset=6272, align_bytes=64),
+            sb.tile([P, BLOCKS], F32, name="bias_col0", align_bytes=64),
             reused.tile([P, BLOCKS], F32, name="bias_col1", offset=6208, align_bytes=64),
         ]
         bias_all = [
@@ -103,9 +103,9 @@ def tile_attend_pairprefs_pl_kernel(tc, query, item_words, item_scales, ib, offs
         item_sc = sb.tile([P, I], U8, name="item_sc", align_bytes=64)
         nc.vector.tensor_copy(item_sc[:], scale_pool[:].indirect(slot_list[:]))
 
-        for h in range(2):
-            nc.scalar.copy(*dealt(h))
+        nc.scalar.copy(*dealt(0))
         bias_to_columns(0)
+        nc.scalar.copy(*dealt(1))
         bias_to_columns(1)
         bias_to_all_rows(0)
         bias_to_all_rows(1)
@@ -119,25 +119,21 @@ def tile_attend_pairprefs_pl_kernel(tc, query, item_words, item_scales, ib, offs
             nc.vector.tensor_copy(item_cd[:, lo : lo + QUARTER], word_pool[:].indirect(entries(slot_list, lo, lo + QUARTER)))
 
         scores = [sb.tile([P, I], F32, name="scores%d" % t, align_bytes=64) for t in range(PACK)]
-        seconds = [sb.tile([P, J], F32, name="seconds%d" % t, align_bytes=64) for t in range(PACK)]
         diff = sb.tile([P, PACK, J], F32, name="diff", align_bytes=64)
         y = sb.tile([P, PACK, J], F32, name="y", align_bytes=64)
-        y_rows = out_0.rearrange("(p t) j -> p t j", t=PACK)
+        y_rows = out_0.rearrange("(p t) j -> p (t j)", t=PACK)
+        y_flat = y[:].rearrange("p t j -> p (t j)")
         y_bf = sb.tile([P, J * PACK], BF16, name="y_bf", align_bytes=64)
         y_cd = sb.tile([P, J], U32, name="y_cd", align_bytes=64)
         y_sc = sb.tile([P, J], U8, name="y_sc", align_bytes=64)
         words_out = out_1[0].rearrange("p c t -> p (c t)").bitcast(I32)
 
-        acc = {
-            (t, h): psum.tile([P, BANK], F32, name="acc%d_%d" % (t, h), tag="bank%d" % (t if h else PACK + t))
-            for t in range(PACK)
-            for h in range(HALVES)
-        }
+        def bank(number, name):
+            return psum.tile([P, BANK], F32, name=name, tag="bank%d" % number)
 
-        def product(t, lo, hi):
-            h = lo // BANK
+        def product(acc, t, lo, hi):
             nc.tensor.matmul_mx(
-                out=acc[t, h][:, lo - h * BANK : hi - h * BANK],
+                out=acc[:, lo % BANK : lo % BANK + hi - lo],
                 lhsT=q_cd[:, t * P : (t + 1) * P].bitcast(FP8X4),
                 lhsT_scale=q_sc[:, t * P : (t + 1) * P],
                 rhs=item_cd[:, lo:hi].bitcast(FP8X4),
@@ -146,42 +142,26 @@ def tile_attend_pairprefs_pl_kernel(tc, query, item_words, item_scales, ib, offs
                 stop=True,
             )
 
-        def quarter_product(t, k):
-            product(t, k * QUARTER, (k + 1) * QUARTER)
+        def add_on_vector(acc, t, lo, hi):
+            cols = slice(lo % BANK, lo % BANK + hi - lo)
+            nc.vector.tensor_tensor(scores[t][:, lo:hi], acc[:, cols], bias_all[lo // BANK][:, cols], ALU.add)
 
-        def add_on_vector(t, lo, hi):
-            h = lo // BANK
-            cols = slice(lo - h * BANK, hi - h * BANK)
-            nc.vector.tensor_tensor(scores[t][:, lo:hi], acc[t, h][:, cols], bias_all[h][:, cols], ALU.add)
+        def add_on_gpsimd(acc, t, lo, hi):
+            sums = sb.tile([P, hi - lo], F32, name="sums%d_%d" % (t, lo), align_bytes=64)
+            nc.scalar.copy(sums[:], acc[:, lo:hi])
+            nc.gpsimd.tensor_tensor(scores[t][:, lo:hi], sums[:], bias_all[0][:, lo:hi], ALU.add)
 
-        def add_on_gpsimd(t, hi):
-            sums = sb.tile([P, hi], F32, name="sums%d" % t, align_bytes=64)
-            nc.scalar.copy(sums[:], acc[t, 0][:, 0:hi])
-            nc.gpsimd.tensor_tensor(scores[t][:, 0:hi], sums[:], bias_all[0][:, 0:hi], ALU.add)
+        def score(add, number, t, lo, hi):
+            acc = bank(number, "acc%d_%d" % (t, lo))
+            product(acc, t, lo, hi)
+            add(acc, t, lo, hi)
+
+        seconds = {}
 
         def look_up_second(t):
+            seconds[t] = sb.tile([P, J], F32, name="seconds%d" % t, align_bytes=64)
             nc.scalar.activation(seconds[t][:], scores[t][:].indirect(second_list[:]), ACT.Copy)
 
-        quarter_product(3, 0)
-        add_on_gpsimd(3, QUARTER)
-        for k in range(2):
-            for t in (1, 0):
-                quarter_product(t, k)
-        add_on_gpsimd(1, BANK)
-        quarter_product(2, 0)
-        quarter_product(0, 2)
-        quarter_product(0, 3)
-        quarter_product(2, 1)
-        add_on_gpsimd(2, BANK)
-        for h in range(HALVES):
-            add_on_vector(0, h * BANK, (h + 1) * BANK)
-        for t in (1, 2):
-            product(t, BANK, I)
-            add_on_vector(t, BANK, I)
-        quarter_product(3, 1)
-        add_on_vector(3, QUARTER, BANK)
-        product(3, BANK, I)
-        add_on_vector(3, BANK, I)
         def subtract(t, lo, hi):
             nc.vector.tensor_tensor(
                 diff[:, t, lo:hi], scores[t][:].indirect(entries(first_list, lo, hi)), seconds[t][:, lo:hi], ALU.subtract
@@ -190,47 +170,67 @@ def tile_attend_pairprefs_pl_kernel(tc, query, item_words, item_scales, ib, offs
         def prefer(tiles, lo, hi):
             nc.scalar.activation(y[:, tiles, lo:hi], diff[:, tiles, lo:hi], ACT.Sigmoid)
 
-        def store(tiles, lo, hi):
-            nc.sync.dma_start(y_rows[:, tiles, lo:hi], y[:, tiles, lo:hi])
+        def store(lo, hi):
+            nc.sync.dma_start(y_rows[:, lo:hi], y_flat[:, lo:hi])
 
-        def woven(tiles, lo, hi):
-            return y_bf[:, lo * PACK : hi * PACK].rearrange("p (c i t) -> p c t i", i=4, t=PACK)[:, :, tiles, :]
+        def woven(lo, hi):
+            return y_bf[:, lo * PACK : hi * PACK].rearrange("p (c i t) -> p c t i", i=4, t=PACK)
 
-        def by_fours(source, tiles, lo, hi):
-            return source[:, tiles, lo:hi].rearrange("p t (c i) -> p c t i", i=4)
-
-        def prefer_rounded(tiles, lo, hi):
-            nc.scalar.activation(woven(tiles, lo, hi), by_fours(diff, tiles, lo, hi), ACT.Sigmoid)
+        def by_fours(source, lo, hi):
+            return source[:, :, lo:hi].rearrange("p t (c i) -> p c t i", i=4)
 
         def quantise(lo, hi):
             nc.vector.quantize_mx(out=y_cd[:, lo:hi].bitcast(FP8X4), scales=y_sc[:, lo:hi], in_=y_bf[:, lo * PACK : hi * PACK])
+
+        def store_words(lo, hi):
             nc.sync.dma_start(words_out[:, lo:hi], y_cd[:, lo:hi].bitcast(I32))
 
-        def finish(t, lo, hi):
-            prefer(slice(t, t + 1), lo, hi)
-            store(slice(t, t + 1), lo, hi)
+        front = bank(6, "front")
+        score(add_on_gpsimd, 4, 0, 0, QUARTER)
+        product(front, 1, 0, QUARTER)
+        score(add_on_gpsimd, 5, 0, QUARTER, BANK)
+        product(front, 1, QUARTER, BANK)
+        add_on_gpsimd(front, 1, 0, BANK)
+        score(add_on_vector, 7, 0, BANK, I - QUARTER)
+        third = bank(0, "third")
+        product(third, 2, 0, QUARTER)
+        product(third, 2, QUARTER, BANK - P)
+        add_on_gpsimd(third, 2, 0, BANK - P)
+        score(add_on_vector, 1, 0, I - QUARTER, I)
+        look_up_second(0)
+        score(add_on_vector, 2, 1, BANK, I)
+        look_up_second(1)
+        score(add_on_vector, 7, 2, BANK - P, BANK)
+        score(add_on_vector, 3, 2, BANK, I)
+        score(add_on_vector, 4, 3, 0, BANK)
+        score(add_on_vector, 5, 3, BANK, I)
+        look_up_second(2)
+        look_up_second(3)
 
-        every, last = slice(0, PACK), PACK - 1
-        for t in range(PACK):
-            look_up_second(t)
-        for t in range(last):
-            subtract(t, 0, J)
-        finish(0, 0, J)
-        for lo, hi in ((0, PAIR_HALF), (PAIR_HALF, LAST_PAIRS), (LAST_PAIRS, J)):
+        last = PACK - 1
+        subtract(0, 0, J)
+        prefer(slice(0, 1), 0, J)
+        store(0, J)
+        subtract(1, 0, J)
+        prefer(slice(1, 2), 0, J)
+        store(J, 2 * J)
+        subtract(2, 0, J)
+        prefer(slice(2, 3), 0, J)
+        for lo, hi in ((0, PAIR_HALF), (PAIR_HALF, J - PAIR_QUARTER), (J - PAIR_QUARTER, J)):
             subtract(last, lo, hi)
-        finish(1, 0, J)
-        prefer(slice(2, 3), 0, PAIR_HALF)
         prefer(slice(last, PACK), 0, PAIR_HALF)
-        prefer(slice(2, 3), PAIR_HALF, J)
-        prefer(slice(last, PACK), PAIR_HALF, LAST_PAIRS)
-        store(slice(2, PACK), 0, LAST_PAIRS)
-        prefer_rounded(every, LAST_PAIRS, J)
-        prefer(slice(last, PACK), LAST_PAIRS, J)
-        store(slice(2, PACK), LAST_PAIRS, J)
-        for lo, hi in ((0, PAIR_HALF), (PAIR_HALF, LAST_PAIRS)):
-            nc.vector.tensor_copy(woven(every, lo, hi), by_fours(y, every, lo, hi))
-        quantise(0, PAIR_HALF)
+        store(2 * J, last * J + PAIR_HALF)
+        for lo in (PAIR_HALF, J - PAIR_QUARTER):
+            nc.scalar.activation(woven(lo, lo + PAIR_QUARTER), by_fours(diff, lo, lo + PAIR_QUARTER), ACT.Sigmoid)
+        prefer(slice(last, PACK), PAIR_HALF, J)
+        for lo in (0, PAIR_QUARTER):
+            nc.vector.tensor_copy(woven(lo, lo + PAIR_QUARTER), by_fours(y, lo, lo + PAIR_QUARTER))
+        for lo in (0, PAIR_QUARTER):
+            quantise(lo, lo + PAIR_QUARTER)
+        store_words(0, PAIR_HALF)
+        store(last * J + PAIR_HALF, PACK * J)
         quantise(PAIR_HALF, J)
+        store_words(PAIR_HALF, J)
         for quad in range(4):
             queue = nc.scalar if quad % 2 else nc.sync
             queue.dma_start(

@@ -215,22 +215,22 @@ def tile_attend_pairprefs_pl_kernel(tc, query, item_words, item_scales, ib, offs
         prefer(slice(1, 2), 0, J)
         store(J, 2 * J)
         subtract(2, 0, J)
-        prefer(slice(2, 3), 0, J)
-        for lo, hi in ((0, PAIR_HALF), (PAIR_HALF, J - PAIR_QUARTER), (J - PAIR_QUARTER, J)):
+        late = J - PAIR_QUARTER
+        for lo, hi in ((0, PAIR_HALF), (PAIR_HALF, late), (late, J)):
             subtract(last, lo, hi)
+        prefer(slice(2, 3), 0, PAIR_HALF)
         prefer(slice(last, PACK), 0, PAIR_HALF)
-        store(2 * J, last * J + PAIR_HALF)
-        for lo in (PAIR_HALF, J - PAIR_QUARTER):
-            nc.scalar.activation(woven(lo, lo + PAIR_QUARTER), by_fours(diff, lo, lo + PAIR_QUARTER), ACT.Sigmoid)
-        prefer(slice(last, PACK), PAIR_HALF, J)
-        for lo in (0, PAIR_QUARTER):
-            nc.vector.tensor_copy(woven(lo, lo + PAIR_QUARTER), by_fours(y, lo, lo + PAIR_QUARTER))
-        for lo in (0, PAIR_QUARTER):
-            quantise(lo, lo + PAIR_QUARTER)
-        store_words(0, PAIR_HALF)
-        store(last * J + PAIR_HALF, PACK * J)
-        quantise(PAIR_HALF, J)
-        store_words(PAIR_HALF, J)
+        prefer(slice(2, 3), PAIR_HALF, J)
+        prefer(slice(last, PACK), PAIR_HALF, late)
+        store(2 * J, last * J + late)
+        nc.scalar.activation(woven(late, J), by_fours(diff, late, J), ACT.Sigmoid)
+        prefer(slice(last, PACK), late, J)
+        store(last * J + late, PACK * J)
+        for lo, hi in ((0, PAIR_HALF), (PAIR_HALF, late)):
+            nc.vector.tensor_copy(woven(lo, hi), by_fours(y, lo, hi))
+        for lo in (0, PAIR_HALF):
+            quantise(lo, lo + PAIR_HALF)
+            store_words(lo, lo + PAIR_HALF)
         for quad in range(4):
             queue = nc.scalar if quad % 2 else nc.sync
             queue.dma_start(

@@ -21,12 +21,12 @@ PACK = 4
 BANK = 512
 BIAS_ROW = P - 1
 BLOCKS = BANK // P
-HALVES = I // BANK
 PAIR_HALF = J // 2
+PAIR_QUARTER = J // 4
 LIST_ROWS = 16
 QUARTER = I // 4
-VECTOR_BIASES = 640
-PAIR_QUARTER = J // 4
+SCALAR_GROUPS = 64
+SHARED_SLOTS = 384
 VECTOR_ZEROES = 1280
 
 
@@ -41,23 +41,26 @@ def tile_attend_pairprefs_pl_kernel(tc, query, item_words, item_scales, ib, offs
         def entries(tile, lo, hi):
             return tile[:, lo // LIST_ROWS : hi // LIST_ROWS]
 
+        def bank(number, name):
+            return psum.tile([P, BANK], F32, name=name, tag="bank%d" % number)
+
         slot_list = lists.tile([P, I // LIST_ROWS], U16, name="slot_list")
         first_list = lists.tile([P, J // LIST_ROWS], U16, name="first_list")
         second_list = lists.tile([P, J // LIST_ROWS], U16, name="second_list")
-        nc.sync.dma_start(slot_list[:], offs)
-
-        bias_pool = sb.tile([P, T], F32, name="bias_pool", align_bytes=64)
-        nc.vector.memset(bias_pool[0:BIAS_ROW, 0:VECTOR_ZEROES].bitcast(I32), 0)
-        nc.sync.dma_start(bias_pool[BIAS_ROW:P, :], ib[0:1, :])
-        q_rows = query.rearrange("(p r) q -> p r q", r=PACK)
-        q_raw = [reused.tile([P, PACK, Q // 2], F32, name="q_raw%d" % h, offset=4096 * h, align_bytes=64) for h in range(2)]
-        nc.sync.dma_start(q_raw[0][:], q_rows[:, :, 0 : Q // 2])
         scale_pool = sb.tile([P, T], U8, name="scale_pool", align_bytes=64)
+        bias_pool = sb.tile([P, T], F32, name="bias_pool", align_bytes=64)
+        q_raw = reused.tile([P, PACK, Q], F32, name="q_raw", offset=0, align_bytes=64)
+        word_pool = sb.tile([P, T], U32, name="word_pool", align_bytes=64)
+
         nc.gpsimd.memset(scale_pool[:].bitcast(I32), 0)
+        nc.vector.memset(bias_pool[0:BIAS_ROW, 0:VECTOR_ZEROES].bitcast(I32), 0)
+        q_rows = query.rearrange("(p r) q -> p r q", r=PACK)
+        nc.sync.dma_start(q_raw[:, 0:1], q_rows[:, 0:1])
+        nc.sync.dma_start(slot_list[:], offs)
+        nc.sync.dma_start(bias_pool[BIAS_ROW:P, :], ib[0:1, :])
         for row in range(4):
             nc.sync.dma_start(scale_pool[row:P:32, :].bitcast(I32), item_scales[0, row:16:4, :].bitcast(I32))
-        nc.sync.dma_start(q_raw[1][:], q_rows[:, :, Q // 2 : Q])
-        word_pool = sb.tile([P, T], U32, name="word_pool", align_bytes=64)
+        nc.sync.dma_start(q_raw[:, 1:PACK], q_rows[:, 1:PACK])
         nc.sync.dma_start(word_pool[:].bitcast(I32), item_words[0].rearrange("p n t -> p (n t)").bitcast(I32))
         nc.sync.dma_start(second_list[:], offs3)
         nc.sync.dma_start(first_list[:], offs2)
@@ -70,45 +73,33 @@ def tile_attend_pairprefs_pl_kernel(tc, query, item_words, item_scales, ib, offs
         ident = sb.tile([P, P], F32, name="ident", align_bytes=64)
         make_identity(nc, ident[:])
 
-        q_bf = sb.tile([P, Q * PACK], BF16, name="q_bf", align_bytes=64)
-        q_dealt = q_bf[:].rearrange("p (t m r) -> p m r t", t=PACK, r=PACK)
-
-        def dealt(h):
-            return q_dealt[:, h * (P // 2) : (h + 1) * (P // 2)], q_raw[h][:].rearrange("p r (m t) -> p m r t", t=PACK)
-
-        bias_row = sb.tile([P, I], F32, name="bias_row", align_bytes=64)
-        bias_col = [
-            sb.tile([P, BLOCKS], F32, name="bias_col0", align_bytes=64),
-            reused.tile([P, BLOCKS], F32, name="bias_col1", offset=6208, align_bytes=64),
-        ]
-        bias_all = [
-            reused.tile([P, BANK], F32, name="bias_all0", offset=4160, align_bytes=64),
-            sb.tile([P, BANK], F32, name="bias_all1", align_bytes=64),
-        ]
-
-        def bias_to_columns(h):
-            turned = psum.tile([P, BANK], F32, name="bias_turned", tag="bank%d" % h)
-            for b in range(BLOCKS):
-                nc.tensor.transpose(turned[:, b * P : (b + 1) * P], bias_row[:, h * BANK + b * P : h * BANK + (b + 1) * P], ident[:])
-            nc.scalar.copy(bias_col[h][:], turned[:, BIAS_ROW:BANK:P])
-
-        def bias_to_all_rows(h):
-            spread = psum.tile([P, BANK], F32, name="bias_spread", tag="bank%d" % (2 + h))
-            for b in range(BLOCKS):
-                nc.tensor.transpose(spread[:, b * P : (b + 1) * P], bias_col[h][:, b : b + 1].to_broadcast([P, P]), ident[:])
-            nc.scalar.copy(bias_all[h][:], spread[:])
-
-        nc.vector.tensor_copy(bias_row[:, 0:VECTOR_BIASES], bias_pool[:].indirect(entries(slot_list, 0, VECTOR_BIASES)))
-        nc.scalar.activation(bias_row[:, VECTOR_BIASES:I], bias_pool[:].indirect(entries(slot_list, VECTOR_BIASES, I)), ACT.Copy)
         item_sc = sb.tile([P, I], U8, name="item_sc", align_bytes=64)
         nc.vector.tensor_copy(item_sc[:], scale_pool[:].indirect(slot_list[:]))
 
-        nc.scalar.copy(*dealt(0))
-        bias_to_columns(0)
-        nc.scalar.copy(*dealt(1))
-        bias_to_columns(1)
-        bias_to_all_rows(0)
-        bias_to_all_rows(1)
+        bias_row = sb.tile([P, I], F32, name="bias_row", align_bytes=64)
+        bias_col = [sb.tile([P, BLOCKS], F32, name="bias_col%d" % h, align_bytes=64) for h in range(2)]
+        bias_all = [reused.tile([P, BANK], F32, name="bias_all%d" % h, offset=4160 + 2048 * h, align_bytes=64) for h in range(2)]
+        for h in range(2):
+            half = slice(h * BANK, (h + 1) * BANK)
+            nc.scalar.activation(bias_row[:, half], bias_pool[:].indirect(entries(slot_list, half.start, half.stop)), ACT.Copy)
+        spread = []
+        for h in range(2):
+            turned = bank(h, "bias_turned")
+            for b in range(BLOCKS):
+                nc.tensor.transpose(turned[:, b * P : (b + 1) * P], bias_row[:, h * BANK + b * P : h * BANK + (b + 1) * P], ident[:])
+            nc.scalar.copy(bias_col[h][:], turned[:, BIAS_ROW:BANK:P])
+        for h in range(2):
+            spread.append(bank(2 + h, "bias_spread"))
+            for b in range(BLOCKS):
+                nc.tensor.transpose(spread[h][:, b * P : (b + 1) * P], bias_col[h][:, b : b + 1].to_broadcast([P, P]), ident[:])
+
+        q_bf = sb.tile([P, Q * PACK], BF16, name="q_bf", align_bytes=64)
+        q_dealt = q_bf[:].rearrange("p (t m r) -> p m r t", t=PACK, r=PACK)
+        q_groups = q_raw[:].rearrange("p r (m t) -> p m r t", t=PACK)
+        nc.scalar.copy(q_dealt[:, 0:SCALAR_GROUPS], q_groups[:, 0:SCALAR_GROUPS])
+        nc.vector.tensor_copy(q_dealt[:, SCALAR_GROUPS:P], q_groups[:, SCALAR_GROUPS:P])
+        for h in range(2):
+            nc.scalar.copy(bias_all[h][:], spread[h][:])
 
         q_cd = sb.tile([P, Q], U32, name="q_cd", align_bytes=64)
         q_sc = sb.tile([P, Q], U8, name="q_sc", align_bytes=64)
@@ -127,9 +118,6 @@ def tile_attend_pairprefs_pl_kernel(tc, query, item_words, item_scales, ib, offs
         y_cd = sb.tile([P, J], U32, name="y_cd", align_bytes=64)
         y_sc = sb.tile([P, J], U8, name="y_sc", align_bytes=64)
         words_out = out_1[0].rearrange("p c t -> p (c t)").bitcast(I32)
-
-        def bank(number, name):
-            return psum.tile([P, BANK], F32, name=name, tag="bank%d" % number)
 
         def product(acc, t, lo, hi):
             nc.tensor.matmul_mx(
@@ -156,11 +144,13 @@ def tile_attend_pairprefs_pl_kernel(tc, query, item_words, item_scales, ib, offs
             product(acc, t, lo, hi)
             add(acc, t, lo, hi)
 
-        seconds = {}
+        seconds = [sb.tile([P, J], F32, name="seconds%d" % t, align_bytes=64) for t in range(PACK)]
 
-        def look_up_second(t):
-            seconds[t] = sb.tile([P, J], F32, name="seconds%d" % t, align_bytes=64)
-            nc.scalar.activation(seconds[t][:], scores[t][:].indirect(second_list[:]), ACT.Copy)
+        def look_up(out, t, pair_list, lo, hi):
+            nc.scalar.activation(out, scores[t][:].indirect(entries(pair_list, lo, hi)), ACT.Copy)
+
+        def look_up_second(t, lo, hi):
+            look_up(seconds[t][:, lo:hi], t, second_list, lo, hi)
 
         def subtract(t, lo, hi):
             nc.vector.tensor_tensor(
@@ -194,18 +184,19 @@ def tile_attend_pairprefs_pl_kernel(tc, query, item_words, item_scales, ib, offs
         score(add_on_vector, 7, 0, BANK, I - QUARTER)
         third = bank(0, "third")
         product(third, 2, 0, QUARTER)
-        product(third, 2, QUARTER, BANK - P)
-        add_on_gpsimd(third, 2, 0, BANK - P)
+        product(third, 2, QUARTER, SHARED_SLOTS)
+        add_on_gpsimd(third, 2, 0, SHARED_SLOTS)
         score(add_on_vector, 1, 0, I - QUARTER, I)
-        look_up_second(0)
+
+        look_up_second(0, 0, J)
         score(add_on_vector, 2, 1, BANK, I)
-        look_up_second(1)
-        score(add_on_vector, 7, 2, BANK - P, BANK)
+        look_up_second(1, 0, J)
+        score(add_on_vector, 7, 2, SHARED_SLOTS, BANK)
         score(add_on_vector, 3, 2, BANK, I)
         score(add_on_vector, 4, 3, 0, BANK)
         score(add_on_vector, 5, 3, BANK, I)
-        look_up_second(2)
-        look_up_second(3)
+        look_up_second(2, 0, J)
+        look_up_second(3, 0, J)
 
         last = PACK - 1
         subtract(0, 0, J)

@@ -25,7 +25,8 @@ PAIR_HALF = J // 2
 PAIR_QUARTER = J // 4
 LIST_ROWS = 16
 QUARTER = I // 4
-SCALAR_GROUPS = 64
+SCALAR_GROUPS = 80
+VECTOR_BIASES = 256
 SHARED_SLOTS = 384
 VECTOR_ZEROES = 1280
 
@@ -73,15 +74,15 @@ def tile_attend_pairprefs_pl_kernel(tc, query, item_words, item_scales, ib, offs
         ident = sb.tile([P, P], F32, name="ident", align_bytes=64)
         make_identity(nc, ident[:])
 
+        bias_row = sb.tile([P, I], F32, name="bias_row", align_bytes=64)
+        nc.vector.tensor_copy(bias_row[:, 0:VECTOR_BIASES], bias_pool[:].indirect(entries(slot_list, 0, VECTOR_BIASES)))
         item_sc = sb.tile([P, I], U8, name="item_sc", align_bytes=64)
         nc.vector.tensor_copy(item_sc[:], scale_pool[:].indirect(slot_list[:]))
 
-        bias_row = sb.tile([P, I], F32, name="bias_row", align_bytes=64)
         bias_col = [sb.tile([P, BLOCKS], F32, name="bias_col%d" % h, align_bytes=64) for h in range(2)]
         bias_all = [reused.tile([P, BANK], F32, name="bias_all%d" % h, offset=4160 + 2048 * h, align_bytes=64) for h in range(2)]
-        for h in range(2):
-            half = slice(h * BANK, (h + 1) * BANK)
-            nc.scalar.activation(bias_row[:, half], bias_pool[:].indirect(entries(slot_list, half.start, half.stop)), ACT.Copy)
+        for lo, hi in ((VECTOR_BIASES, BANK), (BANK, I)):
+            nc.scalar.activation(bias_row[:, lo:hi], bias_pool[:].indirect(entries(slot_list, lo, hi)), ACT.Copy)
         spread = []
         for h in range(2):
             turned = bank(h, "bias_turned")
@@ -96,7 +97,8 @@ def tile_attend_pairprefs_pl_kernel(tc, query, item_words, item_scales, ib, offs
         q_bf = sb.tile([P, Q * PACK], BF16, name="q_bf", align_bytes=64)
         q_dealt = q_bf[:].rearrange("p (t m r) -> p m r t", t=PACK, r=PACK)
         q_groups = q_raw[:].rearrange("p r (m t) -> p m r t", t=PACK)
-        nc.scalar.copy(q_dealt[:, 0:SCALAR_GROUPS], q_groups[:, 0:SCALAR_GROUPS])
+        for lo in (0, SCALAR_GROUPS // 2):
+            nc.scalar.copy(q_dealt[:, lo : lo + SCALAR_GROUPS // 2], q_groups[:, lo : lo + SCALAR_GROUPS // 2])
         nc.vector.tensor_copy(q_dealt[:, SCALAR_GROUPS:P], q_groups[:, SCALAR_GROUPS:P])
         for h in range(2):
             nc.scalar.copy(bias_all[h][:], spread[h][:])

@@ -25,7 +25,7 @@ PAIR_HALF = J // 2
 PAIR_QUARTER = J // 4
 LIST_ROWS = 16
 QUARTER = I // 4
-SCALAR_GROUPS = 80
+SCALAR_GROUPS = 32
 VECTOR_BIASES = 256
 SHARED_SLOTS = 384
 VECTOR_ZEROES = 1280
@@ -97,15 +97,17 @@ def tile_attend_pairprefs_pl_kernel(tc, query, item_words, item_scales, ib, offs
         q_bf = sb.tile([P, Q * PACK], BF16, name="q_bf", align_bytes=64)
         q_dealt = q_bf[:].rearrange("p (t m r) -> p m r t", t=PACK, r=PACK)
         q_groups = q_raw[:].rearrange("p r (m t) -> p m r t", t=PACK)
-        for lo in (0, SCALAR_GROUPS // 2):
-            nc.scalar.copy(q_dealt[:, lo : lo + SCALAR_GROUPS // 2], q_groups[:, lo : lo + SCALAR_GROUPS // 2])
-        nc.vector.tensor_copy(q_dealt[:, SCALAR_GROUPS:P], q_groups[:, SCALAR_GROUPS:P])
+        nc.scalar.copy(q_dealt[:, :, :, 2:4], q_groups[:, :, :, 2:4])
+        nc.scalar.copy(q_dealt[:, 0:SCALAR_GROUPS, :, 0:2], q_groups[:, 0:SCALAR_GROUPS, :, 0:2])
+        nc.vector.tensor_copy(q_dealt[:, SCALAR_GROUPS:P, :, 0:2], q_groups[:, SCALAR_GROUPS:P, :, 0:2])
         for h in range(2):
             nc.scalar.copy(bias_all[h][:], spread[h][:])
 
         q_cd = sb.tile([P, Q], U32, name="q_cd", align_bytes=64)
         q_sc = sb.tile([P, Q], U8, name="q_sc", align_bytes=64)
-        nc.vector.quantize_mx(out=q_cd[:].bitcast(FP8X4), scales=q_sc[:], in_=q_bf[:])
+        for lo in (Q // 2, 0):
+            hi = lo + Q // 2
+            nc.vector.quantize_mx(out=q_cd[:, lo:hi].bitcast(FP8X4), scales=q_sc[:, lo:hi], in_=q_bf[:, lo * PACK : hi * PACK])
 
         item_cd = reused.tile([P, I], U32, name="item_cd", offset=64, align_bytes=64)
         for lo in range(0, I, QUARTER):

@@ -110,8 +110,9 @@ def tile_attend_pairprefs_pl_kernel(tc, query, item_words, item_scales, ib, offs
             nc.vector.quantize_mx(out=q_cd[:, lo:hi].bitcast(FP8X4), scales=q_sc[:, lo:hi], in_=q_bf[:, lo * PACK : hi * PACK])
 
         item_cd = reused.tile([P, I], U32, name="item_cd", offset=64, align_bytes=64)
-        for lo in range(0, I, QUARTER):
-            nc.vector.tensor_copy(item_cd[:, lo : lo + QUARTER], word_pool[:].indirect(entries(slot_list, lo, lo + QUARTER)))
+        edges = (0, P, QUARTER, BANK, I - QUARTER, I - P, I)
+        for lo, hi in zip(edges, edges[1:]):
+            nc.vector.tensor_copy(item_cd[:, lo:hi], word_pool[:].indirect(entries(slot_list, lo, hi)))
 
         scores = [sb.tile([P, I], F32, name="scores%d" % t, align_bytes=64) for t in range(PACK)]
         diff = sb.tile([P, PACK, J], F32, name="diff", align_bytes=64)
@@ -180,25 +181,29 @@ def tile_attend_pairprefs_pl_kernel(tc, query, item_words, item_scales, ib, offs
             nc.sync.dma_start(words_out[:, lo:hi], y_cd[:, lo:hi].bitcast(I32))
 
         front = bank(6, "front")
-        score(add_on_gpsimd, 4, 0, 0, QUARTER)
-        product(front, 1, 0, QUARTER)
-        score(add_on_gpsimd, 5, 0, QUARTER, BANK)
+        third = bank(0, "third")
+        score(add_on_gpsimd, 4, 0, 0, P)
+        product(front, 1, 0, P)
+        product(third, 2, 0, P)
+        score(add_on_gpsimd, 5, 0, P, QUARTER)
+        product(front, 1, P, QUARTER)
+        product(third, 2, P, QUARTER)
+        score(add_on_gpsimd, 7, 0, QUARTER, BANK)
         product(front, 1, QUARTER, BANK)
         add_on_gpsimd(front, 1, 0, BANK)
-        score(add_on_vector, 7, 0, BANK, I - QUARTER)
-        third = bank(0, "third")
-        product(third, 2, 0, QUARTER)
+        score(add_on_vector, 1, 0, BANK, I - QUARTER)
         product(third, 2, QUARTER, SHARED_SLOTS)
         add_on_gpsimd(third, 2, 0, SHARED_SLOTS)
-        score(add_on_vector, 1, 0, I - QUARTER, I)
+        score(add_on_vector, 2, 0, I - QUARTER, I - P)
+        score(add_on_vector, 4, 0, I - P, I)
 
         look_up_second(0, 0, J)
-        score(add_on_vector, 2, 1, BANK, I)
+        score(add_on_vector, 3, 1, BANK, I)
         look_up_second(1, 0, J)
-        score(add_on_vector, 7, 2, SHARED_SLOTS, BANK)
-        score(add_on_vector, 3, 2, BANK, I)
-        score(add_on_vector, 4, 3, 0, BANK)
-        score(add_on_vector, 5, 3, BANK, I)
+        score(add_on_vector, 1, 2, SHARED_SLOTS, BANK)
+        score(add_on_vector, 5, 2, BANK, I)
+        score(add_on_vector, 2, 3, 0, BANK)
+        score(add_on_vector, 7, 3, BANK, I)
         look_up_second(2, 0, J)
         look_up_second(3, 0, J)
 

from contextlib import ExitStack

import concourse.mybir as mybir
from concourse.masks import make_identity

D, T, I, J, Q = 512, 2048, 1024, 512, 512
FLOPS = 2 * D * I * Q

F32 = mybir.dt.float32
BF16 = mybir.dt.bfloat16
I32 = mybir.dt.int32
U32 = mybir.dt.uint32
U16 = mybir.dt.uint16
U8 = mybir.dt.uint8
FP8X4 = mybir.dt.float8_e4m3fn_x4
ACT = mybir.ActivationFunctionType
ALU = mybir.AluOpType

P = 128
PACK = 4
BANK = 512
BIAS_ROW = P - 1
BLOCKS = BANK // P
PAIR_HALF = J // 2
PAIR_QUARTER = J // 4
LIST_ROWS = 16
QUARTER = I // 4
SCALAR_GROUPS = 32
VECTOR_BIASES = 256
SHARED_SLOTS = 384
VECTOR_ZEROES = 1280


def tile_attend_pairprefs_pl_kernel(tc, query, item_words, item_scales, ib, offs, offs2, offs3, out_0, out_1, out_2):
    nc = tc.nc
    with ExitStack() as ctx:
        lists = ctx.enter_context(tc.tile_pool(name="lists", bufs=1))
        sb = ctx.enter_context(tc.tile_pool(name="sb", bufs=1))
        reused = ctx.enter_context(tc.tile_pool(name="reused", bufs=1))
        psum = ctx.enter_context(tc.psum_pool(name="psum", bufs=1))

        def entries(tile, lo, hi):
            return tile[:, lo // LIST_ROWS : hi // LIST_ROWS]

        def bank(number, name):
            return psum.tile([P, BANK], F32, name=name, tag="bank%d" % number)

        slot_list = lists.tile([P, I // LIST_ROWS], U16, name="slot_list")
        first_list = lists.tile([P, J // LIST_ROWS], U16, name="first_list")
        second_list = lists.tile([P, J // LIST_ROWS], U16, name="second_list")
        scale_pool = sb.tile([P, T], U8, name="scale_pool", align_bytes=64)
        bias_pool = sb.tile([P, T], F32, name="bias_pool", align_bytes=64)
        q_raw = reused.tile([P, PACK, Q], F32, name="q_raw", offset=0, align_bytes=64)
        word_pool = sb.tile([P, T], U32, name="word_pool", align_bytes=64)

        nc.gpsimd.memset(scale_pool[:].bitcast(I32), 0)
        nc.vector.memset(bias_pool[0:BIAS_ROW, 0:VECTOR_ZEROES].bitcast(I32), 0)
        q_rows = query.rearrange("(p r) q -> p r q", r=PACK)
        nc.sync.dma_start(q_raw[:, 0:1], q_rows[:, 0:1])
        nc.sync.dma_start(slot_list[:], offs)
        nc.sync.dma_start(bias_pool[BIAS_ROW:P, :], ib[0:1, :])
        for row in range(4):
            nc.sync.dma_start(scale_pool[row:P:32, :].bitcast(I32), item_scales[0, row:16:4, :].bitcast(I32))
        nc.sync.dma_start(q_raw[:, 1:PACK], q_rows[:, 1:PACK])
        nc.sync.dma_start(word_pool[:].bitcast(I32), item_words[0].rearrange("p n t -> p (n t)").bitcast(I32))
        nc.sync.dma_start(second_list[:], offs3)
        nc.sync.dma_start(first_list[:], offs2)

        warm_in = sb.tile([P, 1], F32, name="warm_in", align_bytes=64)
        warm_out = sb.tile([P, 1], F32, name="warm_out", align_bytes=64)
        nc.gpsimd.memset(warm_in[:], 0.0)
        nc.gpsimd.memset(bias_pool[0:BIAS_ROW, VECTOR_ZEROES:T].bitcast(I32), 0)
        nc.scalar.activation(warm_out[:], warm_in[:], ACT.Sigmoid)
        ident = sb.tile([P, P], F32, name="ident", align_bytes=64)
        make_identity(nc, ident[:])

        bias_row = sb.tile([P, I], F32, name="bias_row", align_bytes=64)
        nc.vector.tensor_copy(bias_row[:, 0:VECTOR_BIASES], bias_pool[:].indirect(entries(slot_list, 0, VECTOR_BIASES)))
        item_sc = sb.tile([P, I], U8, name="item_sc", align_bytes=64)
        nc.vector.tensor_copy(item_sc[:], scale_pool[:].indirect(slot_list[:]))

        bias_col = [sb.tile([P, BLOCKS], F32, name="bias_col%d" % h, align_bytes=64) for h in range(2)]
        bias_all = [reused.tile([P, BANK], F32, name="bias_all%d" % h, offset=4160 + 2048 * h, align_bytes=64) for h in range(2)]
        for lo, hi in ((VECTOR_BIASES, BANK), (BANK, I)):
            nc.scalar.activation(bias_row[:, lo:hi], bias_pool[:].indirect(entries(slot_list, lo, hi)), ACT.Copy)
        spread = []
        for h in range(2):
            turned = bank(h, "bias_turned")
            for b in range(BLOCKS):
                nc.tensor.transpose(turned[:, b * P : (b + 1) * P], bias_row[:, h * BANK + b * P : h * BANK + (b + 1) * P], ident[:])
            nc.scalar.copy(bias_col[h][:], turned[:, BIAS_ROW:BANK:P])
        for h in range(2):
            spread.append(bank(2 + h, "bias_spread"))
            for b in range(BLOCKS):
                nc.tensor.transpose(spread[h][:, b * P : (b + 1) * P], bias_col[h][:, b : b + 1].to_broadcast([P, P]), ident[:])

        q_bf = sb.tile([P, Q * PACK], BF16, name="q_bf", align_bytes=64)
        q_dealt = q_bf[:].rearrange("p (t m r) -> p m r t", t=PACK, r=PACK)
        q_groups = q_raw[:].rearrange("p r (m t) -> p m r t", t=PACK)
        nc.scalar.copy(q_dealt[:, :, :, 2:4], q_groups[:, :, :, 2:4])
        nc.scalar.copy(q_dealt[:, 0:SCALAR_GROUPS, :, 0:2], q_groups[:, 0:SCALAR_GROUPS, :, 0:2])
        nc.vector.tensor_copy(q_dealt[:, SCALAR_GROUPS:P, :, 0:2], q_groups[:, SCALAR_GROUPS:P, :, 0:2])
        for h in range(2):
            nc.scalar.copy(bias_all[h][:], spread[h][:])

        q_cd = sb.tile([P, Q], U32, name="q_cd", align_bytes=64)
        q_sc = sb.tile([P, Q], U8, name="q_sc", align_bytes=64)
        for lo in (Q // 2, 0):
            hi = lo + Q // 2
            nc.vector.quantize_mx(out=q_cd[:, lo:hi].bitcast(FP8X4), scales=q_sc[:, lo:hi], in_=q_bf[:, lo * PACK : hi * PACK])

        item_cd = reused.tile([P, I], U32, name="item_cd", offset=64, align_bytes=64)
        edges = (0, P, QUARTER, BANK, I - QUARTER, I - P, I)
        for lo, hi in zip(edges, edges[1:]):
            nc.vector.tensor_copy(item_cd[:, lo:hi], word_pool[:].indirect(entries(slot_list, lo, hi)))

        scores = [sb.tile([P, I], F32, name="scores%d" % t, align_bytes=64) for t in range(PACK)]
        diff = sb.tile([P, PACK, J], F32, name="diff", align_bytes=64)
        y = sb.tile([P, PACK, J], F32, name="y", align_bytes=64)
        y_rows = out_0.rearrange("(p t) j -> p (t j)", t=PACK)
        y_flat = y[:].rearrange("p t j -> p (t j)")
        y_bf = sb.tile([P, J * PACK], BF16, name="y_bf", align_bytes=64)
        y_cd = sb.tile([P, J], U32, name="y_cd", align_bytes=64)
        y_sc = sb.tile([P, J], U8, name="y_sc", align_bytes=64)
        words_out = out_1[0].rearrange("p c t -> p (c t)").bitcast(I32)

        def product(acc, t, lo, hi):
            nc.tensor.matmul_mx(
                out=acc[:, lo % BANK : lo % BANK + hi - lo],
                lhsT=q_cd[:, t * P : (t + 1) * P].bitcast(FP8X4),
                lhsT_scale=q_sc[:, t * P : (t + 1) * P],
                rhs=item_cd[:, lo:hi].bitcast(FP8X4),
                rhs_scale=item_sc[:, lo:hi],
                start=True,
                stop=True,
            )

        def add_on_vector(acc, t, lo, hi):
            cols = slice(lo % BANK, lo % BANK + hi - lo)
            nc.vector.tensor_tensor(scores[t][:, lo:hi], acc[:, cols], bias_all[lo // BANK][:, cols], ALU.add)

        def add_on_gpsimd(acc, t, lo, hi):
            sums = sb.tile([P, hi - lo], F32, name="sums%d_%d" % (t, lo), align_bytes=64)
            nc.scalar.copy(sums[:], acc[:, lo:hi])
            nc.gpsimd.tensor_tensor(scores[t][:, lo:hi], sums[:], bias_all[0][:, lo:hi], ALU.add)

        def score(add, number, t, lo, hi):
            acc = bank(number, "acc%d_%d" % (t, lo))
            product(acc, t, lo, hi)
            add(acc, t, lo, hi)

        seconds = [sb.tile([P, J], F32, name="seconds%d" % t, align_bytes=64) for t in range(PACK)]

        def look_up(out, t, pair_list, lo, hi):
            nc.scalar.activation(out, scores[t][:].indirect(entries(pair_list, lo, hi)), ACT.Copy)

        def look_up_second(t, lo, hi):
            look_up(seconds[t][:, lo:hi], t, second_list, lo, hi)

        def subtract(t, lo, hi):
            nc.vector.tensor_tensor(
                diff[:, t, lo:hi], scores[t][:].indirect(entries(first_list, lo, hi)), seconds[t][:, lo:hi], ALU.subtract
            )

        def prefer(tiles, lo, hi):
            nc.scalar.activation(y[:, tiles, lo:hi], diff[:, tiles, lo:hi], ACT.Sigmoid)

        def store(lo, hi):
            nc.sync.dma_start(y_rows[:, lo:hi], y_flat[:, lo:hi])

        def woven(lo, hi):
            return y_bf[:, lo * PACK : hi * PACK].rearrange("p (c i t) -> p c t i", i=4, t=PACK)

        def by_fours(source, lo, hi):
            return source[:, :, lo:hi].rearrange("p t (c i) -> p c t i", i=4)

        def quantise(lo, hi):
            nc.vector.quantize_mx(out=y_cd[:, lo:hi].bitcast(FP8X4), scales=y_sc[:, lo:hi], in_=y_bf[:, lo * PACK : hi * PACK])

        def store_words(lo, hi):
            nc.sync.dma_start(words_out[:, lo:hi], y_cd[:, lo:hi].bitcast(I32))

        front = bank(6, "front")
        third = bank(0, "third")
        score(add_on_gpsimd, 4, 0, 0, P)
        product(front, 1, 0, P)
        product(third, 2, 0, P)
        score(add_on_gpsimd, 5, 0, P, QUARTER)
        product(front, 1, P, QUARTER)
        product(third, 2, P, QUARTER)
        score(add_on_gpsimd, 7, 0, QUARTER, BANK)
        product(front, 1, QUARTER, BANK)
        add_on_gpsimd(front, 1, 0, BANK)
        score(add_on_vector, 1, 0, BANK, I - QUARTER)
        product(third, 2, QUARTER, SHARED_SLOTS)
        add_on_gpsimd(third, 2, 0, SHARED_SLOTS)
        score(add_on_vector, 2, 0, I - QUARTER, I - P)
        score(add_on_vector, 4, 0, I - P, I)

        look_up_second(0, 0, J)
        score(add_on_vector, 3, 1, BANK, I)
        look_up_second(1, 0, J)
        score(add_on_vector, 1, 2, SHARED_SLOTS, BANK)
        score(add_on_vector, 5, 2, BANK, I)
        score(add_on_vector, 2, 3, 0, BANK)
        score(add_on_vector, 7, 3, BANK, I)
        look_up_second(2, 0, J)
        look_up_second(3, 0, J)

        last = PACK - 1
        subtract(0, 0, J)
        prefer(slice(0, 1), 0, J)
        store(0, J)
        subtract(1, 0, J)
        prefer(slice(1, 2), 0, J)
        store(J, 2 * J)
        subtract(2, 0, J)
        late = J - PAIR_QUARTER
        for lo, hi in ((0, PAIR_HALF), (PAIR_HALF, late), (late, J)):
            subtract(last, lo, hi)
        prefer(slice(2, 3), 0, PAIR_HALF)
        prefer(slice(last, PACK), 0, PAIR_HALF)
        prefer(slice(2, 3), PAIR_HALF, J)
        prefer(slice(last, PACK), PAIR_HALF, late)
        store(2 * J, last * J + late)
        nc.scalar.activation(woven(late, J), by_fours(diff, late, J), ACT.Sigmoid)
        prefer(slice(last, PACK), late, J)
        store(last * J + late, PACK * J)
        for lo, hi in ((0, PAIR_HALF), (PAIR_HALF, late)):
            nc.vector.tensor_copy(woven(lo, hi), by_fours(y, lo, hi))
        for lo in (0, PAIR_HALF):
            quantise(lo, lo + PAIR_HALF)
            store_words(lo, lo + PAIR_HALF)
        for quad in range(4):
            queue = nc.scalar if quad % 2 else nc.sync
            queue.dma_start(
                out_2[0, 4 * quad : 4 * quad + 4, :].bitcast(I32),
                y_sc[32 * quad : 32 * quad + 4, :].bitcast(I32),
            )
